import numpy as np
import ml_dtypes


def mxq(x, axis, fmt="e4m3"):
    dtype, down = {"e4m3": (ml_dtypes.float8_e4m3fn, 7), "e5m2": (ml_dtypes.float8_e5m2, 14)}[fmt]
    v = np.moveaxis(np.asarray(x, np.float32).astype(ml_dtypes.bfloat16).astype(np.float64), axis, -1)
    blocks = v.reshape(v.shape[:-1] + (-1, 32))
    amax = np.abs(blocks).max(-1, keepdims=True)
    byte = np.maximum(np.where(amax > 0, np.frexp(amax)[1] - 1 + 127, 0) - down, 1)
    scale = np.exp2(byte - 127.0)
    codes = (blocks / scale).astype(np.float32).astype(dtype).astype(np.float64)
    return np.moveaxis((codes * scale).reshape(v.shape), -1, axis)


WIDE = False


def mx_kscale(k):
    if not WIDE:
        return np.ones(k)
    levels = np.array([10, -10, 5, -5, 0])
    if k % 512:
        return np.exp2(np.random.permutation(np.resize(levels, k // 32))).repeat(32)
    a = np.empty((k // 512, 16))
    for p in range(k // 512):
        a[p, :8] = np.random.permutation(np.resize(levels, 8))
        for g in range(8):
            far = levels[np.abs(levels - a[p, g]) >= 10]
            a[p, g + 8] = far[np.random.randint(len(far))]
    return np.exp2(a.ravel()).repeat(32)


BF16 = ml_dtypes.bfloat16


def bf(x):
    return np.asarray(x, np.float32).astype(BF16)


def f64(x):
    return np.asarray(x).astype(np.float64)


S, F, G, T, C = 512, 512, 128, 128, 6144


def smooth_modulus(re, im):
    return np.sqrt(re * re + im * im + 0.25)


def draw0():
    s, t = mx_kscale(S), mx_kscale(F)
    a_scale = 1.0 / np.sqrt(S)
    c_scale = 1.5 / np.sqrt(F)
    return {
        "x": bf(np.random.standard_normal((S, C)) * s[:, None]),
        "ar": bf(np.random.standard_normal((F, S)) * a_scale / s[None, :]),
        "aim": bf(np.random.standard_normal((F, S)) * a_scale / s[None, :]),
        "g1": bf((1.0 + 0.1 * np.random.standard_normal(F)) * t),
        "cr": bf(np.random.standard_normal((G, F)) * c_scale / t[None, :]),
        "cim": bf(np.random.standard_normal((G, F)) * c_scale / t[None, :]),
        "phi": bf(np.random.standard_normal((T, F)) * c_scale / t[None, :]),
    }


def core(x, ar, aim, g1, cr, cim, phi):
    xq = mxq(f64(x), 0, "e4m3")
    r1 = mxq(f64(ar), 1, "e4m3") @ xq
    i1 = mxq(f64(aim), 1, "e4m3") @ xq
    u1 = smooth_modulus(r1, i1)
    n1 = f64(g1)[:, None] * (u1 - np.mean(u1, axis=0, keepdims=True))
    nq = mxq(n1, 0, "e4m3")
    s1 = mxq(f64(phi), 1, "e4m3") @ nq
    r2 = mxq(f64(cr), 1, "e4m3") @ nq
    i2 = mxq(f64(cim), 1, "e4m3") @ nq
    u2 = smooth_modulus(r2, i2)
    return s1, u2


def e4m3fn_bytes(y):
    return np.clip(np.asarray(y, np.float64), -448.0, 448.0).astype(np.float32).astype(ml_dtypes.float8_e4m3fn).view(np.uint8)


def e4m3fn_values(b):
    return np.asarray(b, np.uint8).view(ml_dtypes.float8_e4m3fn).astype(np.float64)


def setup_inputs():
    d = draw0()
    x0 = np.asarray(d['x']).astype(np.float64)
    s = (np.max(np.abs(x0), axis=(1,), keepdims=True) / 448.0).astype(np.float32)
    out = {}
    for k, v in d.items():
        if k == 'x':
            out['x_bytes'] = e4m3fn_bytes(x0 / s.astype(np.float64))
            out['x_scale'] = s
        else:
            out[k] = v
    return out


def reference(x_bytes, x_scale, ar, aim, g1, cr, cim, phi):
    return core(e4m3fn_values(x_bytes) * x_scale.astype(np.float64), ar, aim, g1, cr, cim, phi)

@@ -1,0 +1,440 @@
+from contextlib import ExitStack
+
+import concourse.mybir as mybir
+from concourse.masks import make_identity
+
+S, F, G, T, C = 512, 512, 128, 128, 6144
+FLOPS = 2 * C * (2 * F * S + 2 * G * F + T * F)
+
+F32 = mybir.dt.float32
+BF16 = mybir.dt.bfloat16
+U32 = mybir.dt.uint32
+U8 = mybir.dt.uint8
+FP8 = mybir.dt.float8_e4m3fn
+FP8X4 = mybir.dt.float8_e4m3fn_x4
+ACT = mybir.ActivationFunctionType
+ALU = mybir.AluOpType
+
+P = 128
+BATCH = 256
+N_BATCHES = C // BATCH
+FILTER_TILES = F // P
+CHUNKS = [BATCH] * 2 + [2 * BATCH] * 11
+LOADS = [256, 256, 512] + [1024] * 5
+LATE = 4
+
+
+def tile_learnedsecondorderscattering_t_kernel(
+    tc, x_bytes, x_scale, ar, aim, g1, cr, cim, phi, out_0, out_1
+):
+    nc = tc.nc
+    with ExitStack() as ctx:
+        keep = ctx.enter_context(tc.tile_pool(name="keep", bufs=1))
+        stage = ctx.enter_context(tc.tile_pool(name="stage", bufs=2))
+        psum = ctx.enter_context(tc.psum_pool(name="psum", bufs=1))
+        ident = keep.tile([P, P], F32, name="ident")
+        make_identity(nc, ident[:])
+        ctx.enter_context(tc.manual_schedule())
+
+        a_rows, x_loads = {}, []
+
+        def load_a(name, weights, u):
+            rows = keep.tile([P, 2, S], BF16, name=f"{name}_rows{u}", align_bytes=64)
+            nc.sync.dma_start(
+                out=rows[:], in_=weights.rearrange("(q s) k -> q s k", s=4)[:, 2 * u : 2 * u + 2, :]
+            )
+            a_rows[name, u] = rows
+
+        def load_x():
+            i = len(x_loads)
+            first = sum(LOADS[:i])
+            codes_in = keep.tile([P, 4, LOADS[i]], U8, name=f"codes_in{i}", align_bytes=64)
+            nc.sync.dma_start(
+                out=codes_in[:],
+                in_=x_bytes.rearrange("(p t) c -> p t c", t=4)[:, :, first : first + LOADS[i]],
+            )
+            x_loads.append(codes_in)
+
+        scale = keep.tile([P, 4], F32, name="scale")
+        nc.sync.dma_start(out=scale[:], in_=x_scale.rearrange("(p t) o -> p (t o)", t=4))
+        load_a("ar", ar, 0)
+        load_x()
+        load_a("aim", aim, 0)
+        load_a("ar", ar, 1)
+        load_a("aim", aim, 1)
+        load_x()
+        load_x()
+        w2_rows = keep.tile([P, 3, F], BF16, name="w2_rows", align_bytes=64)
+        for m, weights in enumerate((cr, cim, phi)):
+            nc.sync.dma_start(out=w2_rows[:, m, :], in_=weights)
+        gain_plain = keep.tile([P, F], BF16, name="gain_plain")
+        nc.sync.dma_start(out=gain_plain[:], in_=g1.partition_broadcast(P))
+        while len(x_loads) < len(LOADS):
+            load_x()
+
+        quarter = keep.tile([P, 1], F32, name="quarter")
+        nc.vector.memset(quarter[:], 0.25)
+        warm = keep.tile([P, 1], F32, name="warm")
+        nc.scalar.activation(out=warm[:], in_=quarter[:], func=ACT.Sqrt)
+
+        x_wide, x_grouped, x_codes, x_scales = {}, {}, {}, {}
+
+        def widen(k):
+            n = CHUNKS[k]
+            source, first = (x_loads[k], 0) if k < 3 else (x_loads[3 + (k - 3) // 2], (k - 3) % 2 * n)
+            wide = stage.tile([P, 4, n], BF16, name="x_wide", align_bytes=64)
+            for t in range(4):
+                nc.vector.tensor_scalar(
+                    out=wide[:, t, :],
+                    in0=source[:, t, first : first + n].bitcast(FP8),
+                    scalar1=scale[:, t : t + 1],
+                    scalar2=None,
+                    op0=ALU.mult,
+                )
+            x_wide[k] = wide
+
+        def group_x(k, side):
+            n = CHUNKS[k]
+            if side == 0:
+                grouped = stage.tile([P, n, 4], BF16, name="x_grouped", align_bytes=64)
+                x_grouped[k] = grouped
+            cols = slice(side * n // 2, (side + 1) * n // 2)
+            nc.vector.tensor_copy(
+                out=x_grouped[k][:, cols, :].rearrange("p (c i) t -> p c t i", i=4),
+                in_=x_wide[k][:, :, cols].rearrange("p t (c i) -> p c t i", i=4),
+            )
+
+        def quantize_x(k):
+            n = CHUNKS[k]
+            codes = stage.tile([P, n], U32, name="x_codes", bufs=3, align_bytes=64)
+            scales = stage.tile([P, n], U8, name="x_scales", bufs=3, align_bytes=64)
+            nc.vector.quantize_mx(
+                out=codes[:].bitcast(FP8X4),
+                scales=scales[:],
+                in_=x_grouped[k][:].rearrange("p c t -> p (c t)"),
+            )
+            x_codes[k], x_scales[k] = codes, scales
+
+        def prepare_x(p, side):
+            if p % 2 == 1:
+                if (p + 5) // 2 < len(CHUNKS):
+                    group_x((p + 5) // 2, side)
+            elif side == 0:
+                if (p + 4) // 2 < len(CHUNKS):
+                    quantize_x((p + 4) // 2)
+            elif (p + 6) // 2 < len(CHUNKS):
+                widen((p + 6) // 2)
+
+        a_grouped, a_codes, a_scales = {}, {}, {}
+        for name in ("ar", "aim"):
+            grouped = keep.tile([P, F, 4], BF16, name=f"{name}_grouped", align_bytes=64)
+            codes = keep.tile([P, F], U32, name=f"{name}_codes", align_bytes=64)
+            scales = keep.tile([P, F], U8, name=f"{name}_scales", align_bytes=64)
+            a_grouped[name], a_codes[name], a_scales[name] = grouped, codes, scales
+
+        def turn_a(name, u):
+            turned = psum.tile([P, 2, 2, P], F32, name="turned_a", tag="sq", bufs=4)
+            for e in range(2):
+                words = a_rows[name, u][:, e, :].bitcast(F32)
+                for v in range(2):
+                    nc.tensor.transpose(turned[:, e, v, :], words[:, v : S // 2 : 2], ident[:])
+            return turned
+
+        def group_a(name, u, turned):
+            slots = slice(256 * u, 256 * u + 256)
+            nc.scalar.copy(
+                out=a_grouped[name][:, slots, :].bitcast(F32).rearrange("p (q e) v -> p q e v", e=2),
+                in_=turned[:].rearrange("p e v q -> p q e v"),
+            )
+
+        def quantize_a(name, u):
+            slots = slice(256 * u, 256 * u + 256)
+            nc.vector.quantize_mx(
+                out=a_codes[name][:, slots].bitcast(FP8X4),
+                scales=a_scales[name][:, slots],
+                in_=a_grouped[name][:, slots, :].rearrange("p j t -> p (j t)"),
+            )
+
+        w2_grouped = keep.tile([P, 3, P, 4], BF16, name="w2_grouped", align_bytes=64)
+        w2_codes = keep.tile([P, 3 * P], U32, name="w2_codes", align_bytes=64)
+        w2_scales = keep.tile([P, 3 * P], U8, name="w2_scales", align_bytes=64)
+
+        def turn_and_group_w2(first, count, tag):
+            turned = psum.tile([P, 2, 2, P], F32, name="turned_w2", tag=tag, bufs=1)
+            for i in range(count):
+                words = w2_rows[:, first + i, :].bitcast(F32)
+                for v in range(2):
+                    nc.tensor.transpose(turned[:, i, v, :], words[:, v : F // 2 : 2], ident[:])
+            nc.vector.tensor_copy(
+                out=w2_grouped[:, first : first + count, :, :].bitcast(F32),
+                in_=turned[:, 0:count, :, :].rearrange("p m v g -> p m g v"),
+            )
+
+        def quantize_w2(first, count):
+            cols = slice(first * P, (first + count) * P)
+            nc.vector.quantize_mx(
+                out=w2_codes[:, cols].bitcast(FP8X4),
+                scales=w2_scales[:, cols],
+                in_=w2_grouped[:, first : first + count, :, :].rearrange("p m g t -> p (m g t)"),
+            )
+
+        gain = keep.tile([P, F], F32, name="gain")
+
+        def order_gain():
+            nc.gpsimd.tensor_copy(
+                out=gain[:].rearrange("p (u q e) -> p u q e", u=2, e=2),
+                in_=gain_plain[:].rearrange("p (q u e) -> p u q e", u=2, e=2),
+            )
+
+        ri1, squares, sums, u1s, totals, means = {}, {}, {}, {}, {}, {}
+
+        def first_bank(p, tile):
+            k, first = (p, 0) if p < 2 else (p // 2 + 1, p % 2 * BATCH)
+            cols = slice(first, first + BATCH)
+            slots = slice(tile * P, tile * P + P)
+            bank = psum.tile([P, 2, BATCH], F32, name="ri1", tag="sq", bufs=4)
+            for i, name in enumerate(("ar", "aim")):
+                nc.tensor.matmul_mx(
+                    out=bank[:, i, :],
+                    lhsT=a_codes[name][:, slots].bitcast(FP8X4),
+                    lhsT_scale=a_scales[name][:, slots],
+                    rhs=x_codes[k][:, cols].bitcast(FP8X4),
+                    rhs_scale=x_scales[k][:, cols],
+                    start=True,
+                    stop=True,
+                )
+            ri1[p, tile] = bank
+
+        def square1(p, tile):
+            square = stage.tile([P, 2, BATCH], F32, name="square1", bufs=12)
+            nc.scalar.activation(out=square[:], in_=ri1[p, tile][:], func=ACT.Square)
+            squares[p, tile] = square
+
+        def add_squares1(p, half, tile):
+            if tile == 0:
+                bank = psum.tile([P, F], F32, name="sum1", tag="c", bufs=2)
+                sums[p, half] = bank
+            for i in range(2):
+                nc.tensor.matmul(
+                    out=sums[p, half][:, tile * P : tile * P + P],
+                    lhsT=squares[p, tile][:, i, half * P : half * P + P],
+                    rhs=ident[:],
+                    is_transpose=True,
+                    start=(i == 0),
+                    stop=(i == 1),
+                )
+
+        def root1(p, half):
+            if half == 0:
+                total = stage.tile([P, 2], F32, name="total", bufs=6)
+                totals[p] = total
+            u1 = stage.tile([P, F], F32, name="u1", bufs=8)
+            nc.scalar.activation(
+                out=u1[:],
+                in_=sums[p, half][:],
+                func=ACT.Sqrt,
+                bias=quarter[:, 0:1],
+                accum_out=totals[p][:, half : half + 1],
+            )
+            u1s[p, half] = u1
+
+        def average(p):
+            mean = stage.tile([P, 2], F32, name="mean", bufs=6)
+            nc.vector.tensor_scalar(
+                out=mean[:], in0=totals[p][:], scalar1=1.0 / F, scalar2=None, op0=ALU.mult
+            )
+            means[p] = mean
+
+        n1s, n1_turned, n1_grouped, n1_codes, n1_scales = {}, {}, {}, {}, {}
+
+        def centre(p, half):
+            n1 = stage.tile([P, F], BF16, name="n1", bufs=6, align_bytes=64)
+            nc.vector.scalar_tensor_tensor(
+                out=n1[:],
+                in0=u1s[p, half][:],
+                scalar=means[p][:, half : half + 1],
+                in1=gain[:],
+                op0=ALU.subtract,
+                op1=ALU.mult,
+            )
+            n1s[p, half] = n1
+
+        def turn_n1(p, half):
+            if half == 0:
+                bank = psum.tile([P, 2, 2, P], F32, name="n1_turned", tag="tr", bufs=1)
+                n1_turned[p] = bank
+            words = n1s[p, half][:].bitcast(F32)
+            for u in range(2):
+                nc.tensor.transpose(n1_turned[p][:, half, u, :], words[:, u * P : u * P + P], ident[:])
+
+        def group_n1(p):
+            grouped = stage.tile([P, BATCH, 4], BF16, name="n1_grouped", bufs=3, align_bytes=64)
+            nc.vector.tensor_copy(
+                out=grouped[:].bitcast(F32).rearrange("p (h r) u -> p h r u", h=2),
+                in_=n1_turned[p][:].rearrange("p h u r -> p h r u"),
+            )
+            n1_grouped[p] = grouped
+
+        def quantize_n1(p):
+            codes = stage.tile([P, BATCH], U32, name="n1_codes", bufs=4, align_bytes=64)
+            scales = stage.tile([P, BATCH], U8, name="n1_scales", bufs=4, align_bytes=64)
+            nc.vector.quantize_mx(
+                out=codes[:].bitcast(FP8X4),
+                scales=scales[:],
+                in_=n1_grouped[p][:].rearrange("p c t -> p (c t)"),
+            )
+            n1_codes[p], n1_scales[p] = codes, scales
+
+        ri2, outs, squares2 = {}, {}, {}
+
+        def second_bank(p):
+            late = p >= N_BATCHES - LATE
+            bank = psum.tile([P, 2, 2 * G], F32, name="ri2", tag="sq" if late else "tr", bufs=4 if late else 1)
+            for half in range(2):
+                cols = slice(half * P, half * P + P)
+                nc.tensor.matmul_mx(
+                    out=bank[:, half, :],
+                    lhsT=n1_codes[p][:, cols].bitcast(FP8X4),
+                    lhsT_scale=n1_scales[p][:, cols],
+                    rhs=w2_codes[:, 0 : 2 * G].bitcast(FP8X4),
+                    rhs_scale=w2_scales[:, 0 : 2 * G],
+                    start=True,
+                    stop=True,
+                )
+            ri2[p] = bank
+
+        def first_order(p):
+            late = p >= N_BATCHES - LATE
+            bank = psum.tile([P, 2, BATCH], F32, name="out", tag="sq" if late else "o", bufs=4 if late else 1)
+            nc.tensor.matmul_mx(
+                out=bank[:, 0, :],
+                lhsT=w2_codes[:, 2 * G : 3 * G].bitcast(FP8X4),
+                lhsT_scale=w2_scales[:, 2 * G : 3 * G],
+                rhs=n1_codes[p][:].bitcast(FP8X4),
+                rhs_scale=n1_scales[p][:],
+                start=True,
+                stop=True,
+            )
+            outs[p] = bank
+
+        def store_s1(p):
+            s1 = stage.tile([P, BATCH], F32, name="s1", bufs=3)
+            nc.vector.tensor_copy(out=s1[:], in_=outs[p][:, 0, :])
+            nc.sync.dma_start(out=out_0[:, p * BATCH : p * BATCH + BATCH], in_=s1[:])
+
+        def square2(p):
+            square = stage.tile([P, 2, 2 * G], F32, name="square2", bufs=3)
+            nc.scalar.activation(out=square[:], in_=ri2[p][:], func=ACT.Square)
+            squares2[p] = square
+
+        def add_squares2(p):
+            for half in range(2):
+                for i in range(2):
+                    nc.tensor.matmul(
+                        out=outs[p][:, 1, half * P : half * P + P],
+                        lhsT=squares2[p][:, half, i * G : i * G + G],
+                        rhs=ident[:],
+                        is_transpose=True,
+                        start=(i == 0),
+                        stop=(i == 1),
+                    )
+
+        def late_add_squares2(p):
+            if p >= N_BATCHES - LATE:
+                add_squares2(p)
+
+        def store_u2(p):
+            u2 = stage.tile([P, BATCH], F32, name="u2", bufs=3)
+            nc.scalar.activation(out=u2[:], in_=outs[p][:, 1, :], func=ACT.Sqrt, bias=quarter[:, 0:1])
+            nc.sync.dma_start(out=out_1[:, p * BATCH : p * BATCH + BATCH], in_=u2[:])
+
+        turned = turn_a("ar", 0)
+        group_a("ar", 0, turned)
+        widen(0)
+        group_x(0, 0)
+        group_x(0, 1)
+        quantize_a("ar", 0)
+        quantize_x(0)
+        turned = turn_a("aim", 0)
+        group_a("aim", 0, turned)
+        quantize_a("aim", 0)
+        widen(1)
+        turned = turn_a("ar", 1)
+        group_a("ar", 1, turned)
+        quantize_a("ar", 1)
+        turned = turn_a("aim", 1)
+        group_a("aim", 1, turned)
+        group_x(1, 0)
+        quantize_a("aim", 1)
+        group_x(1, 1)
+        quantize_x(1)
+        order_gain()
+        widen(2)
+        group_x(2, 0)
+        group_x(2, 1)
+        first_bank(0, 0)
+        first_bank(0, 1)
+
+        loop_order = [
+            (lambda p: add_squares1(p, 1, 3), 1),
+            (lambda p: square1(p, 0), 0),
+            (group_n1, 3),
+            (lambda p: first_bank(p, 2), 0),
+            (second_bank, 4),
+            (lambda p: first_bank(p, 3), 0),
+            (lambda p: square1(p, 1), 0),
+            (lambda p: centre(p, 0), 2),
+            (lambda p: centre(p, 1), 2),
+            (store_u2, 5),
+            (lambda p: root1(p, 0), 1),
+            (lambda p: square1(p, 2), 0),
+            (square2, 4),
+            (lambda p: root1(p, 1), 1),
+            (first_order, 4),
+            (lambda p: first_bank(p, 0), -1),
+            (quantize_n1, 3),
+            (lambda p: first_bank(p, 1), -1),
+            (lambda p: prepare_x(p, 0), 0),
+            (lambda p: add_squares1(p, 0, 0), 0),
+            (store_s1, 4),
+            (lambda p: add_squares1(p, 0, 1), 0),
+            (lambda p: square1(p, 3), 0),
+            (lambda p: add_squares1(p, 0, 2), 0),
+            (lambda p: turn_n1(p, 0), 2),
+            (lambda p: turn_n1(p, 1), 2),
+            (add_squares2, 4),
+            (lambda p: add_squares1(p, 1, 0), 0),
+            (lambda p: add_squares1(p, 1, 1), 0),
+            (lambda p: add_squares1(p, 1, 2), 0),
+            (lambda p: add_squares1(p, 0, 3), 0),
+            (lambda p: prepare_x(p, 1), 0),
+            (average, 1),
+        ]
+        drain_order = [
+            (lambda p: add_squares1(p, 1, 3), 1),
+            (second_bank, 4),
+            (first_order, 4),
+            (group_n1, 3),
+            (lambda p: root1(p, 0), 1),
+            (lambda p: centre(p, 0), 2),
+            (lambda p: centre(p, 1), 2),
+            (lambda p: root1(p, 1), 1),
+            (square2, 4),
+            (late_add_squares2, 5),
+            (lambda p: turn_n1(p, 0), 2),
+            (store_u2, 5),
+            (lambda p: turn_n1(p, 1), 2),
+            (quantize_n1, 3),
+            (store_s1, 4),
+            (average, 1),
+        ]
+        for p in range(N_BATCHES + 5):
+            if p == 1:
+                turn_and_group_w2(0, 2, "tr")
+                turn_and_group_w2(2, 1, "o")
+            if p == 2:
+                quantize_w2(0, 2)
+                quantize_w2(2, 1)
+            for stage_of, behind in loop_order if p < N_BATCHES else drain_order:
+                if 0 <= p - behind < N_BATCHES:
+                    stage_of(p - behind)

@@ -19,9 +19,16 @@ P = 128
 BATCH = 256
 N_BATCHES = C // BATCH
 FILTER_TILES = F // P
-CHUNKS = [BATCH] * 2 + [2 * BATCH] * 11
+PAIR = 2 * BATCH
 LOADS = [256, 256, 512] + [1024] * 5
-LATE = 4
+
+
+def vector_squares1(p, tile):
+    return False
+
+
+def vector_squares2(p):
+    return p % 5 == 2 and p < 18
 
 
 def tile_learnedsecondorderscattering_t_kernel(
@@ -32,6 +39,15 @@ def tile_learnedsecondorderscattering_t_kernel(
         keep = ctx.enter_context(tc.tile_pool(name="keep", bufs=1))
         stage = ctx.enter_context(tc.tile_pool(name="stage", bufs=2))
         psum = ctx.enter_context(tc.psum_pool(name="psum", bufs=1))
+        rings = {"scalar": [], "vector": []}
+        ring_banks = {"scalar": 5, "vector": 3}
+
+        def next_bank(reader, shape, name):
+            ring = rings[reader]
+            bank = psum.tile(shape, F32, name=name, tag="%s%d" % (reader, len(ring) % ring_banks[reader]))
+            ring.append(name)
+            return bank
+
         ident = keep.tile([P, P], F32, name="ident")
         make_identity(nc, ident[:])
         ctx.enter_context(tc.manual_schedule())
@@ -79,51 +95,48 @@ def tile_learnedsecondorderscattering_t_kernel(
 
         x_wide, x_grouped, x_codes, x_scales = {}, {}, {}, {}
 
-        def widen(k):
-            n = CHUNKS[k]
-            source, first = (x_loads[k], 0) if k < 3 else (x_loads[3 + (k - 3) // 2], (k - 3) % 2 * n)
-            wide = stage.tile([P, 4, n], BF16, name="x_wide", align_bytes=64)
-            for t in range(4):
+        def widen(j, t, cols, on_scalar=False):
+            if j not in x_wide:
+                wide = stage.tile([P, 4, PAIR], BF16, name="x_wide", bufs=3, align_bytes=64)
+                x_wide[j] = wide
+            first = j * PAIR + cols.start
+            load = max(i for i in range(len(LOADS)) if sum(LOADS[:i]) <= first)
+            first = first - sum(LOADS[:load])
+            source = x_loads[load][:, t, first : first + cols.stop - cols.start].bitcast(FP8)
+            if on_scalar:
+                nc.scalar.activation(out=x_wide[j][:, t, cols], in_=source, func=ACT.Copy, scale=scale[:, t : t + 1])
+            else:
                 nc.vector.tensor_scalar(
-                    out=wide[:, t, :],
-                    in0=source[:, t, first : first + n].bitcast(FP8),
-                    scalar1=scale[:, t : t + 1],
-                    scalar2=None,
-                    op0=ALU.mult,
+                    out=x_wide[j][:, t, cols], in0=source, scalar1=scale[:, t : t + 1], scalar2=None, op0=ALU.mult
                 )
-            x_wide[k] = wide
 
-        def group_x(k, side):
-            n = CHUNKS[k]
-            if side == 0:
-                grouped = stage.tile([P, n, 4], BF16, name="x_grouped", align_bytes=64)
-                x_grouped[k] = grouped
-            cols = slice(side * n // 2, (side + 1) * n // 2)
+        def widen_batch(p, on_scalar=False):
+            for t in range(4):
+                widen(p // 2, t, slice(p % 2 * BATCH, p % 2 * BATCH + BATCH), on_scalar)
+
+        def widen_planes(p, on_scalar=False):
+            for t in (p % 2 * 2, p % 2 * 2 + 1):
+                widen(p // 2, t, slice(0, PAIR), on_scalar)
+
+        def group_x(p):
+            grouped = stage.tile([P, BATCH, 4], BF16, name="x_grouped", bufs=3, align_bytes=64)
+            x_grouped[p] = grouped
+            cols = slice(p % 2 * BATCH, p % 2 * BATCH + BATCH)
+
             nc.vector.tensor_copy(
-                out=x_grouped[k][:, cols, :].rearrange("p (c i) t -> p c t i", i=4),
-                in_=x_wide[k][:, :, cols].rearrange("p t (c i) -> p c t i", i=4),
+                out=grouped[:].rearrange("p (c i) t -> p c t i", i=4),
+                in_=x_wide[p // 2][:, :, cols].rearrange("p t (c i) -> p c t i", i=4),
             )
 
-        def quantize_x(k):
-            n = CHUNKS[k]
-            codes = stage.tile([P, n], U32, name="x_codes", bufs=3, align_bytes=64)
-            scales = stage.tile([P, n], U8, name="x_scales", bufs=3, align_bytes=64)
+        def quantize_x(p):
+            codes = stage.tile([P, BATCH], U32, name="x_codes", bufs=4, align_bytes=64)
+            scales = stage.tile([P, BATCH], U8, name="x_scales", bufs=4, align_bytes=64)
             nc.vector.quantize_mx(
                 out=codes[:].bitcast(FP8X4),
                 scales=scales[:],
-                in_=x_grouped[k][:].rearrange("p c t -> p (c t)"),
+                in_=x_grouped[p][:].rearrange("p c t -> p (c t)"),
             )
-            x_codes[k], x_scales[k] = codes, scales
-
-        def prepare_x(p, side):
-            if p % 2 == 1:
-                if (p + 5) // 2 < len(CHUNKS):
-                    group_x((p + 5) // 2, side)
-            elif side == 0:
-                if (p + 4) // 2 < len(CHUNKS):
-                    quantize_x((p + 4) // 2)
-            elif (p + 6) // 2 < len(CHUNKS):
-                widen((p + 6) // 2)
+            x_codes[p], x_scales[p] = codes, scales
 
         a_grouped, a_codes, a_scales = {}, {}, {}
         for name in ("ar", "aim"):
@@ -133,7 +146,7 @@ def tile_learnedsecondorderscattering_t_kernel(
             a_grouped[name], a_codes[name], a_scales[name] = grouped, codes, scales
 
         def turn_a(name, u):
-            turned = psum.tile([P, 2, 2, P], F32, name="turned_a", tag="sq", bufs=4)
+            turned = next_bank("scalar", [P, 2, 2, P], "turned_a")
             for e in range(2):
                 words = a_rows[name, u][:, e, :].bitcast(F32)
                 for v in range(2):
@@ -159,8 +172,8 @@ def tile_learnedsecondorderscattering_t_kernel(
         w2_codes = keep.tile([P, 3 * P], U32, name="w2_codes", align_bytes=64)
         w2_scales = keep.tile([P, 3 * P], U8, name="w2_scales", align_bytes=64)
 
-        def turn_and_group_w2(first, count, tag):
-            turned = psum.tile([P, 2, 2, P], F32, name="turned_w2", tag=tag, bufs=1)
+        def turn_and_group_w2(first, count):
+            turned = next_bank("vector", [P, 2, 2, P], "turned_w2")
             for i in range(count):
                 words = w2_rows[:, first + i, :].bitcast(F32)
                 for v in range(2):
@@ -178,28 +191,31 @@ def tile_learnedsecondorderscattering_t_kernel(
                 in_=w2_grouped[:, first : first + count, :, :].rearrange("p m g t -> p (m g t)"),
             )
 
-        gain = keep.tile([P, F], F32, name="gain")
+        gain = keep.tile([P, F], BF16, name="gain")
 
         def order_gain():
-            nc.gpsimd.tensor_copy(
+            nc.scalar.copy(
                 out=gain[:].rearrange("p (u q e) -> p u q e", u=2, e=2),
                 in_=gain_plain[:].rearrange("p (q u e) -> p u q e", u=2, e=2),
+            )
+
+        def square_on_vector(square, bank):
+            nc.vector.tensor_reduce(
+                out=square, in_=bank.unsqueeze(2).to_broadcast([P, bank.shape[1], 2]), axis=mybir.AxisListType.X, op=ALU.mult
             )
 
         ri1, squares, sums, u1s, totals, means = {}, {}, {}, {}, {}, {}
 
         def first_bank(p, tile):
-            k, first = (p, 0) if p < 2 else (p // 2 + 1, p % 2 * BATCH)
-            cols = slice(first, first + BATCH)
             slots = slice(tile * P, tile * P + P)
-            bank = psum.tile([P, 2, BATCH], F32, name="ri1", tag="sq", bufs=4)
+            bank = next_bank("vector" if vector_squares1(p, tile) else "scalar", [P, 2, BATCH], "ri1")
             for i, name in enumerate(("ar", "aim")):
                 nc.tensor.matmul_mx(
                     out=bank[:, i, :],
                     lhsT=a_codes[name][:, slots].bitcast(FP8X4),
                     lhsT_scale=a_scales[name][:, slots],
-                    rhs=x_codes[k][:, cols].bitcast(FP8X4),
-                    rhs_scale=x_scales[k][:, cols],
+                    rhs=x_codes[p][:].bitcast(FP8X4),
+                    rhs_scale=x_scales[p][:],
                     start=True,
                     stop=True,
                 )
@@ -207,12 +223,15 @@ def tile_learnedsecondorderscattering_t_kernel(
 
         def square1(p, tile):
             square = stage.tile([P, 2, BATCH], F32, name="square1", bufs=12)
-            nc.scalar.activation(out=square[:], in_=ri1[p, tile][:], func=ACT.Square)
+            if vector_squares1(p, tile):
+                square_on_vector(square[:].rearrange("p h g -> p (h g)"), ri1[p, tile][:].rearrange("p h g -> p (h g)"))
+            else:
+                nc.scalar.activation(out=square[:], in_=ri1[p, tile][:], func=ACT.Square)
             squares[p, tile] = square
 
         def add_squares1(p, half, tile):
             if tile == 0:
-                bank = psum.tile([P, F], F32, name="sum1", tag="c", bufs=2)
+                bank = next_bank("scalar", [P, F], "sum1")
                 sums[p, half] = bank
             for i in range(2):
                 nc.tensor.matmul(
@@ -238,203 +257,293 @@ def tile_learnedsecondorderscattering_t_kernel(
             )
             u1s[p, half] = u1
 
-        def average(p):
-            mean = stage.tile([P, 2], F32, name="mean", bufs=6)
+        def average(h, n):
+            p, half = divmod(h, 2)
+            if half == 0:
+                mean = stage.tile([P, 2], F32, name="mean", bufs=6)
+                means[p] = mean
             nc.vector.tensor_scalar(
-                out=mean[:], in0=totals[p][:], scalar1=1.0 / F, scalar2=None, op0=ALU.mult
+                out=means[p][:, half : half + n],
+                in0=totals[p][:, half : half + n],
+                scalar1=1.0 / F,
+                scalar2=None,
+                op0=ALU.mult,
             )
-            means[p] = mean
 
         n1s, n1_turned, n1_grouped, n1_codes, n1_scales = {}, {}, {}, {}, {}
 
-        def centre(p, half):
+        def centre(h):
             n1 = stage.tile([P, F], BF16, name="n1", bufs=6, align_bytes=64)
             nc.vector.scalar_tensor_tensor(
                 out=n1[:],
-                in0=u1s[p, half][:],
-                scalar=means[p][:, half : half + 1],
+                in0=u1s[h // 2, h % 2][:],
+                scalar=means[h // 2][:, h % 2 : h % 2 + 1],
                 in1=gain[:],
                 op0=ALU.subtract,
                 op1=ALU.mult,
             )
-            n1s[p, half] = n1
+            n1s[h] = n1
 
-        def turn_n1(p, half):
-            if half == 0:
-                bank = psum.tile([P, 2, 2, P], F32, name="n1_turned", tag="tr", bufs=1)
-                n1_turned[p] = bank
-            words = n1s[p, half][:].bitcast(F32)
-            for u in range(2):
-                nc.tensor.transpose(n1_turned[p][:, half, u, :], words[:, u * P : u * P + P], ident[:])
+        def turn_n1(h, n):
+            bank = next_bank("vector", [P, n, 2, P], "n1_turned")
+            for i in range(n):
+                words = n1s[h + i][:].bitcast(F32)
+                for u in range(2):
+                    nc.tensor.transpose(bank[:, i, u, :], words[:, u * P : u * P + P], ident[:])
+            n1_turned[h] = bank
 
-        def group_n1(p):
-            grouped = stage.tile([P, BATCH, 4], BF16, name="n1_grouped", bufs=3, align_bytes=64)
+        def group_n1(h, n):
+            grouped = stage.tile([P, n * P, 4], BF16, name="n1_grouped", bufs=3, align_bytes=64)
             nc.vector.tensor_copy(
-                out=grouped[:].bitcast(F32).rearrange("p (h r) u -> p h r u", h=2),
-                in_=n1_turned[p][:].rearrange("p h u r -> p h r u"),
+                out=grouped[:].bitcast(F32).rearrange("p (h r) u -> p h r u", h=n),
+                in_=n1_turned[h][:].rearrange("p h u r -> p h r u"),
             )
-            n1_grouped[p] = grouped
+            n1_grouped[h] = grouped
 
-        def quantize_n1(p):
-            codes = stage.tile([P, BATCH], U32, name="n1_codes", bufs=4, align_bytes=64)
-            scales = stage.tile([P, BATCH], U8, name="n1_scales", bufs=4, align_bytes=64)
+        def quantize_n1(h, n):
+            if h % 4 == 0:
+                codes = stage.tile([P, PAIR], U32, name="n1_codes", bufs=6, align_bytes=64)
+                scales = stage.tile([P, PAIR], U8, name="n1_scales", bufs=6, align_bytes=64)
+                n1_codes[h // 4], n1_scales[h // 4] = codes, scales
+            cols = slice(h % 4 * P, (h % 4 + n) * P)
             nc.vector.quantize_mx(
-                out=codes[:].bitcast(FP8X4),
-                scales=scales[:],
-                in_=n1_grouped[p][:].rearrange("p c t -> p (c t)"),
+                out=n1_codes[h // 4][:, cols].bitcast(FP8X4),
+                scales=n1_scales[h // 4][:, cols],
+                in_=n1_grouped[h][:].rearrange("p c t -> p (c t)"),
             )
-            n1_codes[p], n1_scales[p] = codes, scales
 
-        ri2, outs, squares2 = {}, {}, {}
+        ri2, s1_sums, squares2, sums2 = {}, {}, {}, {}
 
-        def second_bank(p):
-            late = p >= N_BATCHES - LATE
-            bank = psum.tile([P, 2, 2 * G], F32, name="ri2", tag="sq" if late else "tr", bufs=4 if late else 1)
-            for half in range(2):
-                cols = slice(half * P, half * P + P)
+        def second_bank(h, n):
+            bank = next_bank("vector" if vector_squares2(h // 2) else "scalar", [P, n, 2 * G], "ri2")
+            for i in range(n):
+                cols = slice((h + i) % 4 * P, (h + i) % 4 * P + P)
                 nc.tensor.matmul_mx(
-                    out=bank[:, half, :],
-                    lhsT=n1_codes[p][:, cols].bitcast(FP8X4),
-                    lhsT_scale=n1_scales[p][:, cols],
+                    out=bank[:, i, :],
+                    lhsT=n1_codes[h // 4][:, cols].bitcast(FP8X4),
+                    lhsT_scale=n1_scales[h // 4][:, cols],
                     rhs=w2_codes[:, 0 : 2 * G].bitcast(FP8X4),
                     rhs_scale=w2_scales[:, 0 : 2 * G],
                     start=True,
                     stop=True,
                 )
-            ri2[p] = bank
+            ri2[h] = bank
 
-        def first_order(p):
-            late = p >= N_BATCHES - LATE
-            bank = psum.tile([P, 2, BATCH], F32, name="out", tag="sq" if late else "o", bufs=4 if late else 1)
+        def first_order(h, n):
+            bank = next_bank("vector", [P, n * P], "s1_sums")
+            cols = slice(h % 4 * P, (h % 4 + n) * P)
             nc.tensor.matmul_mx(
-                out=bank[:, 0, :],
+                out=bank[:],
                 lhsT=w2_codes[:, 2 * G : 3 * G].bitcast(FP8X4),
                 lhsT_scale=w2_scales[:, 2 * G : 3 * G],
-                rhs=n1_codes[p][:].bitcast(FP8X4),
-                rhs_scale=n1_scales[p][:],
+                rhs=n1_codes[h // 4][:, cols].bitcast(FP8X4),
+                rhs_scale=n1_scales[h // 4][:, cols],
                 start=True,
                 stop=True,
             )
-            outs[p] = bank
+            s1_sums[h] = bank
 
-        def store_s1(p):
-            s1 = stage.tile([P, BATCH], F32, name="s1", bufs=3)
-            nc.vector.tensor_copy(out=s1[:], in_=outs[p][:, 0, :])
-            nc.sync.dma_start(out=out_0[:, p * BATCH : p * BATCH + BATCH], in_=s1[:])
+        def store_s1(h, n):
+            s1 = stage.tile([P, n * P], F32, name="s1", bufs=3)
+            nc.vector.tensor_copy(out=s1[:], in_=s1_sums[h][:])
+            nc.sync.dma_start(out=out_0[:, h * P : (h + n) * P], in_=s1[:])
 
-        def square2(p):
-            square = stage.tile([P, 2, 2 * G], F32, name="square2", bufs=3)
-            nc.scalar.activation(out=square[:], in_=ri2[p][:], func=ACT.Square)
-            squares2[p] = square
+        def square2(h, n):
+            square = stage.tile([P, n, 2 * G], F32, name="square2", bufs=5)
+            if vector_squares2(h // 2):
+                square_on_vector(square[:].rearrange("p h g -> p (h g)"), ri2[h][:].rearrange("p h g -> p (h g)"))
+            else:
+                nc.scalar.activation(out=square[:], in_=ri2[h][:], func=ACT.Square)
+            for i in range(n):
+                squares2[h + i] = square[:, i, :]
 
-        def add_squares2(p):
-            for half in range(2):
-                for i in range(2):
+        def add_squares2(h, n):
+            bank = next_bank("scalar", [P, n, P], "sum2")
+            for i in range(n):
+                for part in range(2):
                     nc.tensor.matmul(
-                        out=outs[p][:, 1, half * P : half * P + P],
-                        lhsT=squares2[p][:, half, i * G : i * G + G],
+                        out=bank[:, i, :],
+                        lhsT=squares2[h + i][:, part * G : part * G + G],
                         rhs=ident[:],
                         is_transpose=True,
-                        start=(i == 0),
-                        stop=(i == 1),
+                        start=(part == 0),
+                        stop=(part == 1),
                     )
+            sums2[h] = bank
 
-        def late_add_squares2(p):
-            if p >= N_BATCHES - LATE:
-                add_squares2(p)
+        def store_u2(h, n):
+            u2 = stage.tile([P, n * P], F32, name="u2", bufs=3)
+            nc.scalar.activation(
+                out=u2[:], in_=sums2[h][:].rearrange("p h c -> p (h c)"), func=ACT.Sqrt, bias=quarter[:, 0:1]
+            )
+            nc.sync.dma_start(out=out_1[:, h * P : (h + n) * P], in_=u2[:])
 
-        def store_u2(p):
-            u2 = stage.tile([P, BATCH], F32, name="u2", bufs=3)
-            nc.scalar.activation(out=u2[:], in_=outs[p][:, 1, :], func=ACT.Sqrt, bias=quarter[:, 0:1])
-            nc.sync.dma_start(out=out_1[:, p * BATCH : p * BATCH + BATCH], in_=u2[:])
+        def at(stage_of, p, *args):
+            if 0 <= p < N_BATCHES:
+                stage_of(p, *args)
 
-        turned = turn_a("ar", 0)
-        group_a("ar", 0, turned)
-        widen(0)
-        group_x(0, 0)
-        group_x(0, 1)
+        def batch(stage_of, p):
+            if 0 <= p < N_BATCHES:
+                stage_of(2 * p, 2)
+
+        def pair(stage_of, p):
+            if p % 2 == 0 and 0 <= p < N_BATCHES:
+                stage_of(2 * p, 4)
+
+        def add_half(p, half):
+            for tile in range(FILTER_TILES):
+                add_squares1(p, half, tile)
+
+        def centre_half(p, half):
+            centre(2 * p + half)
+
+        turned_ar = turn_a("ar", 0)
+        turned_aim = turn_a("aim", 0)
+        widen_batch(0)
+        group_a("ar", 0, turned_ar)
+        group_x(0)
+        group_a("aim", 0, turned_aim)
+        turned_ar = turn_a("ar", 1)
+        turned_aim = turn_a("aim", 1)
         quantize_a("ar", 0)
         quantize_x(0)
-        turned = turn_a("aim", 0)
-        group_a("aim", 0, turned)
+        widen_batch(1)
         quantize_a("aim", 0)
-        widen(1)
-        turned = turn_a("ar", 1)
-        group_a("ar", 1, turned)
-        quantize_a("ar", 1)
-        turned = turn_a("aim", 1)
-        group_a("aim", 1, turned)
-        group_x(1, 0)
-        quantize_a("aim", 1)
-        group_x(1, 1)
-        quantize_x(1)
-        order_gain()
-        widen(2)
-        group_x(2, 0)
-        group_x(2, 1)
         first_bank(0, 0)
         first_bank(0, 1)
+        group_a("ar", 1, turned_ar)
+        group_x(1)
+        group_a("aim", 1, turned_aim)
+        square1(0, 0)
+        quantize_a("ar", 1)
+        quantize_x(1)
+        square1(0, 1)
+        quantize_a("aim", 1)
+        first_bank(1, 0)
+        first_bank(1, 1)
+        first_bank(0, 2)
+        first_bank(0, 3)
+        widen_planes(2)
+        widen_planes(3)
+        square1(1, 0)
+        square1(1, 1)
+        group_x(2)
+        widen_planes(4)
+        square1(0, 2)
+        quantize_x(2)
+        square1(0, 3)
+        order_gain()
 
-        loop_order = [
-            (lambda p: add_squares1(p, 1, 3), 1),
-            (lambda p: square1(p, 0), 0),
-            (group_n1, 3),
-            (lambda p: first_bank(p, 2), 0),
-            (second_bank, 4),
-            (lambda p: first_bank(p, 3), 0),
-            (lambda p: square1(p, 1), 0),
-            (lambda p: centre(p, 0), 2),
-            (lambda p: centre(p, 1), 2),
-            (store_u2, 5),
-            (lambda p: root1(p, 0), 1),
-            (lambda p: square1(p, 2), 0),
-            (square2, 4),
-            (lambda p: root1(p, 1), 1),
-            (first_order, 4),
-            (lambda p: first_bank(p, 0), -1),
-            (quantize_n1, 3),
-            (lambda p: first_bank(p, 1), -1),
-            (lambda p: prepare_x(p, 0), 0),
-            (lambda p: add_squares1(p, 0, 0), 0),
-            (store_s1, 4),
-            (lambda p: add_squares1(p, 0, 1), 0),
-            (lambda p: square1(p, 3), 0),
-            (lambda p: add_squares1(p, 0, 2), 0),
-            (lambda p: turn_n1(p, 0), 2),
-            (lambda p: turn_n1(p, 1), 2),
-            (add_squares2, 4),
-            (lambda p: add_squares1(p, 1, 0), 0),
-            (lambda p: add_squares1(p, 1, 1), 0),
-            (lambda p: add_squares1(p, 1, 2), 0),
-            (lambda p: add_squares1(p, 0, 3), 0),
-            (lambda p: prepare_x(p, 1), 0),
-            (average, 1),
-        ]
-        drain_order = [
-            (lambda p: add_squares1(p, 1, 3), 1),
-            (second_bank, 4),
-            (first_order, 4),
-            (group_n1, 3),
-            (lambda p: root1(p, 0), 1),
-            (lambda p: centre(p, 0), 2),
-            (lambda p: centre(p, 1), 2),
-            (lambda p: root1(p, 1), 1),
-            (square2, 4),
-            (late_add_squares2, 5),
-            (lambda p: turn_n1(p, 0), 2),
-            (store_u2, 5),
-            (lambda p: turn_n1(p, 1), 2),
-            (quantize_n1, 3),
-            (store_s1, 4),
-            (average, 1),
-        ]
-        for p in range(N_BATCHES + 5):
-            if p == 1:
-                turn_and_group_w2(0, 2, "tr")
-                turn_and_group_w2(2, 1, "o")
-            if p == 2:
+
+        def step(s):
+            if s >= 2:
+                first_bank(s, 0)
+                first_bank(s, 1)
+            batch(second_bank, s - 5)
+            at(group_x, s + 2)
+            batch(average, s - 2)
+            batch(quantize_n1, s - 4)
+            at(widen_planes, s + 4)
+            if s >= 2:
+                square1(s, 0)
+                square1(s, 1)
+            at(add_half, s - 1, 0)
+            batch(turn_n1, s - 3)
+            batch(square2, s - 5)
+            at(root1, s - 1, 0)
+            at(centre_half, s - 2, 0)
+            at(quantize_x, s + 2)
+            first_bank(s, 2)
+            first_bank(s, 3)
+            pair(first_order, s - 6)
+            at(centre_half, s - 2, 1)
+            batch(group_n1, s - 3)
+            square1(s, 2)
+            square1(s, 3)
+            at(add_half, s - 1, 1)
+            pair(add_squares2, s - 7)
+            pair(store_s1, s - 6)
+            at(root1, s - 1, 1)
+            pair(store_u2, s - 7)
+
+        for s in range(1, N_BATCHES - 1):
+            if s == 3:
+                turn_and_group_w2(0, 2)
+                turn_and_group_w2(2, 1)
+            if s == 4:
                 quantize_w2(0, 2)
                 quantize_w2(2, 1)
-            for stage_of, behind in loop_order if p < N_BATCHES else drain_order:
-                if 0 <= p - behind < N_BATCHES:
-                    stage_of(p - behind)
+            step(s)
+
+        first_bank(23, 0)
+        first_bank(23, 1)
+        batch(turn_n1, 20)
+        batch(average, 21)
+        batch(quantize_n1, 19)
+        centre(42)
+        centre(43)
+        batch(group_n1, 20)
+        square1(23, 0)
+        square1(23, 1)
+        add_half(22, 0)
+        add_half(22, 1)
+        first_bank(23, 2)
+        root1(22, 0)
+        root1(22, 1)
+        first_bank(23, 3)
+        batch(turn_n1, 21)
+        pair(first_order, 18)
+        batch(second_bank, 18)
+        batch(average, 22)
+        batch(quantize_n1, 20)
+        centre(44)
+        batch(group_n1, 21)
+        centre(45)
+        square1(23, 2)
+        square1(23, 3)
+        batch(second_bank, 19)
+        add_half(23, 0)
+        add_half(23, 1)
+        batch(turn_n1, 22)
+        batch(quantize_n1, 21)
+        pair(store_s1, 18)
+        batch(square2, 18)
+        batch(square2, 19)
+        root1(23, 0)
+        root1(23, 1)
+        batch(second_bank, 20)
+        pair(add_squares2, 16)
+        batch(group_n1, 22)
+        average(46, 1)
+        batch(quantize_n1, 22)
+        centre(46)
+        average(47, 1)
+        batch(second_bank, 21)
+        pair(first_order, 20)
+        pair(add_squares2, 18)
+        batch(second_bank, 22)
+        turn_n1(46, 1)
+        centre(47)
+        turn_n1(47, 1)
+        batch(square2, 20)
+        pair(store_u2, 16)
+        batch(square2, 21)
+        pair(add_squares2, 20)
+        pair(store_u2, 18)
+        batch(square2, 22)
+        group_n1(46, 1)
+        pair(store_s1, 20)
+        group_n1(47, 1)
+        quantize_n1(46, 1)
+        quantize_n1(47, 1)
+        batch(add_squares2, 22)
+        second_bank(46, 1)
+        second_bank(47, 1)
+        pair(first_order, 22)
+        pair(store_u2, 20)
+        batch(store_u2, 22)
+        square2(46, 1)
+        square2(47, 1)
+        pair(store_s1, 22)
+        batch(add_squares2, 23)
+        batch(store_u2, 23)

@@ -28,7 +28,7 @@ def vector_squares1(p, tile):
 
 
 def vector_squares2(p):
-    return p % 5 == 2 and p < 18
+    return False
 
 
 def tile_learnedsecondorderscattering_t_kernel(
@@ -315,15 +315,15 @@ def tile_learnedsecondorderscattering_t_kernel(
         ri2, s1_sums, squares2, sums2 = {}, {}, {}, {}
 
         def second_bank(h, n):
-            bank = next_bank("vector" if vector_squares2(h // 2) else "scalar", [P, n, 2 * G], "ri2")
-            for i in range(n):
-                cols = slice((h + i) % 4 * P, (h + i) % 4 * P + P)
+            bank = next_bank("vector" if vector_squares2(h // 2) else "scalar", [P, 2, n * P], "ri2")
+            cols = slice(h % 4 * P, (h % 4 + n) * P)
+            for part in range(2):
                 nc.tensor.matmul_mx(
-                    out=bank[:, i, :],
-                    lhsT=n1_codes[h // 4][:, cols].bitcast(FP8X4),
-                    lhsT_scale=n1_scales[h // 4][:, cols],
-                    rhs=w2_codes[:, 0 : 2 * G].bitcast(FP8X4),
-                    rhs_scale=w2_scales[:, 0 : 2 * G],
+                    out=bank[:, part, :],
+                    lhsT=w2_codes[:, part * G : part * G + G].bitcast(FP8X4),
+                    lhsT_scale=w2_scales[:, part * G : part * G + G],
+                    rhs=n1_codes[h // 4][:, cols].bitcast(FP8X4),
+                    rhs_scale=n1_scales[h // 4][:, cols],
                     start=True,
                     stop=True,
                 )
@@ -349,33 +349,31 @@ def tile_learnedsecondorderscattering_t_kernel(
             nc.sync.dma_start(out=out_0[:, h * P : (h + n) * P], in_=s1[:])
 
         def square2(h, n):
-            square = stage.tile([P, n, 2 * G], F32, name="square2", bufs=5)
+            if h % 4 == 0:
+                square = stage.tile([P, 2, PAIR], F32, name="square2", bufs=3)
+                squares2[h // 4] = square
+            cols = slice(h % 4 * P, (h % 4 + n) * P)
             if vector_squares2(h // 2):
-                square_on_vector(square[:].rearrange("p h g -> p (h g)"), ri2[h][:].rearrange("p h g -> p (h g)"))
+                nc.vector.tensor_reduce(
+                    out=squares2[h // 4][:, :, cols],
+                    in_=ri2[h][:].unsqueeze(3).to_broadcast([P, 2, n * P, 2]),
+                    axis=mybir.AxisListType.X,
+                    op=ALU.mult,
+                )
             else:
-                nc.scalar.activation(out=square[:], in_=ri2[h][:], func=ACT.Square)
-            for i in range(n):
-                squares2[h + i] = square[:, i, :]
+                nc.scalar.activation(out=squares2[h // 4][:, :, cols], in_=ri2[h][:], func=ACT.Square)
 
         def add_squares2(h, n):
-            bank = next_bank("scalar", [P, n, P], "sum2")
-            for i in range(n):
-                for part in range(2):
-                    nc.tensor.matmul(
-                        out=bank[:, i, :],
-                        lhsT=squares2[h + i][:, part * G : part * G + G],
-                        rhs=ident[:],
-                        is_transpose=True,
-                        start=(part == 0),
-                        stop=(part == 1),
-                    )
-            sums2[h] = bank
+            cols = slice(h % 4 * P, (h % 4 + n) * P)
+            total = stage.tile([P, n * P], F32, name="sum2", bufs=3)
+            nc.vector.tensor_tensor(
+                out=total[:], in0=squares2[h // 4][:, 0, cols], in1=squares2[h // 4][:, 1, cols], op=ALU.add
+            )
+            sums2[h] = total
 
         def store_u2(h, n):
             u2 = stage.tile([P, n * P], F32, name="u2", bufs=3)
-            nc.scalar.activation(
-                out=u2[:], in_=sums2[h][:].rearrange("p h c -> p (h c)"), func=ACT.Sqrt, bias=quarter[:, 0:1]
-            )
+            nc.scalar.activation(out=u2[:], in_=sums2[h][:], func=ACT.Sqrt, bias=quarter[:, 0:1])
             nc.sync.dma_start(out=out_1[:, h * P : (h + n) * P], in_=u2[:])
 
         def at(stage_of, p, *args):
@@ -443,6 +441,7 @@ def tile_learnedsecondorderscattering_t_kernel(
             at(group_x, s + 2)
             batch(average, s - 2)
             batch(quantize_n1, s - 4)
+            pair(add_squares2, s - 7)
             at(widen_planes, s + 4)
             if s >= 2:
                 square1(s, 0)
@@ -461,7 +460,6 @@ def tile_learnedsecondorderscattering_t_kernel(
             square1(s, 2)
             square1(s, 3)
             at(add_half, s - 1, 1)
-            pair(add_squares2, s - 7)
             pair(store_s1, s - 6)
             at(root1, s - 1, 1)
             pair(store_u2, s - 7)

@@ -31,6 +31,10 @@ def vector_squares2(p):
     return False
 
 
+def tensor_adds(p):
+    return p >= 18
+
+
 def tile_learnedsecondorderscattering_t_kernel(
     tc, x_bytes, x_scale, ar, aim, g1, cr, cim, phi, out_0, out_1
 ):
@@ -40,7 +44,7 @@ def tile_learnedsecondorderscattering_t_kernel(
         stage = ctx.enter_context(tc.tile_pool(name="stage", bufs=2))
         psum = ctx.enter_context(tc.psum_pool(name="psum", bufs=1))
         rings = {"scalar": [], "vector": []}
-        ring_banks = {"scalar": 5, "vector": 3}
+        ring_banks = {"scalar": 5, "vector": 2}
 
         def next_bank(reader, shape, name):
             ring = rings[reader]
@@ -79,12 +83,12 @@ def tile_learnedsecondorderscattering_t_kernel(
         load_a("ar", ar, 1)
         load_a("aim", aim, 1)
         load_x()
+        gain_rows = keep.tile([P, 4], BF16, name="gain_rows")
+        nc.sync.dma_start(out=gain_rows[:], in_=g1.rearrange("(q t) -> q t", t=4))
         load_x()
         w2_rows = keep.tile([P, 3, F], BF16, name="w2_rows", align_bytes=64)
         for m, weights in enumerate((cr, cim, phi)):
             nc.sync.dma_start(out=w2_rows[:, m, :], in_=weights)
-        gain_plain = keep.tile([P, F], BF16, name="gain_plain")
-        nc.sync.dma_start(out=gain_plain[:], in_=g1.partition_broadcast(P))
         while len(x_loads) < len(LOADS):
             load_x()
 
@@ -118,11 +122,20 @@ def tile_learnedsecondorderscattering_t_kernel(
             for t in (p % 2 * 2, p % 2 * 2 + 1):
                 widen(p // 2, t, slice(0, PAIR), on_scalar)
 
-        def group_x(p):
-            grouped = stage.tile([P, BATCH, 4], BF16, name="x_grouped", bufs=3, align_bytes=64)
+        def group_x(p, on_gpsimd=False):
+            grouped = stage.tile([P, BATCH, 4], BF16, name="x_grouped", bufs=1, align_bytes=64)
             x_grouped[p] = grouped
             cols = slice(p % 2 * BATCH, p % 2 * BATCH + BATCH)
-
+            if on_gpsimd:
+                nc.gpsimd.tensor_scalar(
+                    out=grouped[:],
+                    in0=x_wide[p // 2][:, :, cols].rearrange("p t c -> p c t"),
+                    scalar1=1.0,
+                    scalar2=0.0,
+                    op0=ALU.mult,
+                    op1=ALU.add,
+                )
+                return
             nc.vector.tensor_copy(
                 out=grouped[:].rearrange("p (c i) t -> p c t i", i=4),
                 in_=x_wide[p // 2][:, :, cols].rearrange("p t (c i) -> p c t i", i=4),
@@ -191,18 +204,16 @@ def tile_learnedsecondorderscattering_t_kernel(
                 in_=w2_grouped[:, first : first + count, :, :].rearrange("p m g t -> p (m g t)"),
             )
 
-        gain = keep.tile([P, F], BF16, name="gain")
+        gain = psum.tile([P, F], F32, name="gain")
+
+        wide = keep.tile([P, 4], F32, name="gain_wide")
 
         def order_gain():
-            nc.scalar.copy(
-                out=gain[:].rearrange("p (u q e) -> p u q e", u=2, e=2),
-                in_=gain_plain[:].rearrange("p (q u e) -> p u q e", u=2, e=2),
-            )
-
-        def square_on_vector(square, bank):
-            nc.vector.tensor_reduce(
-                out=square, in_=bank.unsqueeze(2).to_broadcast([P, bank.shape[1], 2]), axis=mybir.AxisListType.X, op=ALU.mult
-            )
+            for t in range(4):
+                first = t // 2 * 256 + t % 2
+                nc.tensor.transpose(
+                    gain[:, first : first + 255 : 2], wide[:, t : t + 1].to_broadcast([P, P]), ident[:]
+                )
 
         ri1, squares, sums, u1s, totals, means = {}, {}, {}, {}, {}, {}
 
@@ -223,10 +234,7 @@ def tile_learnedsecondorderscattering_t_kernel(
 
         def square1(p, tile):
             square = stage.tile([P, 2, BATCH], F32, name="square1", bufs=12)
-            if vector_squares1(p, tile):
-                square_on_vector(square[:].rearrange("p h g -> p (h g)"), ri1[p, tile][:].rearrange("p h g -> p (h g)"))
-            else:
-                nc.scalar.activation(out=square[:], in_=ri1[p, tile][:], func=ACT.Square)
+            nc.scalar.activation(out=square[:], in_=ri1[p, tile][:], func=ACT.Square)
             squares[p, tile] = square
 
         def add_squares1(p, half, tile):
@@ -312,11 +320,25 @@ def tile_learnedsecondorderscattering_t_kernel(
                 in_=n1_grouped[h][:].rearrange("p c t -> p (c t)"),
             )
 
-        ri2, s1_sums, squares2, sums2 = {}, {}, {}, {}
+        ri2, ri2_copies, s1_sums, squares2, sums2 = {}, {}, {}, {}, {}
 
         def second_bank(h, n):
             bank = next_bank("vector" if vector_squares2(h // 2) else "scalar", [P, 2, n * P], "ri2")
             cols = slice(h % 4 * P, (h % 4 + n) * P)
+            if tensor_adds(h // 2):
+                for i in range(n):
+                    half = slice((h + i) % 4 * P, (h + i) % 4 * P + P)
+                    nc.tensor.matmul_mx(
+                        out=bank[:].rearrange("p a c -> p (a c)")[:, i * 2 * G : (i + 1) * 2 * G],
+                        lhsT=n1_codes[h // 4][:, half].bitcast(FP8X4),
+                        lhsT_scale=n1_scales[h // 4][:, half],
+                        rhs=w2_codes[:, 0 : 2 * G].bitcast(FP8X4),
+                        rhs_scale=w2_scales[:, 0 : 2 * G],
+                        start=True,
+                        stop=True,
+                    )
+                ri2[h] = bank
+                return
             for part in range(2):
                 nc.tensor.matmul_mx(
                     out=bank[:, part, :],
@@ -348,25 +370,53 @@ def tile_learnedsecondorderscattering_t_kernel(
             nc.vector.tensor_copy(out=s1[:], in_=s1_sums[h][:])
             nc.sync.dma_start(out=out_0[:, h * P : (h + n) * P], in_=s1[:])
 
-        def square2(h, n):
-            if h % 4 == 0:
-                square = stage.tile([P, 2, PAIR], F32, name="square2", bufs=3)
+        def copy_ri2(h, n):
+            if vector_squares2(h // 2):
+                plain = stage.tile([P, 2, n * P], F32, name="ri2_copy", bufs=2)
+                nc.vector.tensor_copy(out=plain[:], in_=ri2[h][:])
+                ri2_copies[h] = plain
+
+        def square2(h, n, on_vector=False):
+            if vector_squares2(h // 2) != on_vector:
+                return
+            if h // 4 not in squares2:
+                square = stage.tile([P, 2, PAIR], F32, name="square2", bufs=4)
                 squares2[h // 4] = square
             cols = slice(h % 4 * P, (h % 4 + n) * P)
-            if vector_squares2(h // 2):
-                nc.vector.tensor_reduce(
-                    out=squares2[h // 4][:, :, cols],
-                    in_=ri2[h][:].unsqueeze(3).to_broadcast([P, 2, n * P, 2]),
-                    axis=mybir.AxisListType.X,
-                    op=ALU.mult,
+            if tensor_adds(h // 2):
+                cols = slice(h % 4 * 2 * G, (h % 4 + n) * 2 * G)
+                nc.scalar.activation(
+                    out=squares2[h // 4][:].rearrange("p a c -> p (a c)")[:, cols],
+                    in_=ri2[h][:].rearrange("p a c -> p (a c)"),
+                    func=ACT.Square,
+                )
+            elif on_vector:
+                nc.vector.tensor_tensor(
+                    out=squares2[h // 4][:, :, cols], in0=ri2[h][:], in1=ri2_copies[h][:], op=ALU.mult
                 )
             else:
                 nc.scalar.activation(out=squares2[h // 4][:, :, cols], in_=ri2[h][:], func=ACT.Square)
 
-        def add_squares2(h, n):
+        def add_squares2(h, n, engine=nc.vector):
+            if tensor_adds(h // 2):
+                bank = next_bank("scalar", [P, n * P], "sum2_bank")
+                square = squares2[h // 4][:].rearrange("p a c -> p (a c)")
+                for i in range(n):
+                    for part in range(2):
+                        first = ((h + i) % 4 * 2 + part) * G
+                        nc.tensor.matmul(
+                            out=bank[:, i * P : i * P + P],
+                            lhsT=square[:, first : first + G],
+                            rhs=ident[:],
+                            is_transpose=True,
+                            start=(part == 0),
+                            stop=(part == 1),
+                        )
+                sums2[h] = bank
+                return
             cols = slice(h % 4 * P, (h % 4 + n) * P)
             total = stage.tile([P, n * P], F32, name="sum2", bufs=3)
-            nc.vector.tensor_tensor(
+            engine.tensor_tensor(
                 out=total[:], in0=squares2[h // 4][:, 0, cols], in1=squares2[h // 4][:, 1, cols], op=ALU.add
             )
             sums2[h] = total
@@ -380,13 +430,13 @@ def tile_learnedsecondorderscattering_t_kernel(
             if 0 <= p < N_BATCHES:
                 stage_of(p, *args)
 
-        def batch(stage_of, p):
+        def batch(stage_of, p, *args):
             if 0 <= p < N_BATCHES:
-                stage_of(2 * p, 2)
+                stage_of(2 * p, 2, *args)
 
-        def pair(stage_of, p):
+        def pair(stage_of, p, *args):
             if p % 2 == 0 and 0 <= p < N_BATCHES:
-                stage_of(2 * p, 4)
+                stage_of(2 * p, 4, *args)
 
         def add_half(p, half):
             for tile in range(FILTER_TILES):
@@ -412,136 +462,163 @@ def tile_learnedsecondorderscattering_t_kernel(
         group_a("ar", 1, turned_ar)
         group_x(1)
         group_a("aim", 1, turned_aim)
+        nc.scalar.copy(out=wide[:], in_=gain_rows[:])
         square1(0, 0)
         quantize_a("ar", 1)
         quantize_x(1)
         square1(0, 1)
         quantize_a("aim", 1)
         first_bank(1, 0)
-        first_bank(1, 1)
         first_bank(0, 2)
         first_bank(0, 3)
+        first_bank(1, 1)
         widen_planes(2)
         widen_planes(3)
         square1(1, 0)
-        square1(1, 1)
+        square1(0, 2)
+        first_bank(1, 2)
+        first_bank(1, 3)
+        order_gain()
         group_x(2)
         widen_planes(4)
-        square1(0, 2)
-        quantize_x(2)
         square1(0, 3)
-        order_gain()
-
+        square1(1, 1)
+        add_half(0, 0)
+        widen_planes(5)
+        quantize_x(2)
+        group_x(3, True)
+        square1(1, 2)
+        add_half(0, 1)
+        turn_and_group_w2(0, 2)
+        turn_and_group_w2(2, 1)
+        square1(1, 3)
+        root1(0, 0)
+        root1(0, 1)
 
         def step(s):
-            if s >= 2:
-                first_bank(s, 0)
-                first_bank(s, 1)
-            batch(second_bank, s - 5)
-            at(group_x, s + 2)
-            batch(average, s - 2)
-            batch(quantize_n1, s - 4)
+            first_bank(s, 0)
+            first_bank(s, 1)
+            if not vector_squares2(s - 5):
+                batch(second_bank, s - 5)
+            if s <= TIGHT:
+                batch(average, s - 2)
+            else:
+                average(2 * s - 3, 1)
             pair(add_squares2, s - 7)
             at(widen_planes, s + 4)
-            if s >= 2:
-                square1(s, 0)
-                square1(s, 1)
-            at(add_half, s - 1, 0)
-            batch(turn_n1, s - 3)
+            at(quantize_x, s + 1)
+            batch(quantize_n1, s - 4)
+            if s > TIGHT + 1:
+                batch(quantize_n1, s - 3)
+            at(group_x, s + 2, True)
+            square1(s, 0)
+            square1(s, 1)
+            add_half(s - 1, 0)
+            if s <= TIGHT + 1:
+                batch(turn_n1, s - 3)
             batch(square2, s - 5)
-            at(root1, s - 1, 0)
-            at(centre_half, s - 2, 0)
-            at(quantize_x, s + 2)
+            root1(s - 1, 0)
+            if s <= TIGHT:
+                centre_half(s - 2, 0)
             first_bank(s, 2)
             first_bank(s, 3)
             pair(first_order, s - 6)
-            at(centre_half, s - 2, 1)
-            batch(group_n1, s - 3)
+            if vector_squares2(s - 5):
+                batch(second_bank, s - 5)
+            centre_half(s - 2, 1)
+            batch(copy_ri2, s - 5)
+            if s <= TIGHT + 1:
+                batch(group_n1, s - 3)
+            batch(square2, s - 5, True)
             square1(s, 2)
             square1(s, 3)
-            at(add_half, s - 1, 1)
+            add_half(s - 1, 1)
+            if s > TIGHT:
+                batch(turn_n1, s - 2)
+            if s >= TIGHT:
+                average(2 * s - 2, 1)
             pair(store_s1, s - 6)
-            at(root1, s - 1, 1)
-            pair(store_u2, s - 7)
+            if s >= TIGHT:
+                centre_half(s - 1, 0)
+            if s > TIGHT:
+                batch(group_n1, s - 2)
+            root1(s - 1, 1)
+            pair(store_u2, s - 8)
 
-        for s in range(1, N_BATCHES - 1):
+        TIGHT = N_BATCHES - 4
+        for s in range(2, N_BATCHES - 1):
             if s == 3:
-                turn_and_group_w2(0, 2)
-                turn_and_group_w2(2, 1)
-            if s == 4:
                 quantize_w2(0, 2)
                 quantize_w2(2, 1)
             step(s)
 
         first_bank(23, 0)
         first_bank(23, 1)
-        batch(turn_n1, 20)
-        batch(average, 21)
-        batch(quantize_n1, 19)
-        centre(42)
-        centre(43)
-        batch(group_n1, 20)
-        square1(23, 0)
-        square1(23, 1)
         add_half(22, 0)
-        add_half(22, 1)
-        first_bank(23, 2)
-        root1(22, 0)
-        root1(22, 1)
-        first_bank(23, 3)
-        batch(turn_n1, 21)
         pair(first_order, 18)
-        batch(second_bank, 18)
-        batch(average, 22)
+        average(43, 1)
         batch(quantize_n1, 20)
-        centre(44)
+        pair(add_squares2, 16)
+        centre(43)
+        square1(23, 0)
+        first_bank(23, 2)
+        square1(23, 1)
+        first_bank(23, 3)
+        root1(22, 0)
+        add_half(22, 1)
+        batch(turn_n1, 21)
+        pair(store_s1, 18)
+        average(44, 1)
         batch(group_n1, 21)
-        centre(45)
+        centre(44)
         square1(23, 2)
         square1(23, 3)
-        batch(second_bank, 19)
-        add_half(23, 0)
-        add_half(23, 1)
-        batch(turn_n1, 22)
-        batch(quantize_n1, 21)
-        pair(store_s1, 18)
+        batch(second_bank, 18)
+        for tile in range(FILTER_TILES):
+            add_squares1(23, 0, tile)
+            add_squares1(23, 1, tile)
+        root1(22, 1)
         batch(square2, 18)
-        batch(square2, 19)
+        average(45, 1)
+        batch(quantize_n1, 21)
+        centre(45)
+        batch(second_bank, 19)
+        batch(second_bank, 20)
+        pair(first_order, 20)
         root1(23, 0)
         root1(23, 1)
-        batch(second_bank, 20)
-        pair(add_squares2, 16)
-        batch(group_n1, 22)
-        average(46, 1)
-        batch(quantize_n1, 22)
-        centre(46)
-        average(47, 1)
         batch(second_bank, 21)
-        pair(first_order, 20)
-        pair(add_squares2, 18)
-        batch(second_bank, 22)
-        turn_n1(46, 1)
+        batch(turn_n1, 22)
+        average(46, 1)
+        pair(store_s1, 20)
+        average(47, 1)
+        centre(46)
         centre(47)
+        batch(square2, 19)
+        pair(store_u2, 16)
+        pair(add_squares2, 18)
+        batch(group_n1, 22)
+        turn_n1(46, 1)
         turn_n1(47, 1)
         batch(square2, 20)
-        pair(store_u2, 16)
         batch(square2, 21)
+        group_n1(46, 1)
+        batch(quantize_n1, 22)
+        group_n1(47, 1)
         pair(add_squares2, 20)
         pair(store_u2, 18)
-        batch(square2, 22)
-        group_n1(46, 1)
-        pair(store_s1, 20)
-        group_n1(47, 1)
         quantize_n1(46, 1)
         quantize_n1(47, 1)
-        batch(add_squares2, 22)
+        batch(second_bank, 22)
         second_bank(46, 1)
         second_bank(47, 1)
         pair(first_order, 22)
         pair(store_u2, 20)
-        batch(store_u2, 22)
+        batch(square2, 22)
         square2(46, 1)
         square2(47, 1)
         pair(store_s1, 22)
+        batch(add_squares2, 22)
         batch(add_squares2, 23)
+        batch(store_u2, 22)
         batch(store_u2, 23)

@@ -28,11 +28,11 @@ def vector_squares1(p, tile):
 
 
 def vector_squares2(p):
-    return False
+    return p % 6 in (0, 2) and p < 16
 
 
 def tensor_adds(p):
-    return p >= 18
+    return p >= 16
 
 
 def tile_learnedsecondorderscattering_t_kernel(
@@ -486,139 +486,152 @@ def tile_learnedsecondorderscattering_t_kernel(
         add_half(0, 0)
         widen_planes(5)
         quantize_x(2)
-        group_x(3, True)
+        group_x(3)
         square1(1, 2)
         add_half(0, 1)
         turn_and_group_w2(0, 2)
+        quantize_x(3)
         turn_and_group_w2(2, 1)
+        group_x(4)
         square1(1, 3)
         root1(0, 0)
         root1(0, 1)
+        first_bank(2, 0)
+        first_bank(2, 1)
+        add_half(1, 0)
+        add_half(1, 1)
+        square1(2, 0)
+        square1(2, 1)
 
         def step(s):
-            first_bank(s, 0)
-            first_bank(s, 1)
-            if not vector_squares2(s - 5):
-                batch(second_bank, s - 5)
-            if s <= TIGHT:
-                batch(average, s - 2)
-            else:
-                average(2 * s - 3, 1)
-            pair(add_squares2, s - 7)
-            at(widen_planes, s + 4)
-            at(quantize_x, s + 1)
-            batch(quantize_n1, s - 4)
-            if s > TIGHT + 1:
-                batch(quantize_n1, s - 3)
-            at(group_x, s + 2, True)
-            square1(s, 0)
-            square1(s, 1)
-            add_half(s - 1, 0)
-            if s <= TIGHT + 1:
-                batch(turn_n1, s - 3)
-            batch(square2, s - 5)
-            root1(s - 1, 0)
-            if s <= TIGHT:
-                centre_half(s - 2, 0)
             first_bank(s, 2)
             first_bank(s, 3)
+            batch(second_bank, s - 5)
+            batch(average, s - 2)
+            pair(add_squares2, s - 8)
+            at(widen_planes, s + 4)
+            at(quantize_x, s + 2)
+            batch(quantize_n1, s - 4)
+            at(group_x, s + 3, True)
+            root1(s - 1, 0)
+            first_bank(s + 1, 0)
+            root1(s - 1, 1)
+            first_bank(s + 1, 1)
             pair(first_order, s - 6)
-            if vector_squares2(s - 5):
-                batch(second_bank, s - 5)
-            centre_half(s - 2, 1)
-            batch(copy_ri2, s - 5)
-            if s <= TIGHT + 1:
-                batch(group_n1, s - 3)
-            batch(square2, s - 5, True)
+            batch(turn_n1, s - 3)
             square1(s, 2)
             square1(s, 3)
-            add_half(s - 1, 1)
-            if s > TIGHT:
-                batch(turn_n1, s - 2)
-            if s >= TIGHT:
-                average(2 * s - 2, 1)
+            batch(square2, s - 5)
+            add_half(s, 0)
+            add_half(s, 1)
+            centre_half(s - 2, 0)
+            centre_half(s - 2, 1)
+            batch(copy_ri2, s - 5)
+            batch(group_n1, s - 3)
+            batch(square2, s - 5, True)
             pair(store_s1, s - 6)
-            if s >= TIGHT:
-                centre_half(s - 1, 0)
-            if s > TIGHT:
-                batch(group_n1, s - 2)
-            root1(s - 1, 1)
-            pair(store_u2, s - 8)
+            pair(store_u2, s - 9)
+            square1(s + 1, 0)
+            square1(s + 1, 1)
 
-        TIGHT = N_BATCHES - 4
-        for s in range(2, N_BATCHES - 1):
+        for s in range(2, N_BATCHES - 2):
             if s == 3:
                 quantize_w2(0, 2)
                 quantize_w2(2, 1)
             step(s)
 
+        batch(average, 20)
+        batch(quantize_n1, 18)
+        pair(add_squares2, 14)
+        first_bank(22, 2)
+        first_bank(22, 3)
+        batch(second_bank, 17)
+        root1(21, 0)
         first_bank(23, 0)
+        root1(21, 1)
         first_bank(23, 1)
+        pair(first_order, 16)
+        batch(turn_n1, 19)
+        centre(40)
+        centre(41)
+        batch(group_n1, 19)
+        batch(average, 21)
+        square1(22, 2)
+        square1(22, 3)
+        batch(square2, 17)
         add_half(22, 0)
-        pair(first_order, 18)
-        average(43, 1)
-        batch(quantize_n1, 20)
-        pair(add_squares2, 16)
-        centre(43)
-        square1(23, 0)
-        first_bank(23, 2)
-        square1(23, 1)
-        first_bank(23, 3)
-        root1(22, 0)
         add_half(22, 1)
-        batch(turn_n1, 21)
-        pair(store_s1, 18)
-        average(44, 1)
-        batch(group_n1, 21)
-        centre(44)
-        square1(23, 2)
-        square1(23, 3)
+        pair(store_s1, 16)
+        batch(turn_n1, 20)
+        batch(quantize_n1, 19)
+        centre(42)
+        centre(43)
+        batch(group_n1, 20)
+        square1(23, 0)
+        square1(23, 1)
+
+        first_bank(23, 2)
+        first_bank(23, 3)
         batch(second_bank, 18)
-        for tile in range(FILTER_TILES):
+        root1(22, 0)
+        root1(22, 1)
+        for tile in range(2):
             add_squares1(23, 0, tile)
             add_squares1(23, 1, tile)
-        root1(22, 1)
-        batch(square2, 18)
-        average(45, 1)
-        batch(quantize_n1, 21)
+        batch(turn_n1, 21)
+        batch(average, 22)
+        batch(quantize_n1, 20)
+        centre(44)
+        batch(group_n1, 21)
         centre(45)
+        square1(23, 2)
+        square1(23, 3)
+        for tile in range(2, 4):
+            add_squares1(23, 0, tile)
+            add_squares1(23, 1, tile)
+        batch(square2, 18)
+        pair(store_u2, 14)
         batch(second_bank, 19)
         batch(second_bank, 20)
-        pair(first_order, 20)
+        pair(first_order, 18)
+        pair(add_squares2, 16)
+        batch(turn_n1, 22)
+        batch(quantize_n1, 21)
         root1(23, 0)
         root1(23, 1)
-        batch(second_bank, 21)
-        batch(turn_n1, 22)
         average(46, 1)
-        pair(store_s1, 20)
+        pair(store_s1, 18)
         average(47, 1)
         centre(46)
-        centre(47)
+        batch(second_bank, 21)
         batch(square2, 19)
-        pair(store_u2, 16)
+        batch(square2, 20)
         pair(add_squares2, 18)
+        centre(47)
         batch(group_n1, 22)
         turn_n1(46, 1)
         turn_n1(47, 1)
-        batch(square2, 20)
+        pair(store_u2, 16)
         batch(square2, 21)
         group_n1(46, 1)
         batch(quantize_n1, 22)
         group_n1(47, 1)
         pair(add_squares2, 20)
-        pair(store_u2, 18)
+        pair(first_order, 20)
+        batch(second_bank, 22)
         quantize_n1(46, 1)
         quantize_n1(47, 1)
-        batch(second_bank, 22)
+        pair(store_u2, 18)
+        pair(store_u2, 20)
         second_bank(46, 1)
         second_bank(47, 1)
+        pair(store_s1, 20)
         pair(first_order, 22)
-        pair(store_u2, 20)
         batch(square2, 22)
         square2(46, 1)
         square2(47, 1)
-        pair(store_s1, 22)
         batch(add_squares2, 22)
+        pair(store_s1, 22)
         batch(add_squares2, 23)
         batch(store_u2, 22)
         batch(store_u2, 23)

@@ -20,6 +20,7 @@ BATCH = 256
 N_BATCHES = C // BATCH
 FILTER_TILES = F // P
 PAIR = 2 * BATCH
+QUAD = 4 * BATCH
 LOADS = [256, 256, 512] + [1024] * 5
 
 
@@ -28,7 +29,7 @@ def vector_squares1(p, tile):
 
 
 def vector_squares2(p):
-    return p % 6 in (0, 2) and p < 16
+    return p % 2 == 0 and p < 16
 
 
 def tensor_adds(p):
@@ -101,9 +102,9 @@ def tile_learnedsecondorderscattering_t_kernel(
 
         def widen(j, t, cols, on_scalar=False):
             if j not in x_wide:
-                wide = stage.tile([P, 4, PAIR], BF16, name="x_wide", bufs=3, align_bytes=64)
+                wide = stage.tile([P, 4, QUAD], BF16, name="x_wide", bufs=2, align_bytes=64)
                 x_wide[j] = wide
-            first = j * PAIR + cols.start
+            first = j * QUAD + cols.start
             load = max(i for i in range(len(LOADS)) if sum(LOADS[:i]) <= first)
             first = first - sum(LOADS[:load])
             source = x_loads[load][:, t, first : first + cols.stop - cols.start].bitcast(FP8)
@@ -116,20 +117,23 @@ def tile_learnedsecondorderscattering_t_kernel(
 
         def widen_batch(p, on_scalar=False):
             for t in range(4):
-                widen(p // 2, t, slice(p % 2 * BATCH, p % 2 * BATCH + BATCH), on_scalar)
+                widen(p // 4, t, slice(p % 4 * BATCH, p % 4 * BATCH + BATCH), on_scalar)
 
         def widen_planes(p, on_scalar=False):
             for t in (p % 2 * 2, p % 2 * 2 + 1):
-                widen(p // 2, t, slice(0, PAIR), on_scalar)
+                widen(p // 4, t, slice(p // 2 % 2 * PAIR, p // 2 % 2 * PAIR + PAIR), on_scalar)
+
+        def widen_plane(p):
+            widen(p // 4, p % 4, slice(0, QUAD))
 
         def group_x(p, on_gpsimd=False):
             grouped = stage.tile([P, BATCH, 4], BF16, name="x_grouped", bufs=1, align_bytes=64)
             x_grouped[p] = grouped
-            cols = slice(p % 2 * BATCH, p % 2 * BATCH + BATCH)
+            cols = slice(p % 4 * BATCH, p % 4 * BATCH + BATCH)
             if on_gpsimd:
                 nc.gpsimd.tensor_scalar(
                     out=grouped[:],
-                    in0=x_wide[p // 2][:, :, cols].rearrange("p t c -> p c t"),
+                    in0=x_wide[p // 4][:, :, cols].rearrange("p t c -> p c t"),
                     scalar1=1.0,
                     scalar2=0.0,
                     op0=ALU.mult,
@@ -138,7 +142,7 @@ def tile_learnedsecondorderscattering_t_kernel(
                 return
             nc.vector.tensor_copy(
                 out=grouped[:].rearrange("p (c i) t -> p c t i", i=4),
-                in_=x_wide[p // 2][:, :, cols].rearrange("p t (c i) -> p c t i", i=4),
+                in_=x_wide[p // 4][:, :, cols].rearrange("p t (c i) -> p c t i", i=4),
             )
 
         def quantize_x(p):
@@ -265,17 +269,19 @@ def tile_learnedsecondorderscattering_t_kernel(
             )
             u1s[p, half] = u1
 
-        def average(h, n):
+        def average(h, n, on_gpsimd=False):
             p, half = divmod(h, 2)
             if half == 0:
                 mean = stage.tile([P, 2], F32, name="mean", bufs=6)
                 means[p] = mean
-            nc.vector.tensor_scalar(
+            engine = nc.gpsimd if on_gpsimd else nc.vector
+            engine.tensor_scalar(
                 out=means[p][:, half : half + n],
                 in0=totals[p][:, half : half + n],
                 scalar1=1.0 / F,
-                scalar2=None,
+                scalar2=0.0,
                 op0=ALU.mult,
+                op1=ALU.add,
             )
 
         n1s, n1_turned, n1_grouped, n1_codes, n1_scales = {}, {}, {}, {}, {}
@@ -455,51 +461,51 @@ def tile_learnedsecondorderscattering_t_kernel(
         turned_aim = turn_a("aim", 1)
         quantize_a("ar", 0)
         quantize_x(0)
-        widen_batch(1)
         quantize_a("aim", 0)
         first_bank(0, 0)
         first_bank(0, 1)
         group_a("ar", 1, turned_ar)
-        group_x(1)
         group_a("aim", 1, turned_aim)
+        widen_batch(1)
+        quantize_a("ar", 1)
+        quantize_a("aim", 1)
+        group_x(1)
         nc.scalar.copy(out=wide[:], in_=gain_rows[:])
         square1(0, 0)
-        quantize_a("ar", 1)
-        quantize_x(1)
         square1(0, 1)
-        quantize_a("aim", 1)
-        first_bank(1, 0)
         first_bank(0, 2)
         first_bank(0, 3)
-        first_bank(1, 1)
+        quantize_x(1)
         widen_planes(2)
         widen_planes(3)
-        square1(1, 0)
+        first_bank(1, 0)
         square1(0, 2)
-        first_bank(1, 2)
-        first_bank(1, 3)
-        order_gain()
-        group_x(2)
-        widen_planes(4)
+        first_bank(1, 1)
         square1(0, 3)
-        square1(1, 1)
+        first_bank(1, 2)
+        group_x(2)
+        widen_plane(4)
+        square1(1, 0)
+        first_bank(1, 3)
         add_half(0, 0)
-        widen_planes(5)
         quantize_x(2)
+        widen_plane(5)
         group_x(3)
-        square1(1, 2)
+        widen_plane(6)
+        square1(1, 1)
         add_half(0, 1)
-        turn_and_group_w2(0, 2)
-        quantize_x(3)
-        turn_and_group_w2(2, 1)
-        group_x(4)
+        square1(1, 2)
         square1(1, 3)
-        root1(0, 0)
-        root1(0, 1)
         first_bank(2, 0)
         first_bank(2, 1)
+        root1(0, 0)
+        root1(0, 1)
+        order_gain()
         add_half(1, 0)
         add_half(1, 1)
+        quantize_x(3)
+        widen_plane(7)
+        group_x(4)
         square1(2, 0)
         square1(2, 1)
 
@@ -507,15 +513,18 @@ def tile_learnedsecondorderscattering_t_kernel(
             first_bank(s, 2)
             first_bank(s, 3)
             batch(second_bank, s - 5)
-            batch(average, s - 2)
+            if s <= 5 or s == 21:
+                batch(average, s - 2)
             pair(add_squares2, s - 8)
-            at(widen_planes, s + 4)
+            at(widen_plane, s + 6)
             at(quantize_x, s + 2)
             batch(quantize_n1, s - 4)
             at(group_x, s + 3, True)
             root1(s - 1, 0)
             first_bank(s + 1, 0)
             root1(s - 1, 1)
+            if 5 <= s < 20:
+                batch(average, s - 1, True)
             first_bank(s + 1, 1)
             pair(first_order, s - 6)
             batch(turn_n1, s - 3)
@@ -526,6 +535,9 @@ def tile_learnedsecondorderscattering_t_kernel(
             add_half(s, 1)
             centre_half(s - 2, 0)
             centre_half(s - 2, 1)
+            if s == 2:
+                turn_and_group_w2(0, 2)
+                turn_and_group_w2(2, 1)
             batch(copy_ri2, s - 5)
             batch(group_n1, s - 3)
             batch(square2, s - 5, True)
@@ -535,7 +547,7 @@ def tile_learnedsecondorderscattering_t_kernel(
             square1(s + 1, 1)
 
         for s in range(2, N_BATCHES - 2):
-            if s == 3:
+            if s == 4:
                 quantize_w2(0, 2)
                 quantize_w2(2, 1)
             step(s)

@@ -29,11 +29,11 @@ def vector_squares1(p, tile):
 
 
 def vector_squares2(p):
-    return p % 2 == 0 and p < 16
+    return p % 2 == 0 and p < 17
 
 
 def tensor_adds(p):
-    return p >= 16
+    return p >= 18
 
 
 def tile_learnedsecondorderscattering_t_kernel(
@@ -44,14 +44,17 @@ def tile_learnedsecondorderscattering_t_kernel(
         keep = ctx.enter_context(tc.tile_pool(name="keep", bufs=1))
         stage = ctx.enter_context(tc.tile_pool(name="stage", bufs=2))
         psum = ctx.enter_context(tc.psum_pool(name="psum", bufs=1))
-        rings = {"scalar": [], "vector": []}
-        ring_banks = {"scalar": 5, "vector": 2}
+        rings = {"scalar": ["s0", "s1", "s2", "s3", "s4"], "vector": ["v0", "v1"]}
 
         def next_bank(reader, shape, name):
-            ring = rings[reader]
-            bank = psum.tile(shape, F32, name=name, tag="%s%d" % (reader, len(ring) % ring_banks[reader]))
-            ring.append(name)
+            oldest = rings[reader][0]
+            rings[reader] = rings[reader][1:] + [oldest]
+            bank = psum.tile(shape, F32, name=name, tag=oldest)
             return bank
+
+        def hand_bank_to_vector():
+            rings["vector"] = rings["scalar"][:1] + rings["vector"]
+            rings["scalar"] = rings["scalar"][1:]
 
         ident = keep.tile([P, P], F32, name="ident")
         make_identity(nc, ident[:])
@@ -59,12 +62,13 @@ def tile_learnedsecondorderscattering_t_kernel(
 
         a_rows, x_loads = {}, []
 
-        def load_a(name, weights, u):
-            rows = keep.tile([P, 2, S], BF16, name=f"{name}_rows{u}", align_bytes=64)
+        def load_a(name, weights, first, count):
+            rows = keep.tile([P, count, S], BF16, name=f"{name}_rows{first}", align_bytes=64)
             nc.sync.dma_start(
-                out=rows[:], in_=weights.rearrange("(q s) k -> q s k", s=4)[:, 2 * u : 2 * u + 2, :]
+                out=rows[:], in_=weights.rearrange("(q t) k -> q t k", t=4)[:, first : first + count, :]
             )
-            a_rows[name, u] = rows
+            for t in range(count):
+                a_rows[name, first + t] = rows[:, t, :]
 
         def load_x():
             i = len(x_loads)
@@ -78,11 +82,10 @@ def tile_learnedsecondorderscattering_t_kernel(
 
         scale = keep.tile([P, 4], F32, name="scale")
         nc.sync.dma_start(out=scale[:], in_=x_scale.rearrange("(p t) o -> p (t o)", t=4))
-        load_a("ar", ar, 0)
         load_x()
-        load_a("aim", aim, 0)
-        load_a("ar", ar, 1)
-        load_a("aim", aim, 1)
+        for first, count in ((0, 1), (1, 1), (2, 2)):
+            load_a("ar", ar, first, count)
+            load_a("aim", aim, first, count)
         load_x()
         gain_rows = keep.tile([P, 4], BF16, name="gain_rows")
         nc.sync.dma_start(out=gain_rows[:], in_=g1.rearrange("(q t) -> q t", t=4))
@@ -93,10 +96,10 @@ def tile_learnedsecondorderscattering_t_kernel(
         while len(x_loads) < len(LOADS):
             load_x()
 
+        sixteenth = keep.tile([P, 1], F32, name="sixteenth")
+        nc.vector.memset(sixteenth[:], 0.0625)
         quarter = keep.tile([P, 1], F32, name="quarter")
-        nc.vector.memset(quarter[:], 0.25)
-        warm = keep.tile([P, 1], F32, name="warm")
-        nc.scalar.activation(out=warm[:], in_=quarter[:], func=ACT.Sqrt)
+        nc.scalar.activation(out=quarter[:], in_=sixteenth[:], func=ACT.Sqrt)
 
         x_wide, x_grouped, x_codes, x_scales = {}, {}, {}, {}
 
@@ -155,30 +158,28 @@ def tile_learnedsecondorderscattering_t_kernel(
             )
             x_codes[p], x_scales[p] = codes, scales
 
-        a_grouped, a_codes, a_scales = {}, {}, {}
+        a_turned, a_grouped, a_codes, a_scales = {}, {}, {}, {}
         for name in ("ar", "aim"):
             grouped = keep.tile([P, F, 4], BF16, name=f"{name}_grouped", align_bytes=64)
             codes = keep.tile([P, F], U32, name=f"{name}_codes", align_bytes=64)
             scales = keep.tile([P, F], U8, name=f"{name}_scales", align_bytes=64)
             a_grouped[name], a_codes[name], a_scales[name] = grouped, codes, scales
 
-        def turn_a(name, u):
-            turned = next_bank("scalar", [P, 2, 2, P], "turned_a")
-            for e in range(2):
-                words = a_rows[name, u][:, e, :].bitcast(F32)
-                for v in range(2):
-                    nc.tensor.transpose(turned[:, e, v, :], words[:, v : S // 2 : 2], ident[:])
-            return turned
+        def turn_a(name, tile):
+            turned = next_bank("scalar", [P, 2, P], "turned_a")
+            words = a_rows[name, tile].bitcast(F32)
+            for v in range(2):
+                nc.tensor.transpose(turned[:, v, :], words[:, v : S // 2 : 2], ident[:])
+            a_turned[name, tile] = turned
 
-        def group_a(name, u, turned):
-            slots = slice(256 * u, 256 * u + 256)
+        def group_a(name, tile):
             nc.scalar.copy(
-                out=a_grouped[name][:, slots, :].bitcast(F32).rearrange("p (q e) v -> p q e v", e=2),
-                in_=turned[:].rearrange("p e v q -> p q e v"),
+                out=a_grouped[name][:, tile * P : tile * P + P, :].bitcast(F32),
+                in_=a_turned[name, tile][:].rearrange("p v q -> p q v"),
             )
 
-        def quantize_a(name, u):
-            slots = slice(256 * u, 256 * u + 256)
+        def quantize_a(name, tile, count=1):
+            slots = slice(tile * P, (tile + count) * P)
             nc.vector.quantize_mx(
                 out=a_codes[name][:, slots].bitcast(FP8X4),
                 scales=a_scales[name][:, slots],
@@ -208,16 +209,13 @@ def tile_learnedsecondorderscattering_t_kernel(
                 in_=w2_grouped[:, first : first + count, :, :].rearrange("p m g t -> p (m g t)"),
             )
 
-        gain = psum.tile([P, F], F32, name="gain")
-
-        wide = keep.tile([P, 4], F32, name="gain_wide")
+        gain_words = psum.tile([P, 2, P], F32, name="gain_words")
+        gain = gain_words[:].rearrange("p u q -> p (u q)").bitcast(BF16)
 
         def order_gain():
-            for t in range(4):
-                first = t // 2 * 256 + t % 2
-                nc.tensor.transpose(
-                    gain[:, first : first + 255 : 2], wide[:, t : t + 1].to_broadcast([P, P]), ident[:]
-                )
+            words = gain_rows[:].bitcast(F32)
+            for u in range(2):
+                nc.tensor.transpose(gain_words[:, u, :], words[:, u : u + 1].to_broadcast([P, P]), ident[:])
 
         ri1, squares, sums, u1s, totals, means = {}, {}, {}, {}, {}, {}
 
@@ -261,8 +259,8 @@ def tile_learnedsecondorderscattering_t_kernel(
                 totals[p] = total
             u1 = stage.tile([P, F], F32, name="u1", bufs=8)
             nc.scalar.activation(
-                out=u1[:],
-                in_=sums[p, half][:],
+                out=u1[:].rearrange("p (u q e) -> p u q e", u=2, e=2),
+                in_=sums[p, half][:].rearrange("p (u e q) -> p u q e", u=2, e=2),
                 func=ACT.Sqrt,
                 bias=quarter[:, 0:1],
                 accum_out=totals[p][:, half : half + 1],
@@ -292,7 +290,7 @@ def tile_learnedsecondorderscattering_t_kernel(
                 out=n1[:],
                 in0=u1s[h // 2, h % 2][:],
                 scalar=means[h // 2][:, h % 2 : h % 2 + 1],
-                in1=gain[:],
+                in1=gain,
                 op0=ALU.subtract,
                 op1=ALU.mult,
             )
@@ -357,8 +355,8 @@ def tile_learnedsecondorderscattering_t_kernel(
                 )
             ri2[h] = bank
 
-        def first_order(h, n):
-            bank = next_bank("vector", [P, n * P], "s1_sums")
+        def first_order(h, n, reader="vector"):
+            bank = next_bank(reader, [P, n * P], "s1_sums")
             cols = slice(h % 4 * P, (h % 4 + n) * P)
             nc.tensor.matmul_mx(
                 out=bank[:],
@@ -371,9 +369,9 @@ def tile_learnedsecondorderscattering_t_kernel(
             )
             s1_sums[h] = bank
 
-        def store_s1(h, n):
-            s1 = stage.tile([P, n * P], F32, name="s1", bufs=3)
-            nc.vector.tensor_copy(out=s1[:], in_=s1_sums[h][:])
+        def store_s1(h, n, copy=nc.vector.tensor_copy):
+            s1 = stage.tile([P, n * P], F32, name="s1", bufs=4)
+            copy(out=s1[:], in_=s1_sums[h][:])
             nc.sync.dma_start(out=out_0[:, h * P : (h + n) * P], in_=s1[:])
 
         def copy_ri2(h, n):
@@ -389,7 +387,15 @@ def tile_learnedsecondorderscattering_t_kernel(
                 square = stage.tile([P, 2, PAIR], F32, name="square2", bufs=4)
                 squares2[h // 4] = square
             cols = slice(h % 4 * P, (h % 4 + n) * P)
-            if tensor_adds(h // 2):
+            if tensor_adds(h // 2) and on_vector:
+                cols = slice(h % 4 * 2 * G, (h % 4 + n) * 2 * G)
+                nc.vector.tensor_tensor(
+                    out=squares2[h // 4][:].rearrange("p a c -> p (a c)")[:, cols],
+                    in0=ri2[h][:].rearrange("p a c -> p (a c)"),
+                    in1=ri2_copies[h][:].rearrange("p a c -> p (a c)"),
+                    op=ALU.mult,
+                )
+            elif tensor_adds(h // 2):
                 cols = slice(h % 4 * 2 * G, (h % 4 + n) * 2 * G)
                 nc.scalar.activation(
                     out=squares2[h // 4][:].rearrange("p a c -> p (a c)")[:, cols],
@@ -428,7 +434,7 @@ def tile_learnedsecondorderscattering_t_kernel(
             sums2[h] = total
 
         def store_u2(h, n):
-            u2 = stage.tile([P, n * P], F32, name="u2", bufs=3)
+            u2 = stage.tile([P, n * P], F32, name="u2", bufs=6)
             nc.scalar.activation(out=u2[:], in_=sums2[h][:], func=ACT.Sqrt, bias=quarter[:, 0:1])
             nc.sync.dma_start(out=out_1[:, h * P : (h + n) * P], in_=u2[:])
 
@@ -451,37 +457,47 @@ def tile_learnedsecondorderscattering_t_kernel(
         def centre_half(p, half):
             centre(2 * p + half)
 
-        turned_ar = turn_a("ar", 0)
-        turned_aim = turn_a("aim", 0)
+        for tile in range(2):
+            turn_a("ar", tile)
+            turn_a("aim", tile)
         widen_batch(0)
-        group_a("ar", 0, turned_ar)
+        group_a("ar", 0)
+        group_a("aim", 0)
         group_x(0)
-        group_a("aim", 0, turned_aim)
-        turned_ar = turn_a("ar", 1)
-        turned_aim = turn_a("aim", 1)
         quantize_a("ar", 0)
         quantize_x(0)
         quantize_a("aim", 0)
+        group_a("ar", 1)
+        group_a("aim", 1)
+        turn_a("ar", 2)
+        turn_a("aim", 2)
         first_bank(0, 0)
-        first_bank(0, 1)
-        group_a("ar", 1, turned_ar)
-        group_a("aim", 1, turned_aim)
-        widen_batch(1)
         quantize_a("ar", 1)
         quantize_a("aim", 1)
-        group_x(1)
-        nc.scalar.copy(out=wide[:], in_=gain_rows[:])
+        group_a("ar", 2)
+        group_a("aim", 2)
+        turn_a("ar", 3)
+        turn_a("aim", 3)
+        first_bank(0, 1)
+        widen_batch(1)
+        quantize_a("ar", 2)
+        quantize_a("aim", 2)
         square1(0, 0)
-        square1(0, 1)
+        group_a("ar", 3)
+        group_a("aim", 3)
         first_bank(0, 2)
+        group_x(1)
+        quantize_a("ar", 3)
+        quantize_a("aim", 3)
+        square1(0, 1)
         first_bank(0, 3)
         quantize_x(1)
         widen_planes(2)
         widen_planes(3)
-        first_bank(1, 0)
         square1(0, 2)
-        first_bank(1, 1)
+        first_bank(1, 0)
         square1(0, 3)
+        first_bank(1, 1)
         first_bank(1, 2)
         group_x(2)
         widen_plane(4)
@@ -535,13 +551,14 @@ def tile_learnedsecondorderscattering_t_kernel(
             add_half(s, 1)
             centre_half(s - 2, 0)
             centre_half(s - 2, 1)
-            if s == 2:
-                turn_and_group_w2(0, 2)
-                turn_and_group_w2(2, 1)
             batch(copy_ri2, s - 5)
             batch(group_n1, s - 3)
             batch(square2, s - 5, True)
             pair(store_s1, s - 6)
+            if s == 2:
+                turn_and_group_w2(0, 2)
+            if s == 3:
+                turn_and_group_w2(2, 1)
             pair(store_u2, s - 9)
             square1(s + 1, 0)
             square1(s + 1, 1)
@@ -552,8 +569,12 @@ def tile_learnedsecondorderscattering_t_kernel(
                 quantize_w2(2, 1)
             step(s)
 
+        batch(turn_n1, 19)
         batch(average, 20)
         batch(quantize_n1, 18)
+        batch(group_n1, 19)
+        centre(40)
+        centre(41)
         pair(add_squares2, 14)
         first_bank(22, 2)
         first_bank(22, 3)
@@ -563,22 +584,19 @@ def tile_learnedsecondorderscattering_t_kernel(
         root1(21, 1)
         first_bank(23, 1)
         pair(first_order, 16)
-        batch(turn_n1, 19)
-        centre(40)
-        centre(41)
-        batch(group_n1, 19)
+        batch(turn_n1, 20)
         batch(average, 21)
+        batch(quantize_n1, 19)
+        centre(42)
+        batch(group_n1, 20)
+        centre(43)
+        pair(store_s1, 16)
+        batch(quantize_n1, 20)
         square1(22, 2)
         square1(22, 3)
         batch(square2, 17)
         add_half(22, 0)
         add_half(22, 1)
-        pair(store_s1, 16)
-        batch(turn_n1, 20)
-        batch(quantize_n1, 19)
-        centre(42)
-        centre(43)
-        batch(group_n1, 20)
         square1(23, 0)
         square1(23, 1)
 
@@ -587,63 +605,67 @@ def tile_learnedsecondorderscattering_t_kernel(
         batch(second_bank, 18)
         root1(22, 0)
         root1(22, 1)
+        batch(turn_n1, 21)
         for tile in range(2):
             add_squares1(23, 0, tile)
             add_squares1(23, 1, tile)
-        batch(turn_n1, 21)
         batch(average, 22)
-        batch(quantize_n1, 20)
-        centre(44)
+        pair(add_squares2, 16)
         batch(group_n1, 21)
+        centre(44)
         centre(45)
+        batch(quantize_n1, 21)
         square1(23, 2)
         square1(23, 3)
         for tile in range(2, 4):
             add_squares1(23, 0, tile)
             add_squares1(23, 1, tile)
-        batch(square2, 18)
-        pair(store_u2, 14)
+        hand_bank_to_vector()
         batch(second_bank, 19)
+        batch(square2, 18)
         batch(second_bank, 20)
-        pair(first_order, 18)
-        pair(add_squares2, 16)
         batch(turn_n1, 22)
-        batch(quantize_n1, 21)
+        pair(first_order, 20)
+        pair(store_u2, 14)
         root1(23, 0)
+        batch(second_bank, 21)
         root1(23, 1)
         average(46, 1)
-        pair(store_s1, 18)
+        batch(group_n1, 22)
         average(47, 1)
         centre(46)
-        batch(second_bank, 21)
-        batch(square2, 19)
-        batch(square2, 20)
-        pair(add_squares2, 18)
         centre(47)
-        batch(group_n1, 22)
+        batch(quantize_n1, 22)
+        pair(first_order, 18, "scalar")
+        batch(square2, 19)
+        pair(add_squares2, 18)
+        batch(square2, 20)
+        batch(square2, 21)
         turn_n1(46, 1)
+        pair(add_squares2, 20)
         turn_n1(47, 1)
         pair(store_u2, 16)
-        batch(square2, 21)
-        group_n1(46, 1)
-        batch(quantize_n1, 22)
-        group_n1(47, 1)
-        pair(add_squares2, 20)
-        pair(first_order, 20)
+        pair(store_s1, 18, nc.scalar.copy)
         batch(second_bank, 22)
+        pair(store_u2, 18)
+        pair(store_s1, 20)
+        pair(store_u2, 20)
+        group_n1(46, 1)
+        group_n1(47, 1)
+        batch(first_order, 22)
         quantize_n1(46, 1)
         quantize_n1(47, 1)
-        pair(store_u2, 18)
-        pair(store_u2, 20)
+        batch(square2, 22)
         second_bank(46, 1)
         second_bank(47, 1)
-        pair(store_s1, 20)
-        pair(first_order, 22)
-        batch(square2, 22)
+        batch(first_order, 23)
+        batch(add_squares2, 22)
+        batch(store_s1, 22)
+        batch(store_s1, 23)
         square2(46, 1)
         square2(47, 1)
-        batch(add_squares2, 22)
-        pair(store_s1, 22)
-        batch(add_squares2, 23)
+        add_squares2(46, 1)
+        add_squares2(47, 1)
         batch(store_u2, 22)
-        batch(store_u2, 23)
+        store_u2(46, 1)
+        store_u2(47, 1)

@@ -262,7 +262,7 @@ def tile_learnedsecondorderscattering_t_kernel(
                 out=u1[:].rearrange("p (u q e) -> p u q e", u=2, e=2),
                 in_=sums[p, half][:].rearrange("p (u e q) -> p u q e", u=2, e=2),
                 func=ACT.Sqrt,
-                bias=quarter[:, 0:1],
+                bias=0.25,
                 accum_out=totals[p][:, half : half + 1],
             )
             u1s[p, half] = u1

@@ -101,6 +101,16 @@ def tile_learnedsecondorderscattering_t_kernel(
         quarter = keep.tile([P, 1], F32, name="quarter")
         nc.scalar.activation(out=quarter[:], in_=sixteenth[:], func=ACT.Sqrt)
 
+        zeros = keep.tile([P, F], BF16, name="zeros")
+        nc.vector.memset(zeros[:], 0.0)
+        unread = next_bank("vector", [P, F], "unread")
+
+        def warm_up(count):
+            for i in range(count):
+                nc.tensor.matmul(out=unread[:], lhsT=zeros[:, 0:P], rhs=zeros[:], start=True, stop=True)
+
+        warm_up(5)
+
         x_wide, x_grouped, x_codes, x_scales = {}, {}, {}, {}
 
         def widen(j, t, cols, on_scalar=False):

@@ -200,15 +200,20 @@ def tile_learnedsecondorderscattering_t_kernel(
         w2_codes = keep.tile([P, 3 * P], U32, name="w2_codes", align_bytes=64)
         w2_scales = keep.tile([P, 3 * P], U8, name="w2_scales", align_bytes=64)
 
-        def turn_and_group_w2(first, count):
+        w2_turned = {}
+
+        def turn_w2(first, count):
             turned = next_bank("vector", [P, 2, 2, P], "turned_w2")
+            w2_turned[first] = turned
             for i in range(count):
                 words = w2_rows[:, first + i, :].bitcast(F32)
                 for v in range(2):
                     nc.tensor.transpose(turned[:, i, v, :], words[:, v : F // 2 : 2], ident[:])
+
+        def group_w2(first, count):
             nc.vector.tensor_copy(
                 out=w2_grouped[:, first : first + count, :, :].bitcast(F32),
-                in_=turned[:, 0:count, :, :].rearrange("p m v g -> p m g v"),
+                in_=w2_turned[first][:, 0:count, :, :].rearrange("p m v g -> p m g v"),
             )
 
         def quantize_w2(first, count):
@@ -539,7 +544,7 @@ def tile_learnedsecondorderscattering_t_kernel(
             first_bank(s, 2)
             first_bank(s, 3)
             batch(second_bank, s - 5)
-            if s <= 5 or s == 21:
+            if s <= 5 or s % 2 == 1:
                 batch(average, s - 2)
             pair(add_squares2, s - 8)
             at(widen_plane, s + 6)
@@ -549,11 +554,15 @@ def tile_learnedsecondorderscattering_t_kernel(
             root1(s - 1, 0)
             first_bank(s + 1, 0)
             root1(s - 1, 1)
-            if 5 <= s < 20:
+            if 5 <= s < 20 and s % 2 == 1:
                 batch(average, s - 1, True)
             first_bank(s + 1, 1)
             pair(first_order, s - 6)
             batch(turn_n1, s - 3)
+            if s == 2:
+                turn_w2(0, 2)
+            if s == 3:
+                turn_w2(2, 1)
             square1(s, 2)
             square1(s, 3)
             batch(square2, s - 5)
@@ -566,9 +575,9 @@ def tile_learnedsecondorderscattering_t_kernel(
             batch(square2, s - 5, True)
             pair(store_s1, s - 6)
             if s == 2:
-                turn_and_group_w2(0, 2)
+                group_w2(0, 2)
             if s == 3:
-                turn_and_group_w2(2, 1)
+                group_w2(2, 1)
             pair(store_u2, s - 9)
             square1(s + 1, 0)
             square1(s + 1, 1)

@@ -29,7 +29,7 @@ def vector_squares1(p, tile):
 
 
 def vector_squares2(p):
-    return p % 2 == 0 and p < 17
+    return (p % 2 == 0 or p > 12) and p < 17
 
 
 def tensor_adds(p):
@@ -544,20 +544,20 @@ def tile_learnedsecondorderscattering_t_kernel(
             first_bank(s, 2)
             first_bank(s, 3)
             batch(second_bank, s - 5)
-            if s <= 5 or s % 2 == 1:
+            if s <= 5 or s % 2 == 0:
                 batch(average, s - 2)
-            pair(add_squares2, s - 8)
             at(widen_plane, s + 6)
             at(quantize_x, s + 2)
             batch(quantize_n1, s - 4)
             at(group_x, s + 3, True)
+            pair(add_squares2, s - 7, nc.gpsimd)
             root1(s - 1, 0)
             first_bank(s + 1, 0)
             root1(s - 1, 1)
-            if 5 <= s < 20 and s % 2 == 1:
+            if 5 <= s < 21 and s % 2 == 0:
                 batch(average, s - 1, True)
             first_bank(s + 1, 1)
-            pair(first_order, s - 6)
+            pair(first_order, s - 6, "scalar" if vector_squares2(s - 5) else "vector")
             batch(turn_n1, s - 3)
             if s == 2:
                 turn_w2(0, 2)
@@ -568,12 +568,12 @@ def tile_learnedsecondorderscattering_t_kernel(
             batch(square2, s - 5)
             add_half(s, 0)
             add_half(s, 1)
-            centre_half(s - 2, 0)
-            centre_half(s - 2, 1)
             batch(copy_ri2, s - 5)
-            batch(group_n1, s - 3)
+            centre_half(s - 2, 0)
             batch(square2, s - 5, True)
             pair(store_s1, s - 6)
+            centre_half(s - 2, 1)
+            batch(group_n1, s - 3)
             if s == 2:
                 group_w2(0, 2)
             if s == 3:
@@ -594,7 +594,6 @@ def tile_learnedsecondorderscattering_t_kernel(
         batch(group_n1, 19)
         centre(40)
         centre(41)
-        pair(add_squares2, 14)
         first_bank(22, 2)
         first_bank(22, 3)
         batch(second_bank, 17)

@@ -21,19 +21,8 @@ N_BATCHES = C // BATCH
 FILTER_TILES = F // P
 PAIR = 2 * BATCH
 QUAD = 4 * BATCH
-LOADS = [256, 256, 512] + [1024] * 5
-
-
-def vector_squares1(p, tile):
-    return False
-
-
-def vector_squares2(p):
-    return (p % 2 == 0 or p > 12) and p < 17
-
-
-def tensor_adds(p):
-    return p >= 18
+LOADS = [BATCH, BATCH, BATCH, PAIR] + [QUAD] * 4 + [3 * BATCH]
+LAST_LOOP_STEP = 18
 
 
 def tile_learnedsecondorderscattering_t_kernel(
@@ -44,17 +33,20 @@ def tile_learnedsecondorderscattering_t_kernel(
         keep = ctx.enter_context(tc.tile_pool(name="keep", bufs=1))
         stage = ctx.enter_context(tc.tile_pool(name="stage", bufs=2))
         psum = ctx.enter_context(tc.psum_pool(name="psum", bufs=1))
-        rings = {"scalar": ["s0", "s1", "s2", "s3", "s4"], "vector": ["v0", "v1"]}
+        ring = ["s0", "s1", "s2", "s3", "s4"]
 
-        def next_bank(reader, shape, name):
-            oldest = rings[reader][0]
-            rings[reader] = rings[reader][1:] + [oldest]
+        def ring_bank(shape, name):
+            oldest = ring[0]
+            ring.remove(oldest)
+            ring.append(oldest)
             bank = psum.tile(shape, F32, name=name, tag=oldest)
             return bank
 
-        def hand_bank_to_vector():
-            rings["vector"] = rings["scalar"][:1] + rings["vector"]
-            rings["scalar"] = rings["scalar"][1:]
+        def bank_of(where, shape, name):
+            if where == "ring":
+                return ring_bank(shape, name)
+            bank = psum.tile(shape, F32, name=name, tag=where)
+            return bank
 
         ident = keep.tile([P, P], F32, name="ident")
         make_identity(nc, ident[:])
@@ -62,13 +54,10 @@ def tile_learnedsecondorderscattering_t_kernel(
 
         a_rows, x_loads = {}, []
 
-        def load_a(name, weights, first, count):
-            rows = keep.tile([P, count, S], BF16, name=f"{name}_rows{first}", align_bytes=64)
-            nc.sync.dma_start(
-                out=rows[:], in_=weights.rearrange("(q t) k -> q t k", t=4)[:, first : first + count, :]
-            )
-            for t in range(count):
-                a_rows[name, first + t] = rows[:, t, :]
+        def load_a(name, weights, tile):
+            rows = keep.tile([P, S], BF16, name=f"{name}_rows{tile}", align_bytes=64)
+            nc.sync.dma_start(out=rows[:], in_=weights.rearrange("(q t) k -> q t k", t=4)[:, tile, :])
+            a_rows[name, tile] = rows
 
         def load_x():
             i = len(x_loads)
@@ -83,12 +72,14 @@ def tile_learnedsecondorderscattering_t_kernel(
         scale = keep.tile([P, 4], F32, name="scale")
         nc.sync.dma_start(out=scale[:], in_=x_scale.rearrange("(p t) o -> p (t o)", t=4))
         load_x()
-        for first, count in ((0, 1), (1, 1), (2, 2)):
-            load_a("ar", ar, first, count)
-            load_a("aim", aim, first, count)
+        for tile in range(FILTER_TILES):
+            load_a("ar", ar, tile)
+            load_a("aim", aim, tile)
+        load_x()
         load_x()
         gain_rows = keep.tile([P, 4], BF16, name="gain_rows")
         nc.sync.dma_start(out=gain_rows[:], in_=g1.rearrange("(q t) -> q t", t=4))
+        load_x()
         load_x()
         w2_rows = keep.tile([P, 3, F], BF16, name="w2_rows", align_bytes=64)
         for m, weights in enumerate((cr, cim, phi)):
@@ -103,50 +94,50 @@ def tile_learnedsecondorderscattering_t_kernel(
 
         zeros = keep.tile([P, F], BF16, name="zeros")
         nc.vector.memset(zeros[:], 0.0)
-        unread = next_bank("vector", [P, F], "unread")
-
-        def warm_up(count):
-            for i in range(count):
-                nc.tensor.matmul(out=unread[:], lhsT=zeros[:, 0:P], rhs=zeros[:], start=True, stop=True)
-
-        warm_up(5)
+        unread = bank_of("turned", [P, F], "unread")
+        for i in range(4):
+            nc.tensor.matmul(out=unread[:], lhsT=zeros[:, 0:P], rhs=zeros[:], start=True, stop=True)
+        one_in_f = keep.tile([P, 1], F32, name="one_in_f")
+        nc.vector.memset(one_in_f[:], 1.0 / F)
 
         x_wide, x_grouped, x_codes, x_scales = {}, {}, {}, {}
 
-        def widen(j, t, cols, on_scalar=False):
-            if j not in x_wide:
+        def stretch_of(p):
+            return (p + 3) // 4, (p - 1) % 4 * BATCH if p else 0
+
+        def widen(p, count, t):
+            stretch, place = stretch_of(p)
+            if stretch not in x_wide:
                 wide = stage.tile([P, 4, QUAD], BF16, name="x_wide", bufs=2, align_bytes=64)
-                x_wide[j] = wide
-            first = j * QUAD + cols.start
-            load = max(i for i in range(len(LOADS)) if sum(LOADS[:i]) <= first)
-            first = first - sum(LOADS[:load])
-            source = x_loads[load][:, t, first : first + cols.stop - cols.start].bitcast(FP8)
-            if on_scalar:
-                nc.scalar.activation(out=x_wide[j][:, t, cols], in_=source, func=ACT.Copy, scale=scale[:, t : t + 1])
-            else:
-                nc.vector.tensor_scalar(
-                    out=x_wide[j][:, t, cols], in0=source, scalar1=scale[:, t : t + 1], scalar2=None, op0=ALU.mult
-                )
+                x_wide[stretch] = wide
+            load = max(i for i in range(len(LOADS)) if sum(LOADS[:i]) <= p * BATCH)
+            first = p * BATCH - sum(LOADS[:load])
+            nc.vector.tensor_scalar(
+                out=x_wide[stretch][:, t, place : place + count * BATCH],
+                in0=x_loads[load][:, t, first : first + count * BATCH].bitcast(FP8),
+                scalar1=scale[:, t : t + 1],
+                scalar2=None,
+                op0=ALU.mult,
+            )
 
-        def widen_batch(p, on_scalar=False):
+        def widen_batches(p, count):
             for t in range(4):
-                widen(p // 4, t, slice(p % 4 * BATCH, p % 4 * BATCH + BATCH), on_scalar)
+                widen(p, count, t)
 
-        def widen_planes(p, on_scalar=False):
-            for t in (p % 2 * 2, p % 2 * 2 + 1):
-                widen(p // 4, t, slice(p // 2 % 2 * PAIR, p // 2 % 2 * PAIR + PAIR), on_scalar)
+        def widen_plane(n):
+            p = 5 + n // 4 * 4
+            if p < N_BATCHES:
+                widen(p, min(4, N_BATCHES - p), n % 4)
 
-        def widen_plane(p):
-            widen(p // 4, p % 4, slice(0, QUAD))
-
-        def group_x(p, on_gpsimd=False):
-            grouped = stage.tile([P, BATCH, 4], BF16, name="x_grouped", bufs=1, align_bytes=64)
+        def group_x(p, count, on_gpsimd=False):
+            grouped = stage.tile([P, count * BATCH, 4], BF16, name="x_grouped", bufs=1, align_bytes=64)
             x_grouped[p] = grouped
-            cols = slice(p % 4 * BATCH, p % 4 * BATCH + BATCH)
+            stretch, place = stretch_of(p)
+            planes = x_wide[stretch][:, :, place : place + count * BATCH]
             if on_gpsimd:
                 nc.gpsimd.tensor_scalar(
                     out=grouped[:],
-                    in0=x_wide[p // 4][:, :, cols].rearrange("p t c -> p c t"),
+                    in0=planes.rearrange("p t c -> p c t"),
                     scalar1=1.0,
                     scalar2=0.0,
                     op0=ALU.mult,
@@ -155,55 +146,53 @@ def tile_learnedsecondorderscattering_t_kernel(
                 return
             nc.vector.tensor_copy(
                 out=grouped[:].rearrange("p (c i) t -> p c t i", i=4),
-                in_=x_wide[p // 4][:, :, cols].rearrange("p t (c i) -> p c t i", i=4),
+                in_=planes.rearrange("p t (c i) -> p c t i", i=4),
             )
 
-        def quantize_x(p):
-            codes = stage.tile([P, BATCH], U32, name="x_codes", bufs=4, align_bytes=64)
-            scales = stage.tile([P, BATCH], U8, name="x_scales", bufs=4, align_bytes=64)
+        def quantize_x(p, count):
+            codes = stage.tile([P, count * BATCH], U32, name="x_codes", bufs=3, align_bytes=64)
+            scales = stage.tile([P, count * BATCH], U8, name="x_scales", bufs=3, align_bytes=64)
             nc.vector.quantize_mx(
                 out=codes[:].bitcast(FP8X4),
                 scales=scales[:],
                 in_=x_grouped[p][:].rearrange("p c t -> p (c t)"),
             )
-            x_codes[p], x_scales[p] = codes, scales
+            for i in range(count):
+                x_codes[p + i] = codes[:, i * BATCH : i * BATCH + BATCH]
+                x_scales[p + i] = scales[:, i * BATCH : i * BATCH + BATCH]
 
-        a_turned, a_grouped, a_codes, a_scales = {}, {}, {}, {}
+        a_grouped, a_codes, a_scales = {}, {}, {}
         for name in ("ar", "aim"):
             grouped = keep.tile([P, F, 4], BF16, name=f"{name}_grouped", align_bytes=64)
             codes = keep.tile([P, F], U32, name=f"{name}_codes", align_bytes=64)
             scales = keep.tile([P, F], U8, name=f"{name}_scales", align_bytes=64)
             a_grouped[name], a_codes[name], a_scales[name] = grouped, codes, scales
 
-        def turn_a(name, tile):
-            turned = next_bank("scalar", [P, 2, P], "turned_a")
-            words = a_rows[name, tile].bitcast(F32)
+        def turn_and_group_a(name, tile):
+            turned = ring_bank([P, 2, P], "turned_a")
+            words = a_rows[name, tile][:].bitcast(F32)
             for v in range(2):
                 nc.tensor.transpose(turned[:, v, :], words[:, v : S // 2 : 2], ident[:])
-            a_turned[name, tile] = turned
-
-        def group_a(name, tile):
             nc.scalar.copy(
                 out=a_grouped[name][:, tile * P : tile * P + P, :].bitcast(F32),
-                in_=a_turned[name, tile][:].rearrange("p v q -> p q v"),
+                in_=turned[:].rearrange("p v q -> p q v"),
             )
 
-        def quantize_a(name, tile, count=1):
-            slots = slice(tile * P, (tile + count) * P)
+        def quantize_a(name, tile):
+            cols = slice(tile * P, tile * P + P)
             nc.vector.quantize_mx(
-                out=a_codes[name][:, slots].bitcast(FP8X4),
-                scales=a_scales[name][:, slots],
-                in_=a_grouped[name][:, slots, :].rearrange("p j t -> p (j t)"),
+                out=a_codes[name][:, cols].bitcast(FP8X4),
+                scales=a_scales[name][:, cols],
+                in_=a_grouped[name][:, cols, :].rearrange("p j t -> p (j t)"),
             )
 
         w2_grouped = keep.tile([P, 3, P, 4], BF16, name="w2_grouped", align_bytes=64)
         w2_codes = keep.tile([P, 3 * P], U32, name="w2_codes", align_bytes=64)
         w2_scales = keep.tile([P, 3 * P], U8, name="w2_scales", align_bytes=64)
-
         w2_turned = {}
 
-        def turn_w2(first, count):
-            turned = next_bank("vector", [P, 2, 2, P], "turned_w2")
+        def turn_w2(first, count, where):
+            turned = bank_of(where, [P, count, 2, P], "turned_w2")
             w2_turned[first] = turned
             for i in range(count):
                 words = w2_rows[:, first + i, :].bitcast(F32)
@@ -213,7 +202,7 @@ def tile_learnedsecondorderscattering_t_kernel(
         def group_w2(first, count):
             nc.vector.tensor_copy(
                 out=w2_grouped[:, first : first + count, :, :].bitcast(F32),
-                in_=w2_turned[first][:, 0:count, :, :].rearrange("p m v g -> p m g v"),
+                in_=w2_turned[first][:].rearrange("p m v g -> p m g v"),
             )
 
         def quantize_w2(first, count):
@@ -224,26 +213,29 @@ def tile_learnedsecondorderscattering_t_kernel(
                 in_=w2_grouped[:, first : first + count, :, :].rearrange("p m g t -> p (m g t)"),
             )
 
-        gain_words = psum.tile([P, 2, P], F32, name="gain_words")
-        gain = gain_words[:].rearrange("p u q -> p (u q)").bitcast(BF16)
+        constants = psum.tile([P, 3, P], F32, name="constants")
+        gain = constants[:, 0:2, :].rearrange("p u q -> p (u q)").bitcast(BF16)
 
-        def order_gain():
+        def spread_constants():
             words = gain_rows[:].bitcast(F32)
             for u in range(2):
-                nc.tensor.transpose(gain_words[:, u, :], words[:, u : u + 1].to_broadcast([P, P]), ident[:])
+                nc.tensor.transpose(constants[:, u, :], words[:, u : u + 1].to_broadcast([P, P]), ident[:])
+            nc.tensor.transpose(constants[:, 2, :], one_in_f[:].to_broadcast([P, P]), ident[:])
 
-        ri1, squares, sums, u1s, totals, means = {}, {}, {}, {}, {}, {}
+        ri1, squares, sums, u1s = {}, {}, {}, {}
+        totals = keep.tile([P, 2 * N_BATCHES], F32, name="totals")
+        means = keep.tile([P, 2 * N_BATCHES], F32, name="means")
 
         def first_bank(p, tile):
-            slots = slice(tile * P, tile * P + P)
-            bank = next_bank("vector" if vector_squares1(p, tile) else "scalar", [P, 2, BATCH], "ri1")
+            cols = slice(tile * P, tile * P + P)
+            bank = ring_bank([P, 2, BATCH], "ri1")
             for i, name in enumerate(("ar", "aim")):
                 nc.tensor.matmul_mx(
                     out=bank[:, i, :],
-                    lhsT=a_codes[name][:, slots].bitcast(FP8X4),
-                    lhsT_scale=a_scales[name][:, slots],
-                    rhs=x_codes[p][:].bitcast(FP8X4),
-                    rhs_scale=x_scales[p][:],
+                    lhsT=a_codes[name][:, cols].bitcast(FP8X4),
+                    lhsT_scale=a_scales[name][:, cols],
+                    rhs=x_codes[p].bitcast(FP8X4),
+                    rhs_scale=x_scales[p],
                     start=True,
                     stop=True,
                 )
@@ -254,47 +246,35 @@ def tile_learnedsecondorderscattering_t_kernel(
             nc.scalar.activation(out=square[:], in_=ri1[p, tile][:], func=ACT.Square)
             squares[p, tile] = square
 
-        def add_squares1(p, half, tile):
-            if tile == 0:
-                bank = next_bank("scalar", [P, F], "sum1")
-                sums[p, half] = bank
-            for i in range(2):
-                nc.tensor.matmul(
-                    out=sums[p, half][:, tile * P : tile * P + P],
-                    lhsT=squares[p, tile][:, i, half * P : half * P + P],
-                    rhs=ident[:],
-                    is_transpose=True,
-                    start=(i == 0),
-                    stop=(i == 1),
-                )
+        def add_squares1(p, half, tiles):
+            for tile in tiles:
+                if tile == 0:
+                    bank = ring_bank([P, F], "sum1")
+                    sums[p, half] = bank
+                for i in range(2):
+                    nc.tensor.matmul(
+                        out=sums[p, half][:, tile * P : tile * P + P],
+                        lhsT=squares[p, tile][:, i, half * P : half * P + P],
+                        rhs=ident[:],
+                        is_transpose=True,
+                        start=(i == 0),
+                        stop=(i == 1),
+                    )
 
         def root1(p, half):
-            if half == 0:
-                total = stage.tile([P, 2], F32, name="total", bufs=6)
-                totals[p] = total
             u1 = stage.tile([P, F], F32, name="u1", bufs=8)
             nc.scalar.activation(
                 out=u1[:].rearrange("p (u q e) -> p u q e", u=2, e=2),
                 in_=sums[p, half][:].rearrange("p (u e q) -> p u q e", u=2, e=2),
                 func=ACT.Sqrt,
                 bias=0.25,
-                accum_out=totals[p][:, half : half + 1],
+                accum_out=totals[:, 2 * p + half : 2 * p + half + 1],
             )
-            u1s[p, half] = u1
+            u1s[2 * p + half] = u1
 
-        def average(h, n, on_gpsimd=False):
-            p, half = divmod(h, 2)
-            if half == 0:
-                mean = stage.tile([P, 2], F32, name="mean", bufs=6)
-                means[p] = mean
-            engine = nc.gpsimd if on_gpsimd else nc.vector
-            engine.tensor_scalar(
-                out=means[p][:, half : half + n],
-                in0=totals[p][:, half : half + n],
-                scalar1=1.0 / F,
-                scalar2=0.0,
-                op0=ALU.mult,
-                op1=ALU.add,
+        def average(h, n):
+            nc.vector.tensor_tensor(
+                out=means[:, h : h + n], in0=totals[:, h : h + n], in1=constants[:, 2, 0:n], op=ALU.mult
             )
 
         n1s, n1_turned, n1_grouped, n1_codes, n1_scales = {}, {}, {}, {}, {}
@@ -302,17 +282,12 @@ def tile_learnedsecondorderscattering_t_kernel(
         def centre(h):
             n1 = stage.tile([P, F], BF16, name="n1", bufs=6, align_bytes=64)
             nc.vector.scalar_tensor_tensor(
-                out=n1[:],
-                in0=u1s[h // 2, h % 2][:],
-                scalar=means[h // 2][:, h % 2 : h % 2 + 1],
-                in1=gain,
-                op0=ALU.subtract,
-                op1=ALU.mult,
+                out=n1[:], in0=u1s[h][:], scalar=means[:, h : h + 1], in1=gain, op0=ALU.subtract, op1=ALU.mult
             )
             n1s[h] = n1
 
-        def turn_n1(h, n):
-            bank = next_bank("vector", [P, n, 2, P], "n1_turned")
+        def turn_n1(h, n, where="turned"):
+            bank = bank_of(where, [P, n, 2, P], "n1_turned")
             for i in range(n):
                 words = n1s[h + i][:].bitcast(F32)
                 for u in range(2):
@@ -320,68 +295,72 @@ def tile_learnedsecondorderscattering_t_kernel(
             n1_turned[h] = bank
 
         def group_n1(h, n):
-            grouped = stage.tile([P, n * P, 4], BF16, name="n1_grouped", bufs=3, align_bytes=64)
-            nc.vector.tensor_copy(
-                out=grouped[:].bitcast(F32).rearrange("p (h r) u -> p h r u", h=n),
-                in_=n1_turned[h][:].rearrange("p h u r -> p h r u"),
-            )
-            n1_grouped[h] = grouped
-
-        def quantize_n1(h, n):
             if h % 4 == 0:
+                grouped = stage.tile([P, PAIR, 4], BF16, name="n1_grouped", bufs=2, align_bytes=64)
                 codes = stage.tile([P, PAIR], U32, name="n1_codes", bufs=6, align_bytes=64)
                 scales = stage.tile([P, PAIR], U8, name="n1_scales", bufs=6, align_bytes=64)
-                n1_codes[h // 4], n1_scales[h // 4] = codes, scales
+                n1_grouped[h // 4], n1_codes[h // 4], n1_scales[h // 4] = grouped, codes, scales
+            cols = slice(h % 4 * P, (h % 4 + n) * P)
+            nc.vector.tensor_copy(
+                out=n1_grouped[h // 4][:, cols, :].bitcast(F32).rearrange("p (h r) u -> p h r u", h=n),
+                in_=n1_turned[h][:].rearrange("p h u r -> p h r u"),
+            )
+
+        def quantize_n1(h, n):
             cols = slice(h % 4 * P, (h % 4 + n) * P)
             nc.vector.quantize_mx(
                 out=n1_codes[h // 4][:, cols].bitcast(FP8X4),
                 scales=n1_scales[h // 4][:, cols],
-                in_=n1_grouped[h][:].rearrange("p c t -> p (c t)"),
+                in_=n1_grouped[h // 4][:, cols, :].rearrange("p c t -> p (c t)"),
             )
 
         ri2, ri2_copies, s1_sums, squares2, sums2 = {}, {}, {}, {}, {}
 
-        def second_bank(h, n):
-            bank = next_bank("vector" if vector_squares2(h // 2) else "scalar", [P, 2, n * P], "ri2")
-            cols = slice(h % 4 * P, (h % 4 + n) * P)
-            if tensor_adds(h // 2):
-                for i in range(n):
-                    half = slice((h + i) % 4 * P, (h + i) % 4 * P + P)
-                    nc.tensor.matmul_mx(
-                        out=bank[:].rearrange("p a c -> p (a c)")[:, i * 2 * G : (i + 1) * 2 * G],
-                        lhsT=n1_codes[h // 4][:, half].bitcast(FP8X4),
-                        lhsT_scale=n1_scales[h // 4][:, half],
-                        rhs=w2_codes[:, 0 : 2 * G].bitcast(FP8X4),
-                        rhs_scale=w2_scales[:, 0 : 2 * G],
-                        start=True,
-                        stop=True,
-                    )
-                ri2[h] = bank
-                return
-            for part in range(2):
-                nc.tensor.matmul_mx(
-                    out=bank[:, part, :],
-                    lhsT=w2_codes[:, part * G : part * G + G].bitcast(FP8X4),
-                    lhsT_scale=w2_scales[:, part * G : part * G + G],
-                    rhs=n1_codes[h // 4][:, cols].bitcast(FP8X4),
-                    rhs_scale=n1_scales[h // 4][:, cols],
-                    start=True,
-                    stop=True,
-                )
-            ri2[h] = bank
-
-        def first_order(h, n, reader="vector"):
-            bank = next_bank(reader, [P, n * P], "s1_sums")
+        def second_product(out, matrix, h, n):
             cols = slice(h % 4 * P, (h % 4 + n) * P)
             nc.tensor.matmul_mx(
-                out=bank[:],
-                lhsT=w2_codes[:, 2 * G : 3 * G].bitcast(FP8X4),
-                lhsT_scale=w2_scales[:, 2 * G : 3 * G],
+                out=out,
+                lhsT=w2_codes[:, matrix * G : matrix * G + G].bitcast(FP8X4),
+                lhsT_scale=w2_scales[:, matrix * G : matrix * G + G],
                 rhs=n1_codes[h // 4][:, cols].bitcast(FP8X4),
                 rhs_scale=n1_scales[h // 4][:, cols],
                 start=True,
                 stop=True,
             )
+
+        def second_bank(p, where):
+            bank = bank_of(where, [P, 2, BATCH], "ri2")
+            for part in range(2):
+                second_product(bank[:, part, :], part, 2 * p, 2)
+            ri2[p] = bank
+            if p % 2 == 0:
+                square = stage.tile([P, 2, PAIR], F32, name="square2", bufs=4)
+                squares2[p // 2] = square
+
+        def squares_of(p):
+            return squares2[p // 2][:, :, p % 2 * BATCH : p % 2 * BATCH + BATCH]
+
+        def square2(p):
+            nc.scalar.activation(out=squares_of(p), in_=ri2[p][:], func=ACT.Square)
+
+        def copy_ri2(p):
+            plain = stage.tile([P, 2, BATCH], F32, name="ri2_copy", bufs=2)
+            nc.vector.tensor_copy(out=plain[:], in_=ri2[p][:])
+            ri2_copies[p] = plain
+
+        def multiply_ri2(p):
+            nc.vector.tensor_tensor(out=squares_of(p), in0=ri2[p][:], in1=ri2_copies[p][:], op=ALU.mult)
+
+        def add_squares2(p):
+            total = stage.tile([P, PAIR], F32, name="sum2", bufs=3)
+            nc.gpsimd.tensor_tensor(
+                out=total[:], in0=squares2[p // 2][:, 0, :], in1=squares2[p // 2][:, 1, :], op=ALU.add
+            )
+            sums2[2 * p] = total
+
+        def first_order(h, n, where):
+            bank = bank_of(where, [P, n * P], "s1_sums")
+            second_product(bank[:], 2, h, n)
             s1_sums[h] = bank
 
         def store_s1(h, n, copy=nc.vector.tensor_copy):
@@ -389,301 +368,330 @@ def tile_learnedsecondorderscattering_t_kernel(
             copy(out=s1[:], in_=s1_sums[h][:])
             nc.sync.dma_start(out=out_0[:, h * P : (h + n) * P], in_=s1[:])
 
-        def copy_ri2(h, n):
-            if vector_squares2(h // 2):
-                plain = stage.tile([P, 2, n * P], F32, name="ri2_copy", bufs=2)
-                nc.vector.tensor_copy(out=plain[:], in_=ri2[h][:])
-                ri2_copies[h] = plain
-
-        def square2(h, n, on_vector=False):
-            if vector_squares2(h // 2) != on_vector:
-                return
-            if h // 4 not in squares2:
-                square = stage.tile([P, 2, PAIR], F32, name="square2", bufs=4)
-                squares2[h // 4] = square
-            cols = slice(h % 4 * P, (h % 4 + n) * P)
-            if tensor_adds(h // 2) and on_vector:
-                cols = slice(h % 4 * 2 * G, (h % 4 + n) * 2 * G)
-                nc.vector.tensor_tensor(
-                    out=squares2[h // 4][:].rearrange("p a c -> p (a c)")[:, cols],
-                    in0=ri2[h][:].rearrange("p a c -> p (a c)"),
-                    in1=ri2_copies[h][:].rearrange("p a c -> p (a c)"),
-                    op=ALU.mult,
-                )
-            elif tensor_adds(h // 2):
-                cols = slice(h % 4 * 2 * G, (h % 4 + n) * 2 * G)
-                nc.scalar.activation(
-                    out=squares2[h // 4][:].rearrange("p a c -> p (a c)")[:, cols],
-                    in_=ri2[h][:].rearrange("p a c -> p (a c)"),
-                    func=ACT.Square,
-                )
-            elif on_vector:
-                nc.vector.tensor_tensor(
-                    out=squares2[h // 4][:, :, cols], in0=ri2[h][:], in1=ri2_copies[h][:], op=ALU.mult
-                )
-            else:
-                nc.scalar.activation(out=squares2[h // 4][:, :, cols], in_=ri2[h][:], func=ACT.Square)
-
-        def add_squares2(h, n, engine=nc.vector):
-            if tensor_adds(h // 2):
-                bank = next_bank("scalar", [P, n * P], "sum2_bank")
-                square = squares2[h // 4][:].rearrange("p a c -> p (a c)")
-                for i in range(n):
-                    for part in range(2):
-                        first = ((h + i) % 4 * 2 + part) * G
-                        nc.tensor.matmul(
-                            out=bank[:, i * P : i * P + P],
-                            lhsT=square[:, first : first + G],
-                            rhs=ident[:],
-                            is_transpose=True,
-                            start=(part == 0),
-                            stop=(part == 1),
-                        )
-                sums2[h] = bank
-                return
-            cols = slice(h % 4 * P, (h % 4 + n) * P)
-            total = stage.tile([P, n * P], F32, name="sum2", bufs=3)
-            engine.tensor_tensor(
-                out=total[:], in0=squares2[h // 4][:, 0, cols], in1=squares2[h // 4][:, 1, cols], op=ALU.add
-            )
-            sums2[h] = total
-
         def store_u2(h, n):
             u2 = stage.tile([P, n * P], F32, name="u2", bufs=6)
             nc.scalar.activation(out=u2[:], in_=sums2[h][:], func=ACT.Sqrt, bias=quarter[:, 0:1])
             nc.sync.dma_start(out=out_1[:, h * P : (h + n) * P], in_=u2[:])
 
-        def at(stage_of, p, *args):
-            if 0 <= p < N_BATCHES:
-                stage_of(p, *args)
+        late_ri2, late_squares = {}, {}
 
-        def batch(stage_of, p, *args):
-            if 0 <= p < N_BATCHES:
-                stage_of(2 * p, 2, *args)
+        def late_bank(h, n):
+            bank = ring_bank([P, n, 2 * G], "late_ri2")
+            for i in range(n):
+                cols = slice((h + i) % 4 * P, (h + i) % 4 * P + P)
+                nc.tensor.matmul_mx(
+                    out=bank[:, i, :],
+                    lhsT=n1_codes[h // 4][:, cols].bitcast(FP8X4),
+                    lhsT_scale=n1_scales[h // 4][:, cols],
+                    rhs=w2_codes[:, 0 : 2 * G].bitcast(FP8X4),
+                    rhs_scale=w2_scales[:, 0 : 2 * G],
+                    start=True,
+                    stop=True,
+                )
+            late_ri2[h] = bank
 
-        def pair(stage_of, p, *args):
-            if p % 2 == 0 and 0 <= p < N_BATCHES:
-                stage_of(2 * p, 4, *args)
+        def late_square(h, n):
+            square = stage.tile([P, n, 2 * G], F32, name="late_square", bufs=6)
+            nc.scalar.activation(out=square[:], in_=late_ri2[h][:], func=ACT.Square)
+            for i in range(n):
+                late_squares[h + i] = square[:, i, :]
 
-        def add_half(p, half):
-            for tile in range(FILTER_TILES):
-                add_squares1(p, half, tile)
+        def late_add(h, n):
+            bank = ring_bank([P, n * P], "late_sum")
+            for i in range(n):
+                for part in range(2):
+                    nc.tensor.matmul(
+                        out=bank[:, i * P : i * P + P],
+                        lhsT=late_squares[h + i][:, part * G : part * G + G],
+                        rhs=ident[:],
+                        is_transpose=True,
+                        start=(part == 0),
+                        stop=(part == 1),
+                    )
+            sums2[h] = bank
 
-        def centre_half(p, half):
-            centre(2 * p + half)
-
-        for tile in range(2):
-            turn_a("ar", tile)
-            turn_a("aim", tile)
-        widen_batch(0)
-        group_a("ar", 0)
-        group_a("aim", 0)
-        group_x(0)
-        quantize_a("ar", 0)
-        quantize_x(0)
-        quantize_a("aim", 0)
-        group_a("ar", 1)
-        group_a("aim", 1)
-        turn_a("ar", 2)
-        turn_a("aim", 2)
-        first_bank(0, 0)
-        quantize_a("ar", 1)
-        quantize_a("aim", 1)
-        group_a("ar", 2)
-        group_a("aim", 2)
-        turn_a("ar", 3)
-        turn_a("aim", 3)
-        first_bank(0, 1)
-        widen_batch(1)
-        quantize_a("ar", 2)
-        quantize_a("aim", 2)
+        widen_batches(0, 1)
+        group_x(0, 1)
+        for tile in range(FILTER_TILES):
+            turn_and_group_a("ar", tile)
+            turn_and_group_a("aim", tile)
+            if tile == 3:
+                widen_batches(1, 1)
+            quantize_a("ar", tile)
+            if tile == 0:
+                quantize_x(0, 1)
+            quantize_a("aim", tile)
+        group_x(1, 1)
+        for tile in range(FILTER_TILES):
+            first_bank(0, tile)
+        widen(2, 1, 0)
+        widen(2, 1, 1)
+        quantize_x(1, 1)
+        widen(2, 1, 2)
+        widen(2, 1, 3)
         square1(0, 0)
-        group_a("ar", 3)
-        group_a("aim", 3)
-        first_bank(0, 2)
-        group_x(1)
-        quantize_a("ar", 3)
-        quantize_a("aim", 3)
         square1(0, 1)
-        first_bank(0, 3)
-        quantize_x(1)
-        widen_planes(2)
-        widen_planes(3)
         square1(0, 2)
         first_bank(1, 0)
         square1(0, 3)
         first_bank(1, 1)
         first_bank(1, 2)
-        group_x(2)
-        widen_plane(4)
+        widen(3, 2, 0)
+        group_x(2, 1)
+        widen(3, 2, 1)
         square1(1, 0)
         first_bank(1, 3)
-        add_half(0, 0)
-        quantize_x(2)
-        widen_plane(5)
-        group_x(3)
-        widen_plane(6)
+        add_squares1(0, 0, range(4))
+        quantize_x(2, 1)
+        widen(3, 2, 2)
+        widen(3, 2, 3)
+        widen_plane(0)
+        group_x(3, 2)
+        widen_plane(1)
+        quantize_x(3, 2)
         square1(1, 1)
-        add_half(0, 1)
+        add_squares1(0, 1, range(4))
         square1(1, 2)
         square1(1, 3)
         first_bank(2, 0)
         first_bank(2, 1)
         root1(0, 0)
         root1(0, 1)
-        order_gain()
-        add_half(1, 0)
-        add_half(1, 1)
-        quantize_x(3)
-        widen_plane(7)
-        group_x(4)
+        spread_constants()
+        turn_w2(2, 1, "turned")
+        add_squares1(1, 0, range(4))
+        add_squares1(1, 1, range(4))
+        widen_plane(2)
+        widen_plane(3)
+        widen_plane(4)
         square1(2, 0)
         square1(2, 1)
 
-        def step(s):
+        def sums_and_turn(p, turned):
+            add_squares1(p, 0, range(3))
+            if turned >= 0:
+                turn_n1(2 * turned, 2)
+            add_squares1(p, 0, [3])
+            add_squares1(p, 1, range(4))
+
+        def two_steps(s):
+            second = s - 6
+            both = s >= 99
+            pair_of_x = min(2, N_BATCHES - s - 3)
             first_bank(s, 2)
             first_bank(s, 3)
-            batch(second_bank, s - 5)
-            if s <= 5 or s % 2 == 0:
-                batch(average, s - 2)
-            at(widen_plane, s + 6)
-            at(quantize_x, s + 2)
-            batch(quantize_n1, s - 4)
-            at(group_x, s + 3, True)
-            pair(add_squares2, s - 7, nc.gpsimd)
+            if second >= 0:
+                second_bank(second, "ri2")
+                second_bank(second + 1, "ring")
             root1(s - 1, 0)
             first_bank(s + 1, 0)
             root1(s - 1, 1)
-            if 5 <= s < 21 and s % 2 == 0:
-                batch(average, s - 1, True)
             first_bank(s + 1, 1)
-            pair(first_order, s - 6, "scalar" if vector_squares2(s - 5) else "vector")
-            batch(turn_n1, s - 3)
+            group_x(s + 3, pair_of_x, True)
             if s == 2:
-                turn_w2(0, 2)
-            if s == 3:
-                turn_w2(2, 1)
+                turn_w2(0, 2, "ri2")
+            if both:
+                average(2 * (s - 2), 2)
+                group_n1(2 * (s - 4), 2)
+                centre(2 * (s - 2))
+                centre(2 * (s - 2) + 1)
+                copy_ri2(second + 1)
+                copy_ri2(second)
+                multiply_ri2(second + 1)
+                average(2 * (s - 1), 2)
+                multiply_ri2(second)
+            else:
+                if second >= 0:
+                    copy_ri2(second)
+                if s >= 4:
+                    group_n1(2 * (s - 4), 2)
+                average(2 * (s - 2), 4)
+                if s == 2:
+                    group_w2(2, 1)
+                if second >= 0:
+                    multiply_ri2(second)
             square1(s, 2)
             square1(s, 3)
-            batch(square2, s - 5)
-            add_half(s, 0)
-            add_half(s, 1)
-            batch(copy_ri2, s - 5)
-            centre_half(s - 2, 0)
-            batch(square2, s - 5, True)
-            pair(store_s1, s - 6)
-            centre_half(s - 2, 1)
-            batch(group_n1, s - 3)
+            if both:
+                store_u2(2 * second - 4, 4)
+            elif second >= 0:
+                square2(second + 1)
+            sums_and_turn(s, s - 3)
+            if second >= 0:
+                add_squares2(second)
+            if not both:
+                centre(2 * (s - 2))
+                centre(2 * (s - 2) + 1)
             if s == 2:
                 group_w2(0, 2)
-            if s == 3:
-                group_w2(2, 1)
-            pair(store_u2, s - 9)
+            else:
+                group_n1(2 * (s - 3), 2)
+            centre(2 * (s - 1))
             square1(s + 1, 0)
             square1(s + 1, 1)
 
-        for s in range(2, N_BATCHES - 2):
-            if s == 4:
+            first_bank(s + 1, 2)
+            first_bank(s + 1, 3)
+            if second >= 0:
+                first_order(2 * second, 4, "ring")
+            root1(s, 0)
+            first_bank(s + 2, 0)
+            root1(s, 1)
+            first_bank(s + 2, 1)
+            if second >= 0:
+                store_s1(2 * second, 4)
+            centre(2 * (s - 1) + 1)
+            square1(s + 1, 2)
+            square1(s + 1, 3)
+            if second >= 2 and not both:
+                store_u2(2 * second - 4, 4)
+            sums_and_turn(s + 1, s - 2)
+            if s == 2:
                 quantize_w2(0, 2)
                 quantize_w2(2, 1)
-            step(s)
+            else:
+                quantize_n1(2 * (s - 4), 4)
+            widen_plane(s + 3)
+            quantize_x(s + 3, pair_of_x)
+            widen_plane(s + 4)
+            square1(s + 2, 0)
+            square1(s + 2, 1)
 
-        batch(turn_n1, 19)
-        batch(average, 20)
-        batch(quantize_n1, 18)
-        batch(group_n1, 19)
+        for s in range(2, LAST_LOOP_STEP + 1, 2):
+            two_steps(s)
+
+        first_bank(20, 2)
+        first_bank(20, 3)
+        second_bank(14, "ri2")
+        second_bank(15, "ring")
+        root1(19, 0)
+        first_bank(21, 0)
+        root1(19, 1)
+        first_bank(21, 1)
+        group_x(23, 1, True)
+        average(36, 2)
+        group_n1(32, 2)
+        centre(36)
+        centre(37)
+        copy_ri2(15)
+        copy_ri2(14)
+        multiply_ri2(15)
+        average(38, 2)
+        multiply_ri2(14)
+        square1(20, 2)
+        square1(20, 3)
+        store_u2(24, 4)
+        sums_and_turn(20, 17)
+        add_squares2(14)
+        group_n1(34, 2)
+        centre(38)
+        centre(39)
+        square1(21, 0)
+        square1(21, 1)
+
+        first_bank(21, 2)
+        first_bank(21, 3)
+        first_order(28, 4, "ring")
+        root1(20, 0)
+        first_bank(22, 0)
+        root1(20, 1)
+        first_bank(22, 1)
+        quantize_n1(32, 4)
+        quantize_x(23, 1)
+        square1(21, 2)
+        square1(21, 3)
+        store_u2(28, 4)
+        sums_and_turn(21, 18)
+        turn_n1(38, 2, "ri2")
+        average(40, 2)
+        store_s1(28, 4)
+        group_n1(36, 2)
         centre(40)
         centre(41)
+        square1(22, 0)
+        square1(22, 1)
+
         first_bank(22, 2)
         first_bank(22, 3)
-        batch(second_bank, 17)
+        second_bank(16, "ring")
         root1(21, 0)
         first_bank(23, 0)
         root1(21, 1)
         first_bank(23, 1)
-        pair(first_order, 16)
-        batch(turn_n1, 20)
-        batch(average, 21)
-        batch(quantize_n1, 19)
+        average(42, 2)
+        group_n1(38, 2)
         centre(42)
-        batch(group_n1, 20)
         centre(43)
-        pair(store_s1, 16)
-        batch(quantize_n1, 20)
+        quantize_n1(36, 4)
         square1(22, 2)
         square1(22, 3)
-        batch(square2, 17)
-        add_half(22, 0)
-        add_half(22, 1)
+        square2(16)
+        sums_and_turn(22, 20)
+        turn_n1(42, 2, "ri2")
+        group_n1(40, 2)
+        group_n1(42, 2)
         square1(23, 0)
         square1(23, 1)
 
         first_bank(23, 2)
         first_bank(23, 3)
-        batch(second_bank, 18)
+        second_bank(17, "ring")
         root1(22, 0)
+        late_bank(36, 2)
+        first_order(32, 4, "turned")
         root1(22, 1)
-        batch(turn_n1, 21)
-        for tile in range(2):
-            add_squares1(23, 0, tile)
-            add_squares1(23, 1, tile)
-        batch(average, 22)
-        pair(add_squares2, 16)
-        batch(group_n1, 21)
+        average(44, 2)
+        quantize_n1(40, 4)
         centre(44)
         centre(45)
-        batch(quantize_n1, 21)
+        store_s1(32, 4)
         square1(23, 2)
         square1(23, 3)
-        for tile in range(2, 4):
-            add_squares1(23, 0, tile)
-            add_squares1(23, 1, tile)
-        hand_bank_to_vector()
-        batch(second_bank, 19)
-        batch(square2, 18)
-        batch(second_bank, 20)
-        batch(turn_n1, 22)
-        pair(first_order, 20)
-        pair(store_u2, 14)
+        square2(17)
+        add_squares1(23, 0, range(4))
+        add_squares1(23, 1, range(4))
+        turn_n1(44, 2, "ri2")
+        add_squares2(16)
+        late_square(36, 2)
+        late_bank(38, 2)
+        first_order(36, 4, "turned")
+        late_bank(40, 2)
+        late_bank(42, 2)
+        group_n1(44, 2)
         root1(23, 0)
-        batch(second_bank, 21)
         root1(23, 1)
-        average(46, 1)
-        batch(group_n1, 22)
-        average(47, 1)
+        average(46, 2)
+        quantize_n1(44, 2)
         centre(46)
         centre(47)
-        batch(quantize_n1, 22)
-        pair(first_order, 18, "scalar")
-        batch(square2, 19)
-        pair(add_squares2, 18)
-        batch(square2, 20)
-        batch(square2, 21)
-        turn_n1(46, 1)
-        pair(add_squares2, 20)
-        turn_n1(47, 1)
-        pair(store_u2, 16)
-        pair(store_s1, 18, nc.scalar.copy)
-        batch(second_bank, 22)
-        pair(store_u2, 18)
-        pair(store_s1, 20)
-        pair(store_u2, 20)
+        late_square(38, 2)
+        store_u2(32, 4)
+        store_s1(36, 4)
+        late_add(36, 4)
+        late_square(40, 2)
+        late_square(42, 2)
+        late_bank(44, 2)
+        turn_n1(46, 1, "ri2")
+        turn_n1(47, 1, "ring")
         group_n1(46, 1)
         group_n1(47, 1)
-        batch(first_order, 22)
         quantize_n1(46, 1)
         quantize_n1(47, 1)
-        batch(square2, 22)
-        second_bank(46, 1)
-        second_bank(47, 1)
-        batch(first_order, 23)
-        batch(add_squares2, 22)
-        batch(store_s1, 22)
-        batch(store_s1, 23)
-        square2(46, 1)
-        square2(47, 1)
-        add_squares2(46, 1)
-        add_squares2(47, 1)
-        batch(store_u2, 22)
+        late_square(44, 2)
+        late_add(40, 4)
+        first_order(40, 4, "turned")
+        store_u2(36, 4)
+        late_bank(46, 1)
+        late_bank(47, 1)
+        first_order(44, 4, "ri2")
+        store_u2(40, 4)
+        store_s1(40, 4)
+        late_add(44, 2)
+        late_square(46, 1)
+        late_square(47, 1)
+        store_s1(44, 4)
+        store_u2(44, 2)
+        late_add(46, 1)
+        late_add(47, 1)
         store_u2(46, 1)
         store_u2(47, 1)

@@ -108,7 +108,7 @@ def tile_learnedsecondorderscattering_t_kernel(
         def widen(p, count, t):
             stretch, place = stretch_of(p)
             if stretch not in x_wide:
-                wide = stage.tile([P, 4, QUAD], BF16, name="x_wide", bufs=2, align_bytes=64)
+                wide = stage.tile([P, 4, QUAD], BF16, name="x_wide", bufs=3, align_bytes=64)
                 x_wide[stretch] = wide
             load = max(i for i in range(len(LOADS)) if sum(LOADS[:i]) <= p * BATCH)
             first = p * BATCH - sum(LOADS[:load])
@@ -334,7 +334,7 @@ def tile_learnedsecondorderscattering_t_kernel(
                 second_product(bank[:, part, :], part, 2 * p, 2)
             ri2[p] = bank
             if p % 2 == 0:
-                square = stage.tile([P, 2, PAIR], F32, name="square2", bufs=4)
+                square = stage.tile([P, 2, PAIR], F32, name="square2", bufs=3)
                 squares2[p // 2] = square
 
         def squares_of(p):
@@ -344,19 +344,22 @@ def tile_learnedsecondorderscattering_t_kernel(
             nc.scalar.activation(out=squares_of(p), in_=ri2[p][:], func=ACT.Square)
 
         def copy_ri2(p):
-            plain = stage.tile([P, 2, BATCH], F32, name="ri2_copy", bufs=2)
+            plain = stage.tile([P, 2, BATCH], F32, name="ri2_copy", bufs=3)
             nc.vector.tensor_copy(out=plain[:], in_=ri2[p][:])
             ri2_copies[p] = plain
 
         def multiply_ri2(p):
             nc.vector.tensor_tensor(out=squares_of(p), in0=ri2[p][:], in1=ri2_copies[p][:], op=ALU.mult)
 
+        def square_copy(p):
+            nc.gpsimd.tensor_tensor(out=squares_of(p), in0=ri2_copies[p][:], in1=ri2_copies[p][:], op=ALU.mult)
+
         def add_squares2(p):
             total = stage.tile([P, PAIR], F32, name="sum2", bufs=3)
             nc.gpsimd.tensor_tensor(
                 out=total[:], in0=squares2[p // 2][:, 0, :], in1=squares2[p // 2][:, 1, :], op=ALU.add
             )
-            sums2[2 * p] = total
+            sums2[2 * p], sums2[2 * p + 2] = total, total[:, BATCH:PAIR]
 
         def first_order(h, n, where):
             bank = bank_of(where, [P, n * P], "s1_sums")
@@ -370,7 +373,7 @@ def tile_learnedsecondorderscattering_t_kernel(
 
         def store_u2(h, n):
             u2 = stage.tile([P, n * P], F32, name="u2", bufs=6)
-            nc.scalar.activation(out=u2[:], in_=sums2[h][:], func=ACT.Sqrt, bias=quarter[:, 0:1])
+            nc.scalar.activation(out=u2[:], in_=sums2[h][:, 0 : n * P], func=ACT.Sqrt, bias=quarter[:, 0:1])
             nc.sync.dma_start(out=out_1[:, h * P : (h + n) * P], in_=u2[:])
 
         late_ri2, late_squares = {}, {}
@@ -468,15 +471,16 @@ def tile_learnedsecondorderscattering_t_kernel(
         square1(2, 1)
 
         def sums_and_turn(p, turned):
-            add_squares1(p, 0, range(3))
+            before = 3 if p % 2 == 0 else 0
+            add_squares1(p, 0, range(before))
             if turned >= 0:
                 turn_n1(2 * turned, 2)
-            add_squares1(p, 0, [3])
+            add_squares1(p, 0, range(before, 4))
             add_squares1(p, 1, range(4))
 
         def two_steps(s):
             second = s - 6
-            both = s >= 99
+            both = s >= 12
             pair_of_x = min(2, N_BATCHES - s - 3)
             first_bank(s, 2)
             first_bank(s, 3)
@@ -488,18 +492,19 @@ def tile_learnedsecondorderscattering_t_kernel(
             root1(s - 1, 1)
             first_bank(s + 1, 1)
             group_x(s + 3, pair_of_x, True)
+            if second >= 2:
+                add_squares2(second - 2)
             if s == 2:
                 turn_w2(0, 2, "ri2")
             if both:
-                average(2 * (s - 2), 2)
                 group_n1(2 * (s - 4), 2)
-                centre(2 * (s - 2))
-                centre(2 * (s - 2) + 1)
                 copy_ri2(second + 1)
+                square_copy(second + 1)
+                average(2 * (s - 2), 4)
                 copy_ri2(second)
-                multiply_ri2(second + 1)
-                average(2 * (s - 1), 2)
+                centre(2 * (s - 2))
                 multiply_ri2(second)
+                centre(2 * (s - 2) + 1)
             else:
                 if second >= 0:
                     copy_ri2(second)
@@ -512,13 +517,11 @@ def tile_learnedsecondorderscattering_t_kernel(
                     multiply_ri2(second)
             square1(s, 2)
             square1(s, 3)
-            if both:
-                store_u2(2 * second - 4, 4)
-            elif second >= 0:
+            if both and second >= 4:
+                store_u2(2 * second - 8, 4)
+            elif second >= 0 and not both:
                 square2(second + 1)
             sums_and_turn(s, s - 3)
-            if second >= 0:
-                add_squares2(second)
             if not both:
                 centre(2 * (s - 2))
                 centre(2 * (s - 2) + 1)
@@ -543,17 +546,19 @@ def tile_learnedsecondorderscattering_t_kernel(
             centre(2 * (s - 1) + 1)
             square1(s + 1, 2)
             square1(s + 1, 3)
-            if second >= 2 and not both:
-                store_u2(2 * second - 4, 4)
+            if second >= 4 and not both:
+                store_u2(2 * second - 8, 4)
             sums_and_turn(s + 1, s - 2)
             if s == 2:
                 quantize_w2(0, 2)
                 quantize_w2(2, 1)
             else:
                 quantize_n1(2 * (s - 4), 4)
-            widen_plane(s + 3)
+            planes = {2: [5, 6, 7], 4: [8, 9, 10, 11]}.get(s, [s + 6, s + 7])
+            for n in planes[:-1]:
+                widen_plane(n)
             quantize_x(s + 3, pair_of_x)
-            widen_plane(s + 4)
+            widen_plane(planes[-1])
             square1(s + 2, 0)
             square1(s + 2, 1)
 
@@ -569,23 +574,23 @@ def tile_learnedsecondorderscattering_t_kernel(
         root1(19, 1)
         first_bank(21, 1)
         group_x(23, 1, True)
+        add_squares2(12)
         average(36, 2)
         group_n1(32, 2)
         centre(36)
-        centre(37)
         copy_ri2(15)
+        square_copy(15)
+        centre(37)
         copy_ri2(14)
-        multiply_ri2(15)
         average(38, 2)
         multiply_ri2(14)
+        centre(38)
         square1(20, 2)
         square1(20, 3)
-        store_u2(24, 4)
+        store_u2(20, 4)
         sums_and_turn(20, 17)
         add_squares2(14)
         group_n1(34, 2)
-        centre(38)
-        centre(39)
         square1(21, 0)
         square1(21, 1)
 
@@ -596,15 +601,16 @@ def tile_learnedsecondorderscattering_t_kernel(
         first_bank(22, 0)
         root1(20, 1)
         first_bank(22, 1)
+        store_s1(28, 4)
+        centre(39)
         quantize_n1(32, 4)
         quantize_x(23, 1)
         square1(21, 2)
         square1(21, 3)
-        store_u2(28, 4)
+        store_u2(24, 4)
         sums_and_turn(21, 18)
         turn_n1(38, 2, "ri2")
         average(40, 2)
-        store_s1(28, 4)
         group_n1(36, 2)
         centre(40)
         centre(41)
@@ -626,6 +632,7 @@ def tile_learnedsecondorderscattering_t_kernel(
         square1(22, 2)
         square1(22, 3)
         square2(16)
+        store_u2(28, 4)
         sums_and_turn(22, 20)
         turn_n1(42, 2, "ri2")
         group_n1(40, 2)

@@ -35,16 +35,22 @@ def tile_learnedsecondorderscattering_t_kernel(
         psum = ctx.enter_context(tc.psum_pool(name="psum", bufs=1))
         ring = ["s0", "s1", "s2", "s3", "s4"]
 
-        def ring_bank(shape, name):
+        held = {}
+
+        def ring_bank(shape, name, key):
             oldest = ring[0]
             ring.remove(oldest)
-            ring.append(oldest)
+            held[name, key] = oldest
             bank = psum.tile(shape, F32, name=name, tag=oldest)
             return bank
 
-        def bank_of(where, shape, name):
+        def release(name, key):
+            if (name, key) in held:
+                ring.append(held[name, key])
+
+        def bank_of(where, shape, name, key=0):
             if where == "ring":
-                return ring_bank(shape, name)
+                return ring_bank(shape, name, key)
             bank = psum.tile(shape, F32, name=name, tag=where)
             return bank
 
@@ -54,10 +60,13 @@ def tile_learnedsecondorderscattering_t_kernel(
 
         a_rows, x_loads = {}, []
 
-        def load_a(name, weights, tile):
-            rows = keep.tile([P, S], BF16, name=f"{name}_rows{tile}", align_bytes=64)
-            nc.sync.dma_start(out=rows[:], in_=weights.rearrange("(q t) k -> q t k", t=4)[:, tile, :])
-            a_rows[name, tile] = rows
+        def load_a(name, weights, first, count):
+            rows = keep.tile([P, count, S], BF16, name=f"{name}_rows{first}", align_bytes=64)
+            nc.sync.dma_start(
+                out=rows[:], in_=weights.rearrange("(q t) k -> q t k", t=4)[:, first : first + count, :]
+            )
+            for t in range(count):
+                a_rows[name, first + t] = rows[:, t, :]
 
         def load_x():
             i = len(x_loads)
@@ -72,9 +81,9 @@ def tile_learnedsecondorderscattering_t_kernel(
         scale = keep.tile([P, 4], F32, name="scale")
         nc.sync.dma_start(out=scale[:], in_=x_scale.rearrange("(p t) o -> p (t o)", t=4))
         load_x()
-        for tile in range(FILTER_TILES):
-            load_a("ar", ar, tile)
-            load_a("aim", aim, tile)
+        for first, count in ((0, 1), (1, 1), (2, 1), (3, 1)):
+            load_a("ar", ar, first, count)
+            load_a("aim", aim, first, count)
         load_x()
         load_x()
         gain_rows = keep.tile([P, 4], BF16, name="gain_rows")
@@ -95,8 +104,12 @@ def tile_learnedsecondorderscattering_t_kernel(
         zeros = keep.tile([P, F], BF16, name="zeros")
         nc.vector.memset(zeros[:], 0.0)
         unread = bank_of("turned", [P, F], "unread")
-        for i in range(4):
-            nc.tensor.matmul(out=unread[:], lhsT=zeros[:, 0:P], rhs=zeros[:], start=True, stop=True)
+
+        def warm_up(columns):
+            nc.tensor.matmul(out=unread[:, 0:columns], lhsT=zeros[:, 0:P], rhs=zeros[:, 0:columns], start=True, stop=True)
+
+        for columns in (F, F, F, F):
+            warm_up(columns)
         one_in_f = keep.tile([P, 1], F32, name="one_in_f")
         nc.vector.memset(one_in_f[:], 1.0 / F)
 
@@ -105,24 +118,23 @@ def tile_learnedsecondorderscattering_t_kernel(
         def stretch_of(p):
             return (p + 3) // 4, (p - 1) % 4 * BATCH if p else 0
 
-        def widen(p, count, t):
+        def widen(p, count, t, on_scalar=False):
             stretch, place = stretch_of(p)
             if stretch not in x_wide:
                 wide = stage.tile([P, 4, QUAD], BF16, name="x_wide", bufs=3, align_bytes=64)
                 x_wide[stretch] = wide
             load = max(i for i in range(len(LOADS)) if sum(LOADS[:i]) <= p * BATCH)
             first = p * BATCH - sum(LOADS[:load])
-            nc.vector.tensor_scalar(
-                out=x_wide[stretch][:, t, place : place + count * BATCH],
-                in0=x_loads[load][:, t, first : first + count * BATCH].bitcast(FP8),
-                scalar1=scale[:, t : t + 1],
-                scalar2=None,
-                op0=ALU.mult,
-            )
+            plane = x_wide[stretch][:, t, place : place + count * BATCH]
+            source = x_loads[load][:, t, first : first + count * BATCH].bitcast(FP8)
+            if on_scalar:
+                nc.scalar.activation(out=plane, in_=source, func=ACT.Copy, scale=scale[:, t : t + 1])
+            else:
+                nc.vector.tensor_scalar(out=plane, in0=source, scalar1=scale[:, t : t + 1], scalar2=None, op0=ALU.mult)
 
-        def widen_batches(p, count):
+        def widen_batches(p, count, on_scalar=False):
             for t in range(4):
-                widen(p, count, t)
+                widen(p, count, t, on_scalar)
 
         def widen_plane(n):
             p = 5 + n // 4 * 4
@@ -168,15 +180,25 @@ def tile_learnedsecondorderscattering_t_kernel(
             scales = keep.tile([P, F], U8, name=f"{name}_scales", align_bytes=64)
             a_grouped[name], a_codes[name], a_scales[name] = grouped, codes, scales
 
-        def turn_and_group_a(name, tile):
-            turned = ring_bank([P, 2, P], "turned_a")
-            words = a_rows[name, tile][:].bitcast(F32)
+        a_turned = {}
+
+        def turn_a(name, tile):
+            turned = ring_bank([P, 2, P], "turned_a", (name, tile))
+            words = a_rows[name, tile].bitcast(F32)
             for v in range(2):
                 nc.tensor.transpose(turned[:, v, :], words[:, v : S // 2 : 2], ident[:])
-            nc.scalar.copy(
+            a_turned[name, tile] = turned
+
+        def group_a(name, tile, copy=nc.scalar.copy):
+            copy(
                 out=a_grouped[name][:, tile * P : tile * P + P, :].bitcast(F32),
-                in_=turned[:].rearrange("p v q -> p q v"),
+                in_=a_turned[name, tile][:].rearrange("p v q -> p q v"),
             )
+            release("turned_a", (name, tile))
+
+        def turn_and_group_a(name, tile):
+            turn_a(name, tile)
+            group_a(name, tile)
 
         def quantize_a(name, tile):
             cols = slice(tile * P, tile * P + P)
@@ -228,7 +250,7 @@ def tile_learnedsecondorderscattering_t_kernel(
 
         def first_bank(p, tile):
             cols = slice(tile * P, tile * P + P)
-            bank = ring_bank([P, 2, BATCH], "ri1")
+            bank = ring_bank([P, 2, BATCH], "ri1", (p, tile))
             for i, name in enumerate(("ar", "aim")):
                 nc.tensor.matmul_mx(
                     out=bank[:, i, :],
@@ -245,11 +267,12 @@ def tile_learnedsecondorderscattering_t_kernel(
             square = stage.tile([P, 2, BATCH], F32, name="square1", bufs=12)
             nc.scalar.activation(out=square[:], in_=ri1[p, tile][:], func=ACT.Square)
             squares[p, tile] = square
+            release("ri1", (p, tile))
 
         def add_squares1(p, half, tiles):
             for tile in tiles:
                 if tile == 0:
-                    bank = ring_bank([P, F], "sum1")
+                    bank = ring_bank([P, F], "sum1", (p, half))
                     sums[p, half] = bank
                 for i in range(2):
                     nc.tensor.matmul(
@@ -271,6 +294,7 @@ def tile_learnedsecondorderscattering_t_kernel(
                 accum_out=totals[:, 2 * p + half : 2 * p + half + 1],
             )
             u1s[2 * p + half] = u1
+            release("sum1", (p, half))
 
         def average(h, n):
             nc.vector.tensor_tensor(
@@ -287,7 +311,7 @@ def tile_learnedsecondorderscattering_t_kernel(
             n1s[h] = n1
 
         def turn_n1(h, n, where="turned"):
-            bank = bank_of(where, [P, n, 2, P], "n1_turned")
+            bank = bank_of(where, [P, n, 2, P], "n1_turned", h)
             for i in range(n):
                 words = n1s[h + i][:].bitcast(F32)
                 for u in range(2):
@@ -297,14 +321,15 @@ def tile_learnedsecondorderscattering_t_kernel(
         def group_n1(h, n):
             if h % 4 == 0:
                 grouped = stage.tile([P, PAIR, 4], BF16, name="n1_grouped", bufs=2, align_bytes=64)
-                codes = stage.tile([P, PAIR], U32, name="n1_codes", bufs=6, align_bytes=64)
-                scales = stage.tile([P, PAIR], U8, name="n1_scales", bufs=6, align_bytes=64)
+                codes = stage.tile([P, PAIR], U32, name="n1_codes", bufs=7, align_bytes=64)
+                scales = stage.tile([P, PAIR], U8, name="n1_scales", bufs=7, align_bytes=64)
                 n1_grouped[h // 4], n1_codes[h // 4], n1_scales[h // 4] = grouped, codes, scales
             cols = slice(h % 4 * P, (h % 4 + n) * P)
             nc.vector.tensor_copy(
                 out=n1_grouped[h // 4][:, cols, :].bitcast(F32).rearrange("p (h r) u -> p h r u", h=n),
                 in_=n1_turned[h][:].rearrange("p h u r -> p h r u"),
             )
+            release("n1_turned", h)
 
         def quantize_n1(h, n):
             cols = slice(h % 4 * P, (h % 4 + n) * P)
@@ -329,7 +354,7 @@ def tile_learnedsecondorderscattering_t_kernel(
             )
 
         def second_bank(p, where):
-            bank = bank_of(where, [P, 2, BATCH], "ri2")
+            bank = bank_of(where, [P, 2, BATCH], "ri2", p)
             for part in range(2):
                 second_product(bank[:, part, :], part, 2 * p, 2)
             ri2[p] = bank
@@ -342,27 +367,38 @@ def tile_learnedsecondorderscattering_t_kernel(
 
         def square2(p):
             nc.scalar.activation(out=squares_of(p), in_=ri2[p][:], func=ACT.Square)
+            release("ri2", p)
 
         def copy_ri2(p):
             plain = stage.tile([P, 2, BATCH], F32, name="ri2_copy", bufs=3)
             nc.vector.tensor_copy(out=plain[:], in_=ri2[p][:])
             ri2_copies[p] = plain
 
-        def multiply_ri2(p):
-            nc.vector.tensor_tensor(out=squares_of(p), in0=ri2[p][:], in1=ri2_copies[p][:], op=ALU.mult)
+        def multiply_ri2(p, parts=slice(0, 2)):
+            nc.vector.tensor_tensor(
+                out=squares_of(p)[:, parts, :],
+                in0=ri2[p][:, parts, :],
+                in1=ri2_copies[p][:, parts, :],
+                op=ALU.mult,
+            )
 
-        def square_copy(p):
-            nc.gpsimd.tensor_tensor(out=squares_of(p), in0=ri2_copies[p][:], in1=ri2_copies[p][:], op=ALU.mult)
-
-        def add_squares2(p):
-            total = stage.tile([P, PAIR], F32, name="sum2", bufs=3)
+        def square_copy(p, parts=slice(0, 2)):
             nc.gpsimd.tensor_tensor(
+                out=squares_of(p)[:, parts, :],
+                in0=ri2_copies[p][:, parts, :],
+                in1=ri2_copies[p][:, parts, :],
+                op=ALU.mult,
+            )
+
+        def add_squares2(p, engine=nc.gpsimd):
+            total = stage.tile([P, PAIR], F32, name="sum2", bufs=3)
+            engine.tensor_tensor(
                 out=total[:], in0=squares2[p // 2][:, 0, :], in1=squares2[p // 2][:, 1, :], op=ALU.add
             )
             sums2[2 * p], sums2[2 * p + 2] = total, total[:, BATCH:PAIR]
 
         def first_order(h, n, where):
-            bank = bank_of(where, [P, n * P], "s1_sums")
+            bank = bank_of(where, [P, n * P], "s1_sums", h)
             second_product(bank[:], 2, h, n)
             s1_sums[h] = bank
 
@@ -374,12 +410,13 @@ def tile_learnedsecondorderscattering_t_kernel(
         def store_u2(h, n):
             u2 = stage.tile([P, n * P], F32, name="u2", bufs=6)
             nc.scalar.activation(out=u2[:], in_=sums2[h][:, 0 : n * P], func=ACT.Sqrt, bias=quarter[:, 0:1])
+            release("late_sum", h)
             nc.sync.dma_start(out=out_1[:, h * P : (h + n) * P], in_=u2[:])
 
         late_ri2, late_squares = {}, {}
 
         def late_bank(h, n):
-            bank = ring_bank([P, n, 2 * G], "late_ri2")
+            bank = ring_bank([P, n, 2 * G], "late_ri2", h)
             for i in range(n):
                 cols = slice((h + i) % 4 * P, (h + i) % 4 * P + P)
                 nc.tensor.matmul_mx(
@@ -396,15 +433,28 @@ def tile_learnedsecondorderscattering_t_kernel(
         def late_square(h, n):
             square = stage.tile([P, n, 2 * G], F32, name="late_square", bufs=6)
             nc.scalar.activation(out=square[:], in_=late_ri2[h][:], func=ACT.Square)
+            release("late_ri2", h)
+            for i in range(n):
+                late_squares[h + i] = square[:, i, :]
+
+        def late_copy(h, n):
+            plain = stage.tile([P, n, 2 * G], F32, name="ri2_copy", bufs=3)
+            nc.vector.tensor_copy(out=plain[:], in_=late_ri2[h][:])
+            release("late_ri2", h)
+            square = stage.tile([P, n, 2 * G], F32, name="late_square", bufs=6)
+            nc.gpsimd.tensor_tensor(out=square[:], in0=plain[:], in1=plain[:], op=ALU.mult)
             for i in range(n):
                 late_squares[h + i] = square[:, i, :]
 
         def late_add(h, n):
-            bank = ring_bank([P, n * P], "late_sum")
+            if h == 38:
+                bank, first = sums2[36], 2
+            else:
+                bank, first = ring_bank([P, PAIR], "late_sum", h), 0
             for i in range(n):
                 for part in range(2):
                     nc.tensor.matmul(
-                        out=bank[:, i * P : i * P + P],
+                        out=bank[:, (first + i) * P : (first + i) * P + P],
                         lhsT=late_squares[h + i][:, part * G : part * G + G],
                         rhs=ident[:],
                         is_transpose=True,
@@ -470,27 +520,40 @@ def tile_learnedsecondorderscattering_t_kernel(
         square1(2, 0)
         square1(2, 1)
 
-        def sums_and_turn(p, turned):
-            before = 3 if p % 2 == 0 else 0
-            add_squares1(p, 0, range(before))
+        def sums_and_turn(p, turned, halves=(0, 1)):
+            place = 3 if p % 2 == 0 else 0
+            work = [(half, tile) for half in halves for tile in range(FILTER_TILES)]
+            for half, tile in work[:place]:
+                add_squares1(p, half, [tile])
             if turned >= 0:
                 turn_n1(2 * turned, 2)
-            add_squares1(p, 0, range(before, 4))
-            add_squares1(p, 1, range(4))
+            for half, tile in work[place:]:
+                add_squares1(p, half, [tile])
+
+        def products_and_roots(p, between):
+            first_bank(p, (2, 3)[0])
+            first_bank(p, (2, 3)[1])
+            between()
+            root1(p - 1, 0)
+            first_bank(p + 1, (0, 1)[0])
+            root1(p - 1, 1)
+            first_bank(p + 1, (0, 1)[1])
 
         def two_steps(s):
             second = s - 6
-            both = s >= 12
+            both = s >= 8
             pair_of_x = min(2, N_BATCHES - s - 3)
-            first_bank(s, 2)
-            first_bank(s, 3)
-            if second >= 0:
-                second_bank(second, "ri2")
-                second_bank(second + 1, "ring")
-            root1(s - 1, 0)
-            first_bank(s + 1, 0)
-            root1(s - 1, 1)
-            first_bank(s + 1, 1)
+
+            def second_banks():
+                if second >= 0:
+                    second_bank(second, "ri2")
+                    second_bank(second + 1, "ring")
+
+            def first_order_sums():
+                if second >= 2:
+                    first_order(2 * (second - 2), 4, "ring")
+
+            products_and_roots(s, second_banks)
             group_x(s + 3, pair_of_x, True)
             if second >= 2:
                 add_squares2(second - 2)
@@ -499,11 +562,14 @@ def tile_learnedsecondorderscattering_t_kernel(
             if both:
                 group_n1(2 * (s - 4), 2)
                 copy_ri2(second + 1)
-                square_copy(second + 1)
                 average(2 * (s - 2), 4)
                 copy_ri2(second)
+                if True:
+                    multiply_ri2(second + 1, slice(0, 1))
+                    square_copy(second + 1, slice(1, 2))
+                else:
+                    square_copy(second + 1)
                 centre(2 * (s - 2))
-                multiply_ri2(second)
                 centre(2 * (s - 2) + 1)
             else:
                 if second >= 0:
@@ -517,11 +583,13 @@ def tile_learnedsecondorderscattering_t_kernel(
                     multiply_ri2(second)
             square1(s, 2)
             square1(s, 3)
-            if both and second >= 4:
-                store_u2(2 * second - 8, 4)
-            elif second >= 0 and not both:
+            if both:
+                release("ri2", second + 1)
+                if second >= 4:
+                    store_u2(2 * second - 8, 4)
+            elif second >= 0:
                 square2(second + 1)
-            sums_and_turn(s, s - 3)
+            sums_and_turn(s, s - 3, (0, 1))
             if not both:
                 centre(2 * (s - 2))
                 centre(2 * (s - 2) + 1)
@@ -529,32 +597,30 @@ def tile_learnedsecondorderscattering_t_kernel(
                 group_w2(0, 2)
             else:
                 group_n1(2 * (s - 3), 2)
+            if both:
+                multiply_ri2(second)
             centre(2 * (s - 1))
             square1(s + 1, 0)
             square1(s + 1, 1)
 
-            first_bank(s + 1, 2)
-            first_bank(s + 1, 3)
-            if second >= 0:
-                first_order(2 * second, 4, "ring")
-            root1(s, 0)
-            first_bank(s + 2, 0)
-            root1(s, 1)
-            first_bank(s + 2, 1)
-            if second >= 0:
-                store_s1(2 * second, 4)
+            products_and_roots(s + 1, first_order_sums)
+            if second >= 2:
+                store_s1(2 * (second - 2), 4)
             centre(2 * (s - 1) + 1)
             square1(s + 1, 2)
             square1(s + 1, 3)
+            release("s1_sums", 2 * (second - 2))
+            if both and 4 == 2:
+                store_u2(2 * second - 6, 2)
             if second >= 4 and not both:
                 store_u2(2 * second - 8, 4)
-            sums_and_turn(s + 1, s - 2)
+            sums_and_turn(s + 1, s - 2, (0, 1))
             if s == 2:
                 quantize_w2(0, 2)
                 quantize_w2(2, 1)
             else:
                 quantize_n1(2 * (s - 4), 4)
-            planes = {2: [5, 6, 7], 4: [8, 9, 10, 11]}.get(s, [s + 6, s + 7])
+            planes = {2: [5, 6, 7, 8], 4: [9, 10, 11, 12], 6: [13, 14, 15]}.get(s, [s // 2 + 12])
             for n in planes[:-1]:
                 widen_plane(n)
             quantize_x(s + 3, pair_of_x)
@@ -587,6 +653,7 @@ def tile_learnedsecondorderscattering_t_kernel(
         centre(38)
         square1(20, 2)
         square1(20, 3)
+        release("ri2", 15)
         store_u2(20, 4)
         sums_and_turn(20, 17)
         add_squares2(14)
@@ -596,17 +663,20 @@ def tile_learnedsecondorderscattering_t_kernel(
 
         first_bank(21, 2)
         first_bank(21, 3)
-        first_order(28, 4, "ring")
+        first_order(24, 4, "ring")
+        first_order(28, 4, "ri2")
         root1(20, 0)
         first_bank(22, 0)
         root1(20, 1)
         first_bank(22, 1)
-        store_s1(28, 4)
+        store_s1(24, 4)
         centre(39)
+        store_s1(28, 4)
         quantize_n1(32, 4)
         quantize_x(23, 1)
         square1(21, 2)
         square1(21, 3)
+        release("s1_sums", 24)
         store_u2(24, 4)
         sums_and_turn(21, 18)
         turn_n1(38, 2, "ri2")

@@ -23,6 +23,10 @@ PAIR = 2 * BATCH
 QUAD = 4 * BATCH
 LOADS = [BATCH, BATCH, BATCH, PAIR] + [QUAD] * 4 + [3 * BATCH]
 LAST_LOOP_STEP = 18
+FIRST_STEP_WITHOUT_SCALAR = 8
+STEPS_WITH_A_FREE_BANK = (2, 3, 4, 5, 7)
+PLANES_IN_TURN = {2: 4, 4: 4, 6: 3}
+WARM_UPS = 4
 
 
 def tile_learnedsecondorderscattering_t_kernel(
@@ -33,9 +37,7 @@ def tile_learnedsecondorderscattering_t_kernel(
         keep = ctx.enter_context(tc.tile_pool(name="keep", bufs=1))
         stage = ctx.enter_context(tc.tile_pool(name="stage", bufs=2))
         psum = ctx.enter_context(tc.psum_pool(name="psum", bufs=1))
-        ring = ["s0", "s1", "s2", "s3", "s4"]
-
-        held = {}
+        ring, held = ["s0", "s1", "s2", "s3", "s4"], {}
 
         def ring_bank(shape, name, key):
             oldest = ring[0]
@@ -60,13 +62,10 @@ def tile_learnedsecondorderscattering_t_kernel(
 
         a_rows, x_loads = {}, []
 
-        def load_a(name, weights, first, count):
-            rows = keep.tile([P, count, S], BF16, name=f"{name}_rows{first}", align_bytes=64)
-            nc.sync.dma_start(
-                out=rows[:], in_=weights.rearrange("(q t) k -> q t k", t=4)[:, first : first + count, :]
-            )
-            for t in range(count):
-                a_rows[name, first + t] = rows[:, t, :]
+        def load_a(name, weights, tile):
+            rows = keep.tile([P, S], BF16, name=f"{name}_rows{tile}", align_bytes=64)
+            nc.sync.dma_start(out=rows[:], in_=weights.rearrange("(q t) k -> q t k", t=4)[:, tile, :])
+            a_rows[name, tile] = rows
 
         def load_x():
             i = len(x_loads)
@@ -81,9 +80,9 @@ def tile_learnedsecondorderscattering_t_kernel(
         scale = keep.tile([P, 4], F32, name="scale")
         nc.sync.dma_start(out=scale[:], in_=x_scale.rearrange("(p t) o -> p (t o)", t=4))
         load_x()
-        for first, count in ((0, 1), (1, 1), (2, 1), (3, 1)):
-            load_a("ar", ar, first, count)
-            load_a("aim", aim, first, count)
+        for tile in range(FILTER_TILES):
+            load_a("ar", ar, tile)
+            load_a("aim", aim, tile)
         load_x()
         load_x()
         gain_rows = keep.tile([P, 4], BF16, name="gain_rows")
@@ -104,12 +103,8 @@ def tile_learnedsecondorderscattering_t_kernel(
         zeros = keep.tile([P, F], BF16, name="zeros")
         nc.vector.memset(zeros[:], 0.0)
         unread = bank_of("turned", [P, F], "unread")
-
-        def warm_up(columns):
-            nc.tensor.matmul(out=unread[:, 0:columns], lhsT=zeros[:, 0:P], rhs=zeros[:, 0:columns], start=True, stop=True)
-
-        for columns in (F, F, F, F):
-            warm_up(columns)
+        for i in range(WARM_UPS):
+            nc.tensor.matmul(out=unread[:], lhsT=zeros[:, 0:P], rhs=zeros[:], start=True, stop=True)
         one_in_f = keep.tile([P, 1], F32, name="one_in_f")
         nc.vector.memset(one_in_f[:], 1.0 / F)
 
@@ -118,25 +113,30 @@ def tile_learnedsecondorderscattering_t_kernel(
         def stretch_of(p):
             return (p + 3) // 4, (p - 1) % 4 * BATCH if p else 0
 
-        def widen(p, count, t, on_scalar=False):
+        def widen(p, count, t):
             stretch, place = stretch_of(p)
             if stretch not in x_wide:
                 wide = stage.tile([P, 4, QUAD], BF16, name="x_wide", bufs=3, align_bytes=64)
                 x_wide[stretch] = wide
             load = max(i for i in range(len(LOADS)) if sum(LOADS[:i]) <= p * BATCH)
             first = p * BATCH - sum(LOADS[:load])
-            plane = x_wide[stretch][:, t, place : place + count * BATCH]
-            source = x_loads[load][:, t, first : first + count * BATCH].bitcast(FP8)
-            if on_scalar:
-                nc.scalar.activation(out=plane, in_=source, func=ACT.Copy, scale=scale[:, t : t + 1])
-            else:
-                nc.vector.tensor_scalar(out=plane, in0=source, scalar1=scale[:, t : t + 1], scalar2=None, op0=ALU.mult)
+            nc.vector.tensor_scalar(
+                out=x_wide[stretch][:, t, place : place + count * BATCH],
+                in0=x_loads[load][:, t, first : first + count * BATCH].bitcast(FP8),
+                scalar1=scale[:, t : t + 1],
+                scalar2=None,
+                op0=ALU.mult,
+            )
 
-        def widen_batches(p, count, on_scalar=False):
+        def widen_batch(p):
             for t in range(4):
-                widen(p, count, t, on_scalar)
+                widen(p, 1, t)
 
-        def widen_plane(n):
+        planes_done = []
+
+        def widen_next_plane():
+            n = len(planes_done)
+            planes_done.append(n)
             p = 5 + n // 4 * 4
             if p < N_BATCHES:
                 widen(p, min(4, N_BATCHES - p), n % 4)
@@ -180,25 +180,16 @@ def tile_learnedsecondorderscattering_t_kernel(
             scales = keep.tile([P, F], U8, name=f"{name}_scales", align_bytes=64)
             a_grouped[name], a_codes[name], a_scales[name] = grouped, codes, scales
 
-        a_turned = {}
-
-        def turn_a(name, tile):
+        def turn_and_group_a(name, tile):
             turned = ring_bank([P, 2, P], "turned_a", (name, tile))
-            words = a_rows[name, tile].bitcast(F32)
+            words = a_rows[name, tile][:].bitcast(F32)
             for v in range(2):
                 nc.tensor.transpose(turned[:, v, :], words[:, v : S // 2 : 2], ident[:])
-            a_turned[name, tile] = turned
-
-        def group_a(name, tile, copy=nc.scalar.copy):
-            copy(
+            nc.scalar.copy(
                 out=a_grouped[name][:, tile * P : tile * P + P, :].bitcast(F32),
-                in_=a_turned[name, tile][:].rearrange("p v q -> p q v"),
+                in_=turned[:].rearrange("p v q -> p q v"),
             )
             release("turned_a", (name, tile))
-
-        def turn_and_group_a(name, tile):
-            turn_a(name, tile)
-            group_a(name, tile)
 
         def quantize_a(name, tile):
             cols = slice(tile * P, tile * P + P)
@@ -390,26 +381,26 @@ def tile_learnedsecondorderscattering_t_kernel(
                 op=ALU.mult,
             )
 
-        def add_squares2(p, engine=nc.gpsimd):
+        def add_squares2(p):
             total = stage.tile([P, PAIR], F32, name="sum2", bufs=3)
-            engine.tensor_tensor(
+            nc.gpsimd.tensor_tensor(
                 out=total[:], in0=squares2[p // 2][:, 0, :], in1=squares2[p // 2][:, 1, :], op=ALU.add
             )
-            sums2[2 * p], sums2[2 * p + 2] = total, total[:, BATCH:PAIR]
+            sums2[2 * p] = total
 
         def first_order(h, n, where):
             bank = bank_of(where, [P, n * P], "s1_sums", h)
             second_product(bank[:], 2, h, n)
             s1_sums[h] = bank
 
-        def store_s1(h, n, copy=nc.vector.tensor_copy):
+        def store_s1(h, n):
             s1 = stage.tile([P, n * P], F32, name="s1", bufs=4)
-            copy(out=s1[:], in_=s1_sums[h][:])
+            nc.vector.tensor_copy(out=s1[:], in_=s1_sums[h][:])
             nc.sync.dma_start(out=out_0[:, h * P : (h + n) * P], in_=s1[:])
 
         def store_u2(h, n):
             u2 = stage.tile([P, n * P], F32, name="u2", bufs=6)
-            nc.scalar.activation(out=u2[:], in_=sums2[h][:, 0 : n * P], func=ACT.Sqrt, bias=quarter[:, 0:1])
+            nc.scalar.activation(out=u2[:], in_=sums2[h][:], func=ACT.Sqrt, bias=quarter[:, 0:1])
             release("late_sum", h)
             nc.sync.dma_start(out=out_1[:, h * P : (h + n) * P], in_=u2[:])
 
@@ -437,24 +428,12 @@ def tile_learnedsecondorderscattering_t_kernel(
             for i in range(n):
                 late_squares[h + i] = square[:, i, :]
 
-        def late_copy(h, n):
-            plain = stage.tile([P, n, 2 * G], F32, name="ri2_copy", bufs=3)
-            nc.vector.tensor_copy(out=plain[:], in_=late_ri2[h][:])
-            release("late_ri2", h)
-            square = stage.tile([P, n, 2 * G], F32, name="late_square", bufs=6)
-            nc.gpsimd.tensor_tensor(out=square[:], in0=plain[:], in1=plain[:], op=ALU.mult)
-            for i in range(n):
-                late_squares[h + i] = square[:, i, :]
-
         def late_add(h, n):
-            if h == 38:
-                bank, first = sums2[36], 2
-            else:
-                bank, first = ring_bank([P, PAIR], "late_sum", h), 0
+            bank = ring_bank([P, n * P], "late_sum", h)
             for i in range(n):
                 for part in range(2):
                     nc.tensor.matmul(
-                        out=bank[:, (first + i) * P : (first + i) * P + P],
+                        out=bank[:, i * P : i * P + P],
                         lhsT=late_squares[h + i][:, part * G : part * G + G],
                         rhs=ident[:],
                         is_transpose=True,
@@ -463,13 +442,13 @@ def tile_learnedsecondorderscattering_t_kernel(
                     )
             sums2[h] = bank
 
-        widen_batches(0, 1)
+        widen_batch(0)
         group_x(0, 1)
         for tile in range(FILTER_TILES):
             turn_and_group_a("ar", tile)
             turn_and_group_a("aim", tile)
             if tile == 3:
-                widen_batches(1, 1)
+                widen_batch(1)
             quantize_a("ar", tile)
             if tile == 0:
                 quantize_x(0, 1)
@@ -498,9 +477,9 @@ def tile_learnedsecondorderscattering_t_kernel(
         quantize_x(2, 1)
         widen(3, 2, 2)
         widen(3, 2, 3)
-        widen_plane(0)
+        widen_next_plane()
         group_x(3, 2)
-        widen_plane(1)
+        widen_next_plane()
         quantize_x(3, 2)
         square1(1, 1)
         add_squares1(0, 1, range(4))
@@ -514,35 +493,36 @@ def tile_learnedsecondorderscattering_t_kernel(
         turn_w2(2, 1, "turned")
         add_squares1(1, 0, range(4))
         add_squares1(1, 1, range(4))
-        widen_plane(2)
-        widen_plane(3)
-        widen_plane(4)
+        widen_next_plane()
+        widen_next_plane()
+        widen_next_plane()
         square1(2, 0)
         square1(2, 1)
 
-        def sums_and_turn(p, turned, halves=(0, 1)):
-            place = 3 if p % 2 == 0 else 0
-            work = [(half, tile) for half in halves for tile in range(FILTER_TILES)]
-            for half, tile in work[:place]:
-                add_squares1(p, half, [tile])
-            if turned >= 0:
-                turn_n1(2 * turned, 2)
-            for half, tile in work[place:]:
-                add_squares1(p, half, [tile])
-
-        def products_and_roots(p, between):
-            first_bank(p, (2, 3)[0])
-            first_bank(p, (2, 3)[1])
-            between()
+        def products_and_roots(p, second_stage):
+            if p - 1 not in STEPS_WITH_A_FREE_BANK:
+                first_bank(p, 2)
+            first_bank(p, 3)
+            second_stage()
             root1(p - 1, 0)
-            first_bank(p + 1, (0, 1)[0])
+            first_bank(p + 1, 0)
             root1(p - 1, 1)
-            first_bank(p + 1, (0, 1)[1])
+            first_bank(p + 1, 1)
+
+        def sums_and_turn(p, turned):
+            if turned >= 0 and p % 2 == 1:
+                turn_n1(2 * turned, 2)
+            add_squares1(p, 0, range(3))
+            if turned >= 0 and p % 2 == 0:
+                turn_n1(2 * turned, 2)
+            if p in STEPS_WITH_A_FREE_BANK:
+                first_bank(p + 1, 2)
+            add_squares1(p, 0, [3])
+            add_squares1(p, 1, range(4))
 
         def two_steps(s):
             second = s - 6
-            both = s >= 8
-            pair_of_x = min(2, N_BATCHES - s - 3)
+            without_scalar = s >= FIRST_STEP_WITHOUT_SCALAR
 
             def second_banks():
                 if second >= 0:
@@ -554,50 +534,42 @@ def tile_learnedsecondorderscattering_t_kernel(
                     first_order(2 * (second - 2), 4, "ring")
 
             products_and_roots(s, second_banks)
-            group_x(s + 3, pair_of_x, True)
+            group_x(s + 3, 2, True)
             if second >= 2:
                 add_squares2(second - 2)
             if s == 2:
                 turn_w2(0, 2, "ri2")
-            if both:
-                group_n1(2 * (s - 4), 2)
-                copy_ri2(second + 1)
-                average(2 * (s - 2), 4)
+            if second >= 0 and not without_scalar:
                 copy_ri2(second)
-                if True:
-                    multiply_ri2(second + 1, slice(0, 1))
-                    square_copy(second + 1, slice(1, 2))
-                else:
-                    square_copy(second + 1)
-                centre(2 * (s - 2))
-                centre(2 * (s - 2) + 1)
-            else:
-                if second >= 0:
-                    copy_ri2(second)
-                if s >= 4:
-                    group_n1(2 * (s - 4), 2)
-                average(2 * (s - 2), 4)
-                if s == 2:
-                    group_w2(2, 1)
-                if second >= 0:
-                    multiply_ri2(second)
+            if s >= 4:
+                group_n1(2 * (s - 4), 2)
+            if without_scalar:
+                copy_ri2(second + 1)
+            average(2 * (s - 2), 4)
+            if s == 2:
+                group_w2(2, 1)
+            if without_scalar:
+                copy_ri2(second)
+                multiply_ri2(second + 1, slice(0, 1))
+                square_copy(second + 1, slice(1, 2))
+            elif second >= 0:
+                multiply_ri2(second)
+            centre(2 * (s - 2))
+            centre(2 * (s - 2) + 1)
             square1(s, 2)
             square1(s, 3)
-            if both:
+            if without_scalar:
                 release("ri2", second + 1)
-                if second >= 4:
-                    store_u2(2 * second - 8, 4)
             elif second >= 0:
                 square2(second + 1)
-            sums_and_turn(s, s - 3, (0, 1))
-            if not both:
-                centre(2 * (s - 2))
-                centre(2 * (s - 2) + 1)
+            if second >= 4:
+                store_u2(2 * (second - 4), 4)
+            sums_and_turn(s, s - 3)
             if s == 2:
                 group_w2(0, 2)
             else:
                 group_n1(2 * (s - 3), 2)
-            if both:
+            if without_scalar:
                 multiply_ri2(second)
             centre(2 * (s - 1))
             square1(s + 1, 0)
@@ -610,21 +582,16 @@ def tile_learnedsecondorderscattering_t_kernel(
             square1(s + 1, 2)
             square1(s + 1, 3)
             release("s1_sums", 2 * (second - 2))
-            if both and 4 == 2:
-                store_u2(2 * second - 6, 2)
-            if second >= 4 and not both:
-                store_u2(2 * second - 8, 4)
-            sums_and_turn(s + 1, s - 2, (0, 1))
+            sums_and_turn(s + 1, s - 2)
             if s == 2:
                 quantize_w2(0, 2)
                 quantize_w2(2, 1)
             else:
                 quantize_n1(2 * (s - 4), 4)
-            planes = {2: [5, 6, 7, 8], 4: [9, 10, 11, 12], 6: [13, 14, 15]}.get(s, [s // 2 + 12])
-            for n in planes[:-1]:
-                widen_plane(n)
-            quantize_x(s + 3, pair_of_x)
-            widen_plane(planes[-1])
+            for i in range(PLANES_IN_TURN.get(s, 1) - 1):
+                widen_next_plane()
+            quantize_x(s + 3, 2)
+            widen_next_plane()
             square1(s + 2, 0)
             square1(s + 2, 1)
 
@@ -647,28 +614,28 @@ def tile_learnedsecondorderscattering_t_kernel(
         copy_ri2(15)
         square_copy(15)
         centre(37)
-        copy_ri2(14)
         average(38, 2)
-        multiply_ri2(14)
+        copy_ri2(14)
         centre(38)
         square1(20, 2)
         square1(20, 3)
         release("ri2", 15)
         store_u2(20, 4)
         sums_and_turn(20, 17)
-        add_squares2(14)
         group_n1(34, 2)
+        multiply_ri2(14)
+        add_squares2(14)
         square1(21, 0)
         square1(21, 1)
 
         first_bank(21, 2)
         first_bank(21, 3)
         first_order(24, 4, "ring")
-        first_order(28, 4, "ri2")
         root1(20, 0)
         first_bank(22, 0)
         root1(20, 1)
         first_bank(22, 1)
+        first_order(28, 4, "ri2")
         store_s1(24, 4)
         centre(39)
         store_s1(28, 4)
@@ -704,32 +671,34 @@ def tile_learnedsecondorderscattering_t_kernel(
         square2(16)
         store_u2(28, 4)
         sums_and_turn(22, 20)
-        turn_n1(42, 2, "ri2")
         group_n1(40, 2)
-        group_n1(42, 2)
         square1(23, 0)
         square1(23, 1)
 
         first_bank(23, 2)
         first_bank(23, 3)
+        turn_n1(42, 2, "ri2")
+        group_n1(42, 2)
         second_bank(17, "ring")
         root1(22, 0)
         late_bank(36, 2)
-        first_order(32, 4, "turned")
         root1(22, 1)
         average(44, 2)
         quantize_n1(40, 4)
         centre(44)
         centre(45)
-        store_s1(32, 4)
         square1(23, 2)
         square1(23, 3)
         square2(17)
-        add_squares1(23, 0, range(4))
+        add_squares1(23, 0, range(3))
+        first_order(32, 4, "turned")
+        store_s1(32, 4)
+        add_squares1(23, 0, [3])
         add_squares1(23, 1, range(4))
         turn_n1(44, 2, "ri2")
         add_squares2(16)
         late_square(36, 2)
+
         late_bank(38, 2)
         first_order(36, 4, "turned")
         late_bank(40, 2)

@@ -116,7 +116,7 @@ def tile_learnedsecondorderscattering_t_kernel(
         def widen(p, count, t):
             stretch, place = stretch_of(p)
             if stretch not in x_wide:
-                wide = stage.tile([P, 4, QUAD], BF16, name="x_wide", bufs=3, align_bytes=64)
+                wide = stage.tile([P, 4, QUAD], BF16, name="x_wide", bufs=4, align_bytes=64)
                 x_wide[stretch] = wide
             load = max(i for i in range(len(LOADS)) if sum(LOADS[:i]) <= p * BATCH)
             first = p * BATCH - sum(LOADS[:load])
@@ -493,27 +493,28 @@ def tile_learnedsecondorderscattering_t_kernel(
         turn_w2(2, 1, "turned")
         add_squares1(1, 0, range(4))
         add_squares1(1, 1, range(4))
-        widen_next_plane()
-        widen_next_plane()
-        widen_next_plane()
+        for i in range(4):
+            widen_next_plane()
         square1(2, 0)
         square1(2, 1)
 
-        def products_and_roots(p, second_stage):
+        def products_and_roots(p, second_stage=None):
             if p - 1 not in STEPS_WITH_A_FREE_BANK:
                 first_bank(p, 2)
             first_bank(p, 3)
-            second_stage()
+            if second_stage:
+                second_stage()
             root1(p - 1, 0)
             first_bank(p + 1, 0)
             root1(p - 1, 1)
             first_bank(p + 1, 1)
 
         def sums_and_turn(p, turned):
-            if turned >= 0 and p % 2 == 1:
+            turn_first = p % 2 == 1 and not FIRST_STEP_WITHOUT_SCALAR < p <= LAST_LOOP_STEP + 1
+            if turned >= 0 and turn_first:
                 turn_n1(2 * turned, 2)
             add_squares1(p, 0, range(3))
-            if turned >= 0 and p % 2 == 0:
+            if turned >= 0 and not turn_first:
                 turn_n1(2 * turned, 2)
             if p in STEPS_WITH_A_FREE_BANK:
                 first_bank(p + 1, 2)
@@ -528,10 +529,6 @@ def tile_learnedsecondorderscattering_t_kernel(
                 if second >= 0:
                     second_bank(second, "ri2")
                     second_bank(second + 1, "ring")
-
-            def first_order_sums():
-                if second >= 2:
-                    first_order(2 * (second - 2), 4, "ring")
 
             products_and_roots(s, second_banks)
             group_x(s + 3, 2, True)
@@ -555,6 +552,8 @@ def tile_learnedsecondorderscattering_t_kernel(
             elif second >= 0:
                 multiply_ri2(second)
             centre(2 * (s - 2))
+            if without_scalar:
+                multiply_ri2(second)
             centre(2 * (s - 2) + 1)
             square1(s, 2)
             square1(s, 3)
@@ -569,19 +568,18 @@ def tile_learnedsecondorderscattering_t_kernel(
                 group_w2(0, 2)
             else:
                 group_n1(2 * (s - 3), 2)
-            if without_scalar:
-                multiply_ri2(second)
             centre(2 * (s - 1))
             square1(s + 1, 0)
             square1(s + 1, 1)
 
-            products_and_roots(s + 1, first_order_sums)
+            products_and_roots(s + 1)
+            if second >= 2:
+                first_order(2 * (second - 2), 4, "ri2")
+            centre(2 * (s - 1) + 1)
             if second >= 2:
                 store_s1(2 * (second - 2), 4)
-            centre(2 * (s - 1) + 1)
             square1(s + 1, 2)
             square1(s + 1, 3)
-            release("s1_sums", 2 * (second - 2))
             sums_and_turn(s + 1, s - 2)
             if s == 2:
                 quantize_w2(0, 2)

@@ -25,7 +25,8 @@ LOADS = [BATCH, BATCH, BATCH, PAIR] + [QUAD] * 4 + [3 * BATCH]
 LAST_LOOP_STEP = 18
 FIRST_STEP_WITHOUT_SCALAR = 8
 STEPS_WITH_A_FREE_BANK = (2, 3, 4, 5, 7)
-PLANES_IN_TURN = {2: 4, 4: 4, 6: 3}
+PLANES_IN_TURN = {2: 3, 4: 4, 6: 4}
+SIGNALS_ON_VECTOR = 64
 WARM_UPS = 4
 
 
@@ -365,19 +366,19 @@ def tile_learnedsecondorderscattering_t_kernel(
             nc.vector.tensor_copy(out=plain[:], in_=ri2[p][:])
             ri2_copies[p] = plain
 
-        def multiply_ri2(p, parts=slice(0, 2)):
+        def multiply_ri2(p, signals=slice(0, BATCH)):
             nc.vector.tensor_tensor(
-                out=squares_of(p)[:, parts, :],
-                in0=ri2[p][:, parts, :],
-                in1=ri2_copies[p][:, parts, :],
+                out=squares_of(p)[:, :, signals],
+                in0=ri2[p][:, :, signals],
+                in1=ri2_copies[p][:, :, signals],
                 op=ALU.mult,
             )
 
-        def square_copy(p, parts=slice(0, 2)):
+        def square_copy(p, signals=slice(0, BATCH)):
             nc.gpsimd.tensor_tensor(
-                out=squares_of(p)[:, parts, :],
-                in0=ri2_copies[p][:, parts, :],
-                in1=ri2_copies[p][:, parts, :],
+                out=squares_of(p)[:, :, signals],
+                in0=ri2_copies[p][:, :, signals],
+                in1=ri2_copies[p][:, :, signals],
                 op=ALU.mult,
             )
 
@@ -547,8 +548,8 @@ def tile_learnedsecondorderscattering_t_kernel(
                 group_w2(2, 1)
             if without_scalar:
                 copy_ri2(second)
-                multiply_ri2(second + 1, slice(0, 1))
-                square_copy(second + 1, slice(1, 2))
+                multiply_ri2(second + 1, slice(0, SIGNALS_ON_VECTOR))
+                square_copy(second + 1, slice(SIGNALS_ON_VECTOR, BATCH))
             elif second >= 0:
                 multiply_ri2(second)
             centre(2 * (s - 2))
@@ -614,6 +615,7 @@ def tile_learnedsecondorderscattering_t_kernel(
         centre(37)
         average(38, 2)
         copy_ri2(14)
+        square_copy(14)
         centre(38)
         square1(20, 2)
         square1(20, 3)
@@ -621,7 +623,6 @@ def tile_learnedsecondorderscattering_t_kernel(
         store_u2(20, 4)
         sums_and_turn(20, 17)
         group_n1(34, 2)
-        multiply_ri2(14)
         add_squares2(14)
         square1(21, 0)
         square1(21, 1)

@@ -149,8 +149,8 @@ def tile_learnedsecondorderscattering_t_kernel(
             planes = x_wide[stretch][:, :, place : place + count * BATCH]
             if on_gpsimd:
                 nc.gpsimd.tensor_scalar(
-                    out=grouped[:],
-                    in0=planes.rearrange("p t c -> p c t"),
+                    out=grouped[:].rearrange("p (c i) t -> p c t i", i=4),
+                    in0=planes.rearrange("p t (c i) -> p c t i", i=4),
                     scalar1=1.0,
                     scalar2=0.0,
                     op0=ALU.mult,

@@ -23,10 +23,10 @@ PAIR = 2 * BATCH
 QUAD = 4 * BATCH
 LOADS = [BATCH, BATCH, BATCH, PAIR] + [QUAD] * 4 + [3 * BATCH]
 LAST_LOOP_STEP = 18
-FIRST_STEP_WITHOUT_SCALAR = 8
+FIRST_STEP_WITHOUT_SCALAR = 6
 STEPS_WITH_A_FREE_BANK = (2, 3, 4, 5, 7)
-PLANES_IN_TURN = {2: 3, 4: 4, 6: 4}
-SIGNALS_ON_VECTOR = 64
+PLANES_IN_TURN = {2: 3, 4: 4, 6: 2, 8: 2, 10: 2}
+SIGNALS_ON_VECTOR = 32
 WARM_UPS = 4
 
 

@@ -25,8 +25,8 @@ LOADS = [BATCH, BATCH, BATCH, PAIR] + [QUAD] * 4 + [3 * BATCH]
 LAST_LOOP_STEP = 18
 FIRST_STEP_WITHOUT_SCALAR = 6
 STEPS_WITH_A_FREE_BANK = (2, 3, 4, 5, 7)
-PLANES_IN_TURN = {2: 3, 4: 4, 6: 2, 8: 2, 10: 2}
-SIGNALS_ON_VECTOR = 32
+PLANES_IN_TURN = {2: 3, 4: 4, 6: 2, 8: 1, 10: 1, 12: 1, 14: 1, 16: 1}
+SIGNALS_ON_VECTOR = 80
 WARM_UPS = 4
 
 
@@ -448,18 +448,19 @@ def tile_learnedsecondorderscattering_t_kernel(
         for tile in range(FILTER_TILES):
             turn_and_group_a("ar", tile)
             turn_and_group_a("aim", tile)
-            if tile == 3:
+            if tile == 2:
                 widen_batch(1)
+            if tile == 3:
+                group_x(1, 1)
             quantize_a("ar", tile)
             if tile == 0:
                 quantize_x(0, 1)
             quantize_a("aim", tile)
-        group_x(1, 1)
+        quantize_x(1, 1)
         for tile in range(FILTER_TILES):
             first_bank(0, tile)
         widen(2, 1, 0)
         widen(2, 1, 1)
-        quantize_x(1, 1)
         widen(2, 1, 2)
         widen(2, 1, 3)
         square1(0, 0)

@@ -27,7 +27,7 @@ FIRST_STEP_WITHOUT_SCALAR = 6
 STEPS_WITH_A_FREE_BANK = (2, 3, 4, 5, 7)
 PLANES_IN_TURN = {2: 3, 4: 4, 6: 2, 8: 1, 10: 1, 12: 1, 14: 1, 16: 1}
 SIGNALS_ON_VECTOR = 80
-WARM_UPS = 4
+WARM_UPS = 6
 
 
 def tile_learnedsecondorderscattering_t_kernel(

from contextlib import ExitStack

import concourse.mybir as mybir
from concourse.masks import make_identity

S, F, G, T, C = 512, 512, 128, 128, 6144
FLOPS = 2 * C * (2 * F * S + 2 * G * F + T * F)

F32 = mybir.dt.float32
BF16 = mybir.dt.bfloat16
U32 = mybir.dt.uint32
U8 = mybir.dt.uint8
FP8 = mybir.dt.float8_e4m3fn
FP8X4 = mybir.dt.float8_e4m3fn_x4
ACT = mybir.ActivationFunctionType
ALU = mybir.AluOpType

P = 128
BATCH = 256
N_BATCHES = C // BATCH
FILTER_TILES = F // P
PAIR = 2 * BATCH
QUAD = 4 * BATCH
LOADS = [BATCH, BATCH, BATCH, PAIR] + [QUAD] * 4 + [3 * BATCH]
LAST_LOOP_STEP = 18
FIRST_STEP_WITHOUT_SCALAR = 6
STEPS_WITH_A_FREE_BANK = (2, 3, 4, 5, 7)
PLANES_IN_TURN = {2: 3, 4: 4, 6: 2, 8: 1, 10: 1, 12: 1, 14: 1, 16: 1}
SIGNALS_ON_VECTOR = 80
WARM_UPS = 6


def tile_learnedsecondorderscattering_t_kernel(
    tc, x_bytes, x_scale, ar, aim, g1, cr, cim, phi, out_0, out_1
):
    nc = tc.nc
    with ExitStack() as ctx:
        keep = ctx.enter_context(tc.tile_pool(name="keep", bufs=1))
        stage = ctx.enter_context(tc.tile_pool(name="stage", bufs=2))
        psum = ctx.enter_context(tc.psum_pool(name="psum", bufs=1))
        ring, held = ["s0", "s1", "s2", "s3", "s4"], {}

        def ring_bank(shape, name, key):
            oldest = ring[0]
            ring.remove(oldest)
            held[name, key] = oldest
            bank = psum.tile(shape, F32, name=name, tag=oldest)
            return bank

        def release(name, key):
            if (name, key) in held:
                ring.append(held[name, key])

        def bank_of(where, shape, name, key=0):
            if where == "ring":
                return ring_bank(shape, name, key)
            bank = psum.tile(shape, F32, name=name, tag=where)
            return bank

        ident = keep.tile([P, P], F32, name="ident")
        make_identity(nc, ident[:])
        ctx.enter_context(tc.manual_schedule())

        a_rows, x_loads = {}, []

        def load_a(name, weights, tile):
            rows = keep.tile([P, S], BF16, name=f"{name}_rows{tile}", align_bytes=64)
            nc.sync.dma_start(out=rows[:], in_=weights.rearrange("(q t) k -> q t k", t=4)[:, tile, :])
            a_rows[name, tile] = rows

        def load_x():
            i = len(x_loads)
            first = sum(LOADS[:i])
            codes_in = keep.tile([P, 4, LOADS[i]], U8, name=f"codes_in{i}", align_bytes=64)
            nc.sync.dma_start(
                out=codes_in[:],
                in_=x_bytes.rearrange("(p t) c -> p t c", t=4)[:, :, first : first + LOADS[i]],
            )
            x_loads.append(codes_in)

        scale = keep.tile([P, 4], F32, name="scale")
        nc.sync.dma_start(out=scale[:], in_=x_scale.rearrange("(p t) o -> p (t o)", t=4))
        load_x()
        for tile in range(FILTER_TILES):
            load_a("ar", ar, tile)
            load_a("aim", aim, tile)
        load_x()
        load_x()
        gain_rows = keep.tile([P, 4], BF16, name="gain_rows")
        nc.sync.dma_start(out=gain_rows[:], in_=g1.rearrange("(q t) -> q t", t=4))
        load_x()
        load_x()
        w2_rows = keep.tile([P, 3, F], BF16, name="w2_rows", align_bytes=64)
        for m, weights in enumerate((cr, cim, phi)):
            nc.sync.dma_start(out=w2_rows[:, m, :], in_=weights)
        while len(x_loads) < len(LOADS):
            load_x()

        sixteenth = keep.tile([P, 1], F32, name="sixteenth")
        nc.vector.memset(sixteenth[:], 0.0625)
        quarter = keep.tile([P, 1], F32, name="quarter")
        nc.scalar.activation(out=quarter[:], in_=sixteenth[:], func=ACT.Sqrt)

        zeros = keep.tile([P, F], BF16, name="zeros")
        nc.vector.memset(zeros[:], 0.0)
        unread = bank_of("turned", [P, F], "unread")
        for i in range(WARM_UPS):
            nc.tensor.matmul(out=unread[:], lhsT=zeros[:, 0:P], rhs=zeros[:], start=True, stop=True)
        one_in_f = keep.tile([P, 1], F32, name="one_in_f")
        nc.vector.memset(one_in_f[:], 1.0 / F)

        x_wide, x_grouped, x_codes, x_scales = {}, {}, {}, {}

        def stretch_of(p):
            return (p + 3) // 4, (p - 1) % 4 * BATCH if p else 0

        def widen(p, count, t):
            stretch, place = stretch_of(p)
            if stretch not in x_wide:
                wide = stage.tile([P, 4, QUAD], BF16, name="x_wide", bufs=4, align_bytes=64)
                x_wide[stretch] = wide
            load = max(i for i in range(len(LOADS)) if sum(LOADS[:i]) <= p * BATCH)
            first = p * BATCH - sum(LOADS[:load])
            nc.vector.tensor_scalar(
                out=x_wide[stretch][:, t, place : place + count * BATCH],
                in0=x_loads[load][:, t, first : first + count * BATCH].bitcast(FP8),
                scalar1=scale[:, t : t + 1],
                scalar2=None,
                op0=ALU.mult,
            )

        def widen_batch(p):
            for t in range(4):
                widen(p, 1, t)

        planes_done = []

        def widen_next_plane():
            n = len(planes_done)
            planes_done.append(n)
            p = 5 + n // 4 * 4
            if p < N_BATCHES:
                widen(p, min(4, N_BATCHES - p), n % 4)

        def group_x(p, count, on_gpsimd=False):
            grouped = stage.tile([P, count * BATCH, 4], BF16, name="x_grouped", bufs=1, align_bytes=64)
            x_grouped[p] = grouped
            stretch, place = stretch_of(p)
            planes = x_wide[stretch][:, :, place : place + count * BATCH]
            if on_gpsimd:
                nc.gpsimd.tensor_scalar(
                    out=grouped[:].rearrange("p (c i) t -> p c t i", i=4),
                    in0=planes.rearrange("p t (c i) -> p c t i", i=4),
                    scalar1=1.0,
                    scalar2=0.0,
                    op0=ALU.mult,
                    op1=ALU.add,
                )
                return
            nc.vector.tensor_copy(
                out=grouped[:].rearrange("p (c i) t -> p c t i", i=4),
                in_=planes.rearrange("p t (c i) -> p c t i", i=4),
            )

        def quantize_x(p, count):
            codes = stage.tile([P, count * BATCH], U32, name="x_codes", bufs=3, align_bytes=64)
            scales = stage.tile([P, count * BATCH], U8, name="x_scales", bufs=3, align_bytes=64)
            nc.vector.quantize_mx(
                out=codes[:].bitcast(FP8X4),
                scales=scales[:],
                in_=x_grouped[p][:].rearrange("p c t -> p (c t)"),
            )
            for i in range(count):
                x_codes[p + i] = codes[:, i * BATCH : i * BATCH + BATCH]
                x_scales[p + i] = scales[:, i * BATCH : i * BATCH + BATCH]

        a_grouped, a_codes, a_scales = {}, {}, {}
        for name in ("ar", "aim"):
            grouped = keep.tile([P, F, 4], BF16, name=f"{name}_grouped", align_bytes=64)
            codes = keep.tile([P, F], U32, name=f"{name}_codes", align_bytes=64)
            scales = keep.tile([P, F], U8, name=f"{name}_scales", align_bytes=64)
            a_grouped[name], a_codes[name], a_scales[name] = grouped, codes, scales

        def turn_and_group_a(name, tile):
            turned = ring_bank([P, 2, P], "turned_a", (name, tile))
            words = a_rows[name, tile][:].bitcast(F32)
            for v in range(2):
                nc.tensor.transpose(turned[:, v, :], words[:, v : S // 2 : 2], ident[:])
            nc.scalar.copy(
                out=a_grouped[name][:, tile * P : tile * P + P, :].bitcast(F32),
                in_=turned[:].rearrange("p v q -> p q v"),
            )
            release("turned_a", (name, tile))

        def quantize_a(name, tile):
            cols = slice(tile * P, tile * P + P)
            nc.vector.quantize_mx(
                out=a_codes[name][:, cols].bitcast(FP8X4),
                scales=a_scales[name][:, cols],
                in_=a_grouped[name][:, cols, :].rearrange("p j t -> p (j t)"),
            )

        w2_grouped = keep.tile([P, 3, P, 4], BF16, name="w2_grouped", align_bytes=64)
        w2_codes = keep.tile([P, 3 * P], U32, name="w2_codes", align_bytes=64)
        w2_scales = keep.tile([P, 3 * P], U8, name="w2_scales", align_bytes=64)
        w2_turned = {}

        def turn_w2(first, count, where):
            turned = bank_of(where, [P, count, 2, P], "turned_w2")
            w2_turned[first] = turned
            for i in range(count):
                words = w2_rows[:, first + i, :].bitcast(F32)
                for v in range(2):
                    nc.tensor.transpose(turned[:, i, v, :], words[:, v : F // 2 : 2], ident[:])

        def group_w2(first, count):
            nc.vector.tensor_copy(
                out=w2_grouped[:, first : first + count, :, :].bitcast(F32),
                in_=w2_turned[first][:].rearrange("p m v g -> p m g v"),
            )

        def quantize_w2(first, count):
            cols = slice(first * P, (first + count) * P)
            nc.vector.quantize_mx(
                out=w2_codes[:, cols].bitcast(FP8X4),
                scales=w2_scales[:, cols],
                in_=w2_grouped[:, first : first + count, :, :].rearrange("p m g t -> p (m g t)"),
            )

        constants = psum.tile([P, 3, P], F32, name="constants")
        gain = constants[:, 0:2, :].rearrange("p u q -> p (u q)").bitcast(BF16)

        def spread_constants():
            words = gain_rows[:].bitcast(F32)
            for u in range(2):
                nc.tensor.transpose(constants[:, u, :], words[:, u : u + 1].to_broadcast([P, P]), ident[:])
            nc.tensor.transpose(constants[:, 2, :], one_in_f[:].to_broadcast([P, P]), ident[:])

        ri1, squares, sums, u1s = {}, {}, {}, {}
        totals = keep.tile([P, 2 * N_BATCHES], F32, name="totals")
        means = keep.tile([P, 2 * N_BATCHES], F32, name="means")

        def first_bank(p, tile):
            cols = slice(tile * P, tile * P + P)
            bank = ring_bank([P, 2, BATCH], "ri1", (p, tile))
            for i, name in enumerate(("ar", "aim")):
                nc.tensor.matmul_mx(
                    out=bank[:, i, :],
                    lhsT=a_codes[name][:, cols].bitcast(FP8X4),
                    lhsT_scale=a_scales[name][:, cols],
                    rhs=x_codes[p].bitcast(FP8X4),
                    rhs_scale=x_scales[p],
                    start=True,
                    stop=True,
                )
            ri1[p, tile] = bank

        def square1(p, tile):
            square = stage.tile([P, 2, BATCH], F32, name="square1", bufs=12)
            nc.scalar.activation(out=square[:], in_=ri1[p, tile][:], func=ACT.Square)
            squares[p, tile] = square
            release("ri1", (p, tile))

        def add_squares1(p, half, tiles):
            for tile in tiles:
                if tile == 0:
                    bank = ring_bank([P, F], "sum1", (p, half))
                    sums[p, half] = bank
                for i in range(2):
                    nc.tensor.matmul(
                        out=sums[p, half][:, tile * P : tile * P + P],
                        lhsT=squares[p, tile][:, i, half * P : half * P + P],
                        rhs=ident[:],
                        is_transpose=True,
                        start=(i == 0),
                        stop=(i == 1),
                    )

        def root1(p, half):
            u1 = stage.tile([P, F], F32, name="u1", bufs=8)
            nc.scalar.activation(
                out=u1[:].rearrange("p (u q e) -> p u q e", u=2, e=2),
                in_=sums[p, half][:].rearrange("p (u e q) -> p u q e", u=2, e=2),
                func=ACT.Sqrt,
                bias=0.25,
                accum_out=totals[:, 2 * p + half : 2 * p + half + 1],
            )
            u1s[2 * p + half] = u1
            release("sum1", (p, half))

        def average(h, n):
            nc.vector.tensor_tensor(
                out=means[:, h : h + n], in0=totals[:, h : h + n], in1=constants[:, 2, 0:n], op=ALU.mult
            )

        n1s, n1_turned, n1_grouped, n1_codes, n1_scales = {}, {}, {}, {}, {}

        def centre(h):
            n1 = stage.tile([P, F], BF16, name="n1", bufs=6, align_bytes=64)
            nc.vector.scalar_tensor_tensor(
                out=n1[:], in0=u1s[h][:], scalar=means[:, h : h + 1], in1=gain, op0=ALU.subtract, op1=ALU.mult
            )
            n1s[h] = n1

        def turn_n1(h, n, where="turned"):
            bank = bank_of(where, [P, n, 2, P], "n1_turned", h)
            for i in range(n):
                words = n1s[h + i][:].bitcast(F32)
                for u in range(2):
                    nc.tensor.transpose(bank[:, i, u, :], words[:, u * P : u * P + P], ident[:])
            n1_turned[h] = bank

        def group_n1(h, n):
            if h % 4 == 0:
                grouped = stage.tile([P, PAIR, 4], BF16, name="n1_grouped", bufs=2, align_bytes=64)
                codes = stage.tile([P, PAIR], U32, name="n1_codes", bufs=7, align_bytes=64)
                scales = stage.tile([P, PAIR], U8, name="n1_scales", bufs=7, align_bytes=64)
                n1_grouped[h // 4], n1_codes[h // 4], n1_scales[h // 4] = grouped, codes, scales
            cols = slice(h % 4 * P, (h % 4 + n) * P)
            nc.vector.tensor_copy(
                out=n1_grouped[h // 4][:, cols, :].bitcast(F32).rearrange("p (h r) u -> p h r u", h=n),
                in_=n1_turned[h][:].rearrange("p h u r -> p h r u"),
            )
            release("n1_turned", h)

        def quantize_n1(h, n):
            cols = slice(h % 4 * P, (h % 4 + n) * P)
            nc.vector.quantize_mx(
                out=n1_codes[h // 4][:, cols].bitcast(FP8X4),
                scales=n1_scales[h // 4][:, cols],
                in_=n1_grouped[h // 4][:, cols, :].rearrange("p c t -> p (c t)"),
            )

        ri2, ri2_copies, s1_sums, squares2, sums2 = {}, {}, {}, {}, {}

        def second_product(out, matrix, h, n):
            cols = slice(h % 4 * P, (h % 4 + n) * P)
            nc.tensor.matmul_mx(
                out=out,
                lhsT=w2_codes[:, matrix * G : matrix * G + G].bitcast(FP8X4),
                lhsT_scale=w2_scales[:, matrix * G : matrix * G + G],
                rhs=n1_codes[h // 4][:, cols].bitcast(FP8X4),
                rhs_scale=n1_scales[h // 4][:, cols],
                start=True,
                stop=True,
            )

        def second_bank(p, where):
            bank = bank_of(where, [P, 2, BATCH], "ri2", p)
            for part in range(2):
                second_product(bank[:, part, :], part, 2 * p, 2)
            ri2[p] = bank
            if p % 2 == 0:
                square = stage.tile([P, 2, PAIR], F32, name="square2", bufs=3)
                squares2[p // 2] = square

        def squares_of(p):
            return squares2[p // 2][:, :, p % 2 * BATCH : p % 2 * BATCH + BATCH]

        def square2(p):
            nc.scalar.activation(out=squares_of(p), in_=ri2[p][:], func=ACT.Square)
            release("ri2", p)

        def copy_ri2(p):
            plain = stage.tile([P, 2, BATCH], F32, name="ri2_copy", bufs=3)
            nc.vector.tensor_copy(out=plain[:], in_=ri2[p][:])
            ri2_copies[p] = plain

        def multiply_ri2(p, signals=slice(0, BATCH)):
            nc.vector.tensor_tensor(
                out=squares_of(p)[:, :, signals],
                in0=ri2[p][:, :, signals],
                in1=ri2_copies[p][:, :, signals],
                op=ALU.mult,
            )

        def square_copy(p, signals=slice(0, BATCH)):
            nc.gpsimd.tensor_tensor(
                out=squares_of(p)[:, :, signals],
                in0=ri2_copies[p][:, :, signals],
                in1=ri2_copies[p][:, :, signals],
                op=ALU.mult,
            )

        def add_squares2(p):
            total = stage.tile([P, PAIR], F32, name="sum2", bufs=3)
            nc.gpsimd.tensor_tensor(
                out=total[:], in0=squares2[p // 2][:, 0, :], in1=squares2[p // 2][:, 1, :], op=ALU.add
            )
            sums2[2 * p] = total

        def first_order(h, n, where):
            bank = bank_of(where, [P, n * P], "s1_sums", h)
            second_product(bank[:], 2, h, n)
            s1_sums[h] = bank

        def store_s1(h, n):
            s1 = stage.tile([P, n * P], F32, name="s1", bufs=4)
            nc.vector.tensor_copy(out=s1[:], in_=s1_sums[h][:])
            nc.sync.dma_start(out=out_0[:, h * P : (h + n) * P], in_=s1[:])

        def store_u2(h, n):
            u2 = stage.tile([P, n * P], F32, name="u2", bufs=6)
            nc.scalar.activation(out=u2[:], in_=sums2[h][:], func=ACT.Sqrt, bias=quarter[:, 0:1])
            release("late_sum", h)
            nc.sync.dma_start(out=out_1[:, h * P : (h + n) * P], in_=u2[:])

        late_ri2, late_squares = {}, {}

        def late_bank(h, n):
            bank = ring_bank([P, n, 2 * G], "late_ri2", h)
            for i in range(n):
                cols = slice((h + i) % 4 * P, (h + i) % 4 * P + P)
                nc.tensor.matmul_mx(
                    out=bank[:, i, :],
                    lhsT=n1_codes[h // 4][:, cols].bitcast(FP8X4),
                    lhsT_scale=n1_scales[h // 4][:, cols],
                    rhs=w2_codes[:, 0 : 2 * G].bitcast(FP8X4),
                    rhs_scale=w2_scales[:, 0 : 2 * G],
                    start=True,
                    stop=True,
                )
            late_ri2[h] = bank

        def late_square(h, n):
            square = stage.tile([P, n, 2 * G], F32, name="late_square", bufs=6)
            nc.scalar.activation(out=square[:], in_=late_ri2[h][:], func=ACT.Square)
            release("late_ri2", h)
            for i in range(n):
                late_squares[h + i] = square[:, i, :]

        def late_add(h, n):
            bank = ring_bank([P, n * P], "late_sum", h)
            for i in range(n):
                for part in range(2):
                    nc.tensor.matmul(
                        out=bank[:, i * P : i * P + P],
                        lhsT=late_squares[h + i][:, part * G : part * G + G],
                        rhs=ident[:],
                        is_transpose=True,
                        start=(part == 0),
                        stop=(part == 1),
                    )
            sums2[h] = bank

        widen_batch(0)
        group_x(0, 1)
        for tile in range(FILTER_TILES):
            turn_and_group_a("ar", tile)
            turn_and_group_a("aim", tile)
            if tile == 2:
                widen_batch(1)
            if tile == 3:
                group_x(1, 1)
            quantize_a("ar", tile)
            if tile == 0:
                quantize_x(0, 1)
            quantize_a("aim", tile)
        quantize_x(1, 1)
        for tile in range(FILTER_TILES):
            first_bank(0, tile)
        widen(2, 1, 0)
        widen(2, 1, 1)
        widen(2, 1, 2)
        widen(2, 1, 3)
        square1(0, 0)
        square1(0, 1)
        square1(0, 2)
        first_bank(1, 0)
        square1(0, 3)
        first_bank(1, 1)
        first_bank(1, 2)
        widen(3, 2, 0)
        group_x(2, 1)
        widen(3, 2, 1)
        square1(1, 0)
        first_bank(1, 3)
        add_squares1(0, 0, range(4))
        quantize_x(2, 1)
        widen(3, 2, 2)
        widen(3, 2, 3)
        widen_next_plane()
        group_x(3, 2)
        widen_next_plane()
        quantize_x(3, 2)
        square1(1, 1)
        add_squares1(0, 1, range(4))
        square1(1, 2)
        square1(1, 3)
        first_bank(2, 0)
        first_bank(2, 1)
        root1(0, 0)
        root1(0, 1)
        spread_constants()
        turn_w2(2, 1, "turned")
        add_squares1(1, 0, range(4))
        add_squares1(1, 1, range(4))
        for i in range(4):
            widen_next_plane()
        square1(2, 0)
        square1(2, 1)

        def products_and_roots(p, second_stage=None):
            if p - 1 not in STEPS_WITH_A_FREE_BANK:
                first_bank(p, 2)
            first_bank(p, 3)
            if second_stage:
                second_stage()
            root1(p - 1, 0)
            first_bank(p + 1, 0)
            root1(p - 1, 1)
            first_bank(p + 1, 1)

        def sums_and_turn(p, turned):
            turn_first = p % 2 == 1 and not FIRST_STEP_WITHOUT_SCALAR < p <= LAST_LOOP_STEP + 1
            if turned >= 0 and turn_first:
                turn_n1(2 * turned, 2)
            add_squares1(p, 0, range(3))
            if turned >= 0 and not turn_first:
                turn_n1(2 * turned, 2)
            if p in STEPS_WITH_A_FREE_BANK:
                first_bank(p + 1, 2)
            add_squares1(p, 0, [3])
            add_squares1(p, 1, range(4))

        def two_steps(s):
            second = s - 6
            without_scalar = s >= FIRST_STEP_WITHOUT_SCALAR

            def second_banks():
                if second >= 0:
                    second_bank(second, "ri2")
                    second_bank(second + 1, "ring")

            products_and_roots(s, second_banks)
            group_x(s + 3, 2, True)
            if second >= 2:
                add_squares2(second - 2)
            if s == 2:
                turn_w2(0, 2, "ri2")
            if second >= 0 and not without_scalar:
                copy_ri2(second)
            if s >= 4:
                group_n1(2 * (s - 4), 2)
            if without_scalar:
                copy_ri2(second + 1)
            average(2 * (s - 2), 4)
            if s == 2:
                group_w2(2, 1)
            if without_scalar:
                copy_ri2(second)
                multiply_ri2(second + 1, slice(0, SIGNALS_ON_VECTOR))
                square_copy(second + 1, slice(SIGNALS_ON_VECTOR, BATCH))
            elif second >= 0:
                multiply_ri2(second)
            centre(2 * (s - 2))
            if without_scalar:
                multiply_ri2(second)
            centre(2 * (s - 2) + 1)
            square1(s, 2)
            square1(s, 3)
            if without_scalar:
                release("ri2", second + 1)
            elif second >= 0:
                square2(second + 1)
            if second >= 4:
                store_u2(2 * (second - 4), 4)
            sums_and_turn(s, s - 3)
            if s == 2:
                group_w2(0, 2)
            else:
                group_n1(2 * (s - 3), 2)
            centre(2 * (s - 1))
            square1(s + 1, 0)
            square1(s + 1, 1)

            products_and_roots(s + 1)
            if second >= 2:
                first_order(2 * (second - 2), 4, "ri2")
            centre(2 * (s - 1) + 1)
            if second >= 2:
                store_s1(2 * (second - 2), 4)
            square1(s + 1, 2)
            square1(s + 1, 3)
            sums_and_turn(s + 1, s - 2)
            if s == 2:
                quantize_w2(0, 2)
                quantize_w2(2, 1)
            else:
                quantize_n1(2 * (s - 4), 4)
            for i in range(PLANES_IN_TURN.get(s, 1) - 1):
                widen_next_plane()
            quantize_x(s + 3, 2)
            widen_next_plane()
            square1(s + 2, 0)
            square1(s + 2, 1)

        for s in range(2, LAST_LOOP_STEP + 1, 2):
            two_steps(s)

        first_bank(20, 2)
        first_bank(20, 3)
        second_bank(14, "ri2")
        second_bank(15, "ring")
        root1(19, 0)
        first_bank(21, 0)
        root1(19, 1)
        first_bank(21, 1)
        group_x(23, 1, True)
        add_squares2(12)
        average(36, 2)
        group_n1(32, 2)
        centre(36)
        copy_ri2(15)
        square_copy(15)
        centre(37)
        average(38, 2)
        copy_ri2(14)
        square_copy(14)
        centre(38)
        square1(20, 2)
        square1(20, 3)
        release("ri2", 15)
        store_u2(20, 4)
        sums_and_turn(20, 17)
        group_n1(34, 2)
        add_squares2(14)
        square1(21, 0)
        square1(21, 1)

        first_bank(21, 2)
        first_bank(21, 3)
        first_order(24, 4, "ring")
        root1(20, 0)
        first_bank(22, 0)
        root1(20, 1)
        first_bank(22, 1)
        first_order(28, 4, "ri2")
        store_s1(24, 4)
        centre(39)
        store_s1(28, 4)
        quantize_n1(32, 4)
        quantize_x(23, 1)
        square1(21, 2)
        square1(21, 3)
        release("s1_sums", 24)
        store_u2(24, 4)
        sums_and_turn(21, 18)
        turn_n1(38, 2, "ri2")
        average(40, 2)
        group_n1(36, 2)
        centre(40)
        centre(41)
        square1(22, 0)
        square1(22, 1)

        first_bank(22, 2)
        first_bank(22, 3)
        second_bank(16, "ring")
        root1(21, 0)
        first_bank(23, 0)
        root1(21, 1)
        first_bank(23, 1)
        average(42, 2)
        group_n1(38, 2)
        centre(42)
        centre(43)
        quantize_n1(36, 4)
        square1(22, 2)
        square1(22, 3)
        square2(16)
        store_u2(28, 4)
        sums_and_turn(22, 20)
        group_n1(40, 2)
        square1(23, 0)
        square1(23, 1)

        first_bank(23, 2)
        first_bank(23, 3)
        turn_n1(42, 2, "ri2")
        group_n1(42, 2)
        second_bank(17, "ring")
        root1(22, 0)
        late_bank(36, 2)
        root1(22, 1)
        average(44, 2)
        quantize_n1(40, 4)
        centre(44)
        centre(45)
        square1(23, 2)
        square1(23, 3)
        square2(17)
        add_squares1(23, 0, range(3))
        first_order(32, 4, "turned")
        store_s1(32, 4)
        add_squares1(23, 0, [3])
        add_squares1(23, 1, range(4))
        turn_n1(44, 2, "ri2")
        add_squares2(16)
        late_square(36, 2)

        late_bank(38, 2)
        first_order(36, 4, "turned")
        late_bank(40, 2)
        late_bank(42, 2)
        group_n1(44, 2)
        root1(23, 0)
        root1(23, 1)
        average(46, 2)
        quantize_n1(44, 2)
        centre(46)
        centre(47)
        late_square(38, 2)
        store_u2(32, 4)
        store_s1(36, 4)
        late_add(36, 4)
        late_square(40, 2)
        late_square(42, 2)
        late_bank(44, 2)
        turn_n1(46, 1, "ri2")
        turn_n1(47, 1, "ring")
        group_n1(46, 1)
        group_n1(47, 1)
        quantize_n1(46, 1)
        quantize_n1(47, 1)
        late_square(44, 2)
        late_add(40, 4)
        first_order(40, 4, "turned")
        store_u2(36, 4)
        late_bank(46, 1)
        late_bank(47, 1)
        first_order(44, 4, "ri2")
        store_u2(40, 4)
        store_s1(40, 4)
        late_add(44, 2)
        late_square(46, 1)
        late_square(47, 1)
        store_s1(44, 4)
        store_u2(44, 2)
        late_add(46, 1)
        late_add(47, 1)
        store_u2(46, 1)
        store_u2(47, 1)
